import numpy as np
import ml_dtypes


def mxq(x, axis, fmt="e4m3"):
    dtype, down = {"e4m3": (ml_dtypes.float8_e4m3fn, 7), "e5m2": (ml_dtypes.float8_e5m2, 14)}[fmt]
    v = np.moveaxis(np.asarray(x, np.float32).astype(ml_dtypes.bfloat16).astype(np.float64), axis, -1)
    blocks = v.reshape(v.shape[:-1] + (-1, 32))
    amax = np.abs(blocks).max(-1, keepdims=True)
    byte = np.maximum(np.where(amax > 0, np.frexp(amax)[1] - 1 + 127, 0) - down, 1)
    scale = np.exp2(byte - 127.0)
    codes = (blocks / scale).astype(np.float32).astype(dtype).astype(np.float64)
    return np.moveaxis((codes * scale).reshape(v.shape), -1, axis)


WIDE = False


def mx_kscale(k):
    if not WIDE:
        return np.ones(k)
    levels = np.array([10, -10, 5, -5, 0])
    if k % 512:
        return np.exp2(np.random.permutation(np.resize(levels, k // 32))).repeat(32)
    a = np.empty((k // 512, 16))
    for p in range(k // 512):
        a[p, :8] = np.random.permutation(np.resize(levels, 8))
        for g in range(8):
            far = levels[np.abs(levels - a[p, g]) >= 10]
            a[p, g + 8] = far[np.random.randint(len(far))]
    return np.exp2(a.ravel()).repeat(32)


def f64(x):
    return np.asarray(x).astype(np.float64)


def striped(idx):
    return np.tile(idx.reshape(-1, 16).T, (8, 1)).astype(np.uint16)


def unstriped(offs):
    return offs[:16].T.reshape(-1).astype(np.int64)


E2M1 = np.array([0.0, 0.5, 1.0, 1.5, 2.0, 3.0, 4.0, 6.0, -0.0, -0.5, -1.0, -1.5, -2.0, -3.0, -4.0, -6.0])


def pack_weight(w, fmt):
    k, n = w.shape
    w = f64(np.asarray(w, np.float32).astype(ml_dtypes.bfloat16)).reshape(k // 32, 32, n)
    amax = np.abs(w).max(1)
    if fmt == "e4m3":
        byte = np.frexp(amax)[1] - 1 + 127 - 7
    else:
        mant, ex = np.frexp(amax / 6.0)
        byte = np.where(mant > 0.5, ex, ex - 1) + 127
    byte = np.clip(np.where(amax > 0, byte, 1), 1, 254)
    scaled = (w * np.exp2(127.0 - byte)[:, None, :]).reshape(k, n).astype(np.float32)
    by_word = np.ascontiguousarray(scaled.reshape(k // 512, 128, 4, n).transpose(0, 1, 3, 2))
    if fmt == "e4m3":
        words = by_word.astype(ml_dtypes.float8_e4m3fn).view(np.uint8)
    else:
        c = by_word.astype(ml_dtypes.float4_e2m1fn).view(np.uint8) & 0xF
        words = (c[..., 0::2] | (c[..., 1::2] << 4)).reshape(k // 512, 128, 2 * n)
    return np.ascontiguousarray(words), np.ascontiguousarray(byte.astype(np.uint8).reshape(k // 512, 16, n))


def unpack_weight(words, scales, fmt):
    g, _, n = scales.shape
    words = np.ascontiguousarray(words).reshape(g, 128, n, -1)
    if fmt == "e4m3":
        vals = words.view(ml_dtypes.float8_e4m3fn).astype(np.float64)
    else:
        nib = np.empty((g, 128, n, 4), np.uint8)
        nib[..., 0::2] = words & 0xF
        nib[..., 1::2] = words >> 4
        vals = E2M1[nib]
    vals = vals * np.repeat(np.exp2(scales.astype(np.float64) - 127.0), 8, axis=1)[..., None]
    return vals.transpose(0, 1, 3, 2).reshape(g * 512, n)


def gelu(v):
    return 0.5 * v * (1.0 + np.tanh(np.sqrt(2.0 / np.pi) * (v + 0.044715 * v**3)))


def bf(x):
    return np.asarray(x, np.float32).astype(ml_dtypes.bfloat16)

def planes(Y):
    n, m = Y.shape
    b = f64(bf(Y)).reshape(n // 32, 32, m)
    amax = np.abs(b).max(1)
    byte = np.clip(np.where(amax > 0, np.frexp(amax)[1] - 1 + 127 - 7, 1), 1, 254)
    codes = (b * np.exp2(127.0 - byte)[:, None, :]).reshape(n, m).astype(np.float32).astype(ml_dtypes.float8_e4m3fn).view(np.uint8)
    words = codes.reshape(n // 512, 128, 4, m).transpose(0, 1, 3, 2)
    return np.ascontiguousarray(words), np.ascontiguousarray(byte.astype(np.uint8).reshape(n // 512, 16, m))


K, T, S, P, H, N = 512, 4096, 1536, 768, 1024, 512

def setup_inputs():
    n = np.random.standard_normal
    s = mx_kscale(K)[:, None]
    u = mx_kscale(H)[:, None]
    tab_words, tab_scales = pack_weight(n((K, T)) * s, "e4m3")
    w1_words, w1_scales = pack_weight(n((K, H)) / np.sqrt(K) / s, "e2m1")
    g = (np.exp(0.3 * n(H)) * u[:, 0]).astype(np.float32)
    w2 = n((H, N)) * (2.5 / np.sqrt(H)) * np.exp(0.8 * n(N))[None, :]
    w2 = (w2 / u).astype(np.float32)
    offs = striped(np.random.permutation(T)[:S])
    perm = np.random.permutation(S)
    pos1, pos2 = striped(perm[:P]), striped(perm[P:])
    return {"tab_words": tab_words, "tab_scales": tab_scales,
            "w1_words": w1_words, "w1_scales": w1_scales,
            "g": g, "w2": w2, "offs": offs, "pos1": pos1, "pos2": pos2}

def reference(tab_words, tab_scales, w1_words, w1_scales, g, w2, offs, pos1, pos2):
    v = unpack_weight(tab_words, tab_scales, "e4m3")[:, unstriped(offs)]
    w1 = unpack_weight(w1_words, w1_scales, "e2m1")
    m = w1.T @ v
    h = 1.0 / (1.0 + np.exp(-m))
    a = h[:, unstriped(pos1)]
    b = h[:, unstriped(pos2)]
    z = f64(g)[:, None] * ((a - b) / (a + b))
    y = mxq(f64(w2), 0, "e4m3").T @ mxq(z, 0, "e4m3")
    words, scales = planes(y)
    return y, words, scales

@@ -1,0 +1,225 @@
+from contextlib import ExitStack
+
+import concourse.mybir as mybir
+from concourse.masks import make_identity
+
+K, T, S, PAIRS, H, N = 512, 4096, 1536, 768, 1024, 512
+FLOPS = 2 * K * H * S + 2 * H * N * PAIRS
+
+F32 = mybir.dt.float32
+BF16 = mybir.dt.bfloat16
+I32 = mybir.dt.int32
+U32 = mybir.dt.uint32
+U16 = mybir.dt.uint16
+U8 = mybir.dt.uint8
+FP8X4 = mybir.dt.float8_e4m3fn_x4
+FP4X4 = mybir.dt.float4_e2m1fn_x4
+ACT = mybir.ActivationFunctionType
+ALU = mybir.AluOpType
+
+P = 128
+PACK = 4
+PASSES = H // (P * PACK)
+SLICES = H // P
+BANK = 512
+HALF = PAIRS // 2
+Y_COLS = 128
+
+
+def tile_list_vegetation_change_indices_kernel(
+    tc, tab_words, tab_scales, w1_words, w1_scales, g, w2, offs, pos1, pos2, out_0, out_1, out_2
+):
+    nc = tc.nc
+    with ExitStack() as ctx:
+        keep = ctx.enter_context(tc.tile_pool(name="keep", bufs=1))
+        ring = ctx.enter_context(tc.tile_pool(name="ring", bufs=2))
+        psum = ctx.enter_context(tc.psum_pool(name="psum", bufs=2))
+
+        offs_t = keep.tile([P, S // 16], U16, name="offs_t")
+        pos1_t = keep.tile([P, PAIRS // 16], U16, name="pos1_t")
+        pos2_t = keep.tile([P, PAIRS // 16], U16, name="pos2_t")
+        tabs = keep.tile([P, T], U8, name="tabs")
+        w1s_raw = keep.tile([P, H], U8, name="w1s_raw", tag="then_w2")
+        w1w_raw = [
+            keep.tile([P, H], U8, name="w1w_raw0", tag="then_table"),
+            keep.tile([P, H], U8, name="w1w_raw1"),
+        ]
+        g_t = keep.tile([P, PASSES, PACK], F32, name="g_t")
+        nc.vector.memset(tabs[:].bitcast(I32), 0)
+        nc.vector.memset(w1s_raw[:].bitcast(I32), 0)
+        nc.sync.dma_start(w1w_raw[0][:].bitcast(I32), w1_words[0, :, 0:H].bitcast(I32))
+        nc.sync.dma_start(offs_t[:], offs)
+        nc.sync.dma_start(w1w_raw[1][:].bitcast(I32), w1_words[0, :, H : 2 * H].bitcast(I32))
+        nc.sync.dma_start(pos2_t[:], pos2)
+        nc.sync.dma_start(pos1_t[:], pos1)
+        for q in range(4):
+            nc.sync.dma_start(
+                tabs[32 * q : 32 * q + 4, :].bitcast(I32), tab_scales[0, 4 * q : 4 * q + 4, :].bitcast(I32)
+            )
+        for q in range(4):
+            nc.sync.dma_start(
+                w1s_raw[32 * q : 32 * q + 4, :].bitcast(I32), w1_scales[0, 4 * q : 4 * q + 4, :].bitcast(I32)
+            )
+        nc.gpsimd.dma_start(g_t[:], g.rearrange("(b p t) -> p b t", b=PASSES, t=PACK))
+
+        zero = ring.tile([P, 1], F32, name="zero", tag="root")
+        one = ring.tile([P, 1], F32, name="one", tag="root")
+        nc.gpsimd.memset(zero[:], 0.0)
+        nc.gpsimd.memset(one[:], 1.0)
+        ident = keep.tile([P, P], F32, name="ident")
+        make_identity(nc, ident[:])
+
+        w1w = [keep.tile([P, 1024], U8, name=f"w1w{b}", align_bytes=64) for b in range(PASSES)]
+        w1s = [keep.tile([P, 512], U8, name=f"w1s{b}", align_bytes=64) for b in range(PASSES)]
+        for b in range(PASSES):
+            nc.vector.tensor_copy(
+                w1w[b][:].rearrange("p (t m e) -> p t m e", t=PACK, e=2),
+                w1w_raw[b][:].rearrange("p (m t e) -> p t m e", t=PACK, e=2),
+            )
+        tabw = keep.tile([P, T], I32, name="tabw", tag="then_table")
+        nc.sync.dma_start(tabw[:], tab_words[0].rearrange("p t i -> p (t i)").bitcast(I32))
+
+        vs = keep.tile([P, S], U8, name="vs", align_bytes=64)
+        nc.vector.tensor_copy(vs[:], tabs[:].indirect(offs_t[:]))
+        for b in range(PASSES):
+            nc.vector.tensor_copy(
+                w1s[b][:].rearrange("p (t m) -> p t m", t=PACK),
+                w1s_raw[:, 512 * b : 512 * (b + 1)].rearrange("p (m t) -> p t m", t=PACK),
+            )
+        vw = [keep.tile([P, BANK], U32, name=f"vw{c}", align_bytes=64) for c in range(S // BANK)]
+        for c in range(S // BANK):
+            nc.vector.tensor_copy(vw[c][:], tabw[:].bitcast(U32).indirect(offs_t[:, 32 * c : 32 * (c + 1)]))
+
+        w2_raw = keep.tile([P, PASSES, PACK * N], F32, name="w2_raw", tag="then_w2")
+        nc.sync.dma_start(w2_raw[:], w2.rearrange("(b p j) n -> p b (j n)", b=PASSES, j=PACK))
+
+        h = [keep.tile([P, S], F32, name=f"h{j}") for j in range(SLICES)]
+
+        def respond(j, c):
+            b, t = divmod(j, PACK)
+            acc = psum.tile([P, BANK], F32, name="acc", tag="acc", bufs=4)
+            nc.tensor.matmul_mx(
+                out=acc[:],
+                lhsT=w1w[b][:, 256 * t : 256 * (t + 1)].bitcast(FP4X4),
+                lhsT_scale=w1s[b][:, P * t : P * (t + 1)],
+                rhs=vw[c][:].bitcast(FP8X4),
+                rhs_scale=vs[:, BANK * c : BANK * (c + 1)],
+                start=True,
+                stop=True,
+            )
+            nc.scalar.activation(h[j][:, BANK * c : BANK * (c + 1)], acc[:], ACT.Sigmoid, bias=zero[:], scale=one[:])
+
+        for c in range(S // BANK):
+            for j in range(2):
+                respond(j, c)
+        for j in range(2, SLICES):
+            for c in range(S // BANK):
+                respond(j, c)
+
+        w2c = [keep.tile([P, N], U32, name=f"w2c{b}", align_bytes=64) for b in range(PASSES)]
+        w2s = [keep.tile([P, N], U8, name=f"w2s{b}", align_bytes=64) for b in range(PASSES)]
+        w2b = [keep.tile([P, N * PACK], BF16, name=f"w2b{b}", align_bytes=64) for b in range(PASSES)]
+        for b in range(PASSES):
+            nc.scalar.copy(
+                w2b[b][:].rearrange("p (t m j) -> p m j t", t=PACK, j=PACK),
+                w2_raw[:, b, :].rearrange("p (j m t) -> p m j t", j=PACK, t=PACK),
+            )
+
+        early = [[keep.tile([P, HALF], F32, name=f"early{j}_{u}") for u in range(2)] for j in range(SLICES)]
+        diff = [[keep.tile([P, HALF], F32, name=f"diff{j}_{u}") for u in range(2)] for j in range(SLICES)]
+        for j in range(SLICES):
+            for u in range(2):
+                nc.vector.tensor_copy(early[j][u][:], h[j][:].indirect(pos2_t[:, 24 * u : 24 * (u + 1)]))
+            for u in range(2):
+                nc.vector.tensor_tensor(
+                    diff[j][u][:], h[j][:].indirect(pos1_t[:, 24 * u : 24 * (u + 1)]), early[j][u][:], ALU.subtract
+                )
+        for j in range(SLICES):
+            for u in range(2):
+                total = psum.tile([P, HALF], F32, name="total", tag="total")
+                for k in range(HALF // P):
+                    cols = slice(P * k, P * (k + 1))
+                    for n, src in enumerate((early[j][u], early[j][u], diff[j][u])):
+                        nc.tensor.matmul(
+                            total[:, cols], src[:, cols], ident[:], start=(n == 0), stop=(n == 2), is_transpose=True
+                        )
+                root = ring.tile([P, HALF], F32, name="root", tag="root")
+                nc.scalar.activation(root[:], total[:], ACT.Abs_reciprocal_sqrt)
+                back = psum.tile([P, HALF], F32, name="back", tag="back")
+                for k in range(HALF // P):
+                    cols = slice(P * k, P * (k + 1))
+                    nc.tensor.transpose(back[:, cols], root[:, cols], ident[:])
+                nc.scalar.activation(early[j][u][:], back[:], ACT.Square)
+
+        for b in range(PASSES):
+            nc.vector.quantize_mx(out=w2c[b][:].bitcast(FP8X4), scales=w2s[b][:], in_=w2b[b][:])
+
+        zc = [keep.tile([P, PAIRS], U32, name=f"zc{b}", align_bytes=64) for b in range(PASSES)]
+        zs = [keep.tile([P, PAIRS], U8, name=f"zs{b}", align_bytes=64) for b in range(PASSES)]
+        zrow = [keep.tile([P, PACK, PAIRS], BF16, name=f"zrow{b}") for b in range(PASSES)]
+
+        def ratio(b, c0, c1):
+            for t in range(PACK):
+                j = PACK * b + t
+                for u in range(2):
+                    lo, hi = max(c0, HALF * u), min(c1, HALF * (u + 1))
+                    if lo < hi:
+                        nc.vector.scalar_tensor_tensor(
+                            zrow[b][:, t, lo:hi],
+                            diff[j][u][:, lo - HALF * u : hi - HALF * u],
+                            g_t[:, b, t : t + 1],
+                            early[j][u][:, lo - HALF * u : hi - HALF * u],
+                            ALU.mult,
+                            ALU.mult,
+                        )
+
+        def quantise_z(b, c0, c1):
+            woven = ring.tile([P, 512 * PACK], BF16, name="woven", tag="woven", align_bytes=64)
+            w = c1 - c0
+            nc.vector.tensor_copy(
+                woven[:, 0 : w * PACK].rearrange("p (c i t) -> p c t i", i=4, t=PACK),
+                zrow[b][:, :, c0:c1].rearrange("p t (c i) -> p c t i", i=4),
+            )
+            nc.vector.quantize_mx(
+                out=zc[b][:, c0:c1].bitcast(FP8X4), scales=zs[b][:, c0:c1], in_=woven[:, 0 : w * PACK]
+            )
+
+        yc = keep.tile([P, PAIRS], U32, name="yc", align_bytes=64)
+        ys = keep.tile([P, PAIRS], U8, name="ys", align_bytes=64)
+        out_rows = out_0.rearrange("(p t) q -> p t q", t=PACK)
+        out_words = out_1[0].rearrange("p m t -> p (m t)").bitcast(I32)
+
+        def mix(c0, c1):
+            yf = ring.tile([P, PACK, 256], F32, name="yf", tag="yf")
+            for s0 in range(c0, c1, Y_COLS):
+                cols = slice(s0, s0 + Y_COLS)
+                acc = psum.tile([P, PACK, Y_COLS], F32, name="yacc", tag="acc", bufs=4)
+                for t in range(PACK):
+                    for b in range(PASSES):
+                        nc.tensor.matmul_mx(
+                            out=acc[:, t, :],
+                            lhsT=w2c[b][:, P * t : P * (t + 1)].bitcast(FP8X4),
+                            lhsT_scale=w2s[b][:, P * t : P * (t + 1)],
+                            rhs=zc[b][:, cols].bitcast(FP8X4),
+                            rhs_scale=zs[b][:, cols],
+                            start=(b == 0),
+                            stop=(b == PASSES - 1),
+                        )
+                yb = ring.tile([P, Y_COLS * PACK], BF16, name="yb", tag="yb", align_bytes=64)
+                nc.scalar.copy(yb[:].rearrange("p (n t) -> p n t", t=PACK), acc[:].rearrange("p t n -> p n t"))
+                nc.scalar.copy(yf[:, :, s0 - c0 : s0 - c0 + Y_COLS], acc[:])
+                nc.vector.quantize_mx(out=yc[:, cols].bitcast(FP8X4), scales=ys[:, cols], in_=yb[:])
+            nc.sync.dma_start(out_rows[:, :, c0:c1], yf[:, :, 0 : c1 - c0])
+            nc.sync.dma_start(out_words[:, c0:c1], yc[:, c0:c1].bitcast(I32))
+
+        ratio(0, 0, PAIRS)
+        quantise_z(0, 0, 512)
+        quantise_z(0, 512, PAIRS)
+        for c0, c1 in ((0, 256), (256, 512), (512, 640), (640, 768)):
+            ratio(1, c0, c1)
+            quantise_z(1, c0, c1)
+            mix(c0, c1)
+        for q in range(4):
+            nc.scalar.dma_start(
+                out_2[0, 4 * q : 4 * q + 4, :].bitcast(I32), ys[32 * q : 32 * q + 4, :].bitcast(I32)
+            )

@@ -33,7 +33,6 @@ def tile_list_vegetation_change_indices_kernel(
     with ExitStack() as ctx:
         keep = ctx.enter_context(tc.tile_pool(name="keep", bufs=1))
         ring = ctx.enter_context(tc.tile_pool(name="ring", bufs=2))
-        psum = ctx.enter_context(tc.psum_pool(name="psum", bufs=2))
 
         offs_t = keep.tile([P, S // 16], U16, name="offs_t")
         pos1_t = keep.tile([P, PAIRS // 16], U16, name="pos1_t")
@@ -62,8 +61,8 @@ def tile_list_vegetation_change_indices_kernel(
             )
         nc.gpsimd.dma_start(g_t[:], g.rearrange("(b p t) -> p b t", b=PASSES, t=PACK))
 
-        zero = ring.tile([P, 1], F32, name="zero", tag="root")
-        one = ring.tile([P, 1], F32, name="one", tag="root")
+        zero = ring.tile([P, 1], F32, name="zero", tag="root", align_bytes=64)
+        one = ring.tile([P, 1], F32, name="one", tag="root", align_bytes=64)
         nc.gpsimd.memset(zero[:], 0.0)
         nc.gpsimd.memset(one[:], 1.0)
         ident = keep.tile([P, P], F32, name="ident")
@@ -73,8 +72,8 @@ def tile_list_vegetation_change_indices_kernel(
         w1s = [keep.tile([P, 512], U8, name=f"w1s{b}", align_bytes=64) for b in range(PASSES)]
         for b in range(PASSES):
             nc.vector.tensor_copy(
-                w1w[b][:].rearrange("p (t m e) -> p t m e", t=PACK, e=2),
-                w1w_raw[b][:].rearrange("p (m t e) -> p t m e", t=PACK, e=2),
+                w1w[b][:].bitcast(U16).rearrange("p (t m) -> p t m", t=PACK),
+                w1w_raw[b][:].bitcast(U16).rearrange("p (m t) -> p t m", t=PACK),
             )
         tabw = keep.tile([P, T], I32, name="tabw", tag="then_table")
         nc.sync.dma_start(tabw[:], tab_words[0].rearrange("p t i -> p (t i)").bitcast(I32))
@@ -86,7 +85,7 @@ def tile_list_vegetation_change_indices_kernel(
                 w1s[b][:].rearrange("p (t m) -> p t m", t=PACK),
                 w1s_raw[:, 512 * b : 512 * (b + 1)].rearrange("p (m t) -> p t m", t=PACK),
             )
-        vw = [keep.tile([P, BANK], U32, name=f"vw{c}", align_bytes=64) for c in range(S // BANK)]
+        vw = [keep.tile([P, BANK], U32, name=f"vw{c}", tag=f"vw{c}", align_bytes=64) for c in range(S // BANK)]
         for c in range(S // BANK):
             nc.vector.tensor_copy(vw[c][:], tabw[:].bitcast(U32).indirect(offs_t[:, 32 * c : 32 * (c + 1)]))
 
@@ -95,9 +94,9 @@ def tile_list_vegetation_change_indices_kernel(
 
         h = [keep.tile([P, S], F32, name=f"h{j}") for j in range(SLICES)]
 
-        def respond(j, c):
+        def respond(psum, j, c):
             b, t = divmod(j, PACK)
-            acc = psum.tile([P, BANK], F32, name="acc", tag="acc", bufs=4)
+            acc = psum.tile([P, BANK], F32, name="acc")
             nc.tensor.matmul_mx(
                 out=acc[:],
                 lhsT=w1w[b][:, 256 * t : 256 * (t + 1)].bitcast(FP4X4),
@@ -109,47 +108,59 @@ def tile_list_vegetation_change_indices_kernel(
             )
             nc.scalar.activation(h[j][:, BANK * c : BANK * (c + 1)], acc[:], ACT.Sigmoid, bias=zero[:], scale=one[:])
 
-        for c in range(S // BANK):
-            for j in range(2):
-                respond(j, c)
-        for j in range(2, SLICES):
+        with tc.psum_pool(name="first", bufs=8) as first:
             for c in range(S // BANK):
-                respond(j, c)
+                for j in range(2):
+                    respond(first, j, c)
+            for j in range(2, SLICES):
+                for c in range(S // BANK):
+                    respond(first, j, c)
+        psum = ctx.enter_context(tc.psum_pool(name="psum", bufs=2))
 
         w2c = [keep.tile([P, N], U32, name=f"w2c{b}", align_bytes=64) for b in range(PASSES)]
         w2s = [keep.tile([P, N], U8, name=f"w2s{b}", align_bytes=64) for b in range(PASSES)]
-        w2b = [keep.tile([P, N * PACK], BF16, name=f"w2b{b}", align_bytes=64) for b in range(PASSES)]
-        for b in range(PASSES):
+        w2b = [keep.tile([P, N * PACK], BF16, name=f"w2b{b}", tag=f"vw{b}", align_bytes=64) for b in range(PASSES)]
+
+        def round_w2(piece):
+            b, k = divmod(piece, 4)
             nc.scalar.copy(
-                w2b[b][:].rearrange("p (t m j) -> p m j t", t=PACK, j=PACK),
-                w2_raw[:, b, :].rearrange("p (j m t) -> p m j t", j=PACK, t=PACK),
+                w2b[b][:].rearrange("p (t m j) -> p m j t", t=PACK, j=PACK)[:, 32 * k : 32 * (k + 1)],
+                w2_raw[:, b, :].rearrange("p (j m t) -> p m j t", j=PACK, t=PACK)[:, 32 * k : 32 * (k + 1)],
             )
 
         early = [[keep.tile([P, HALF], F32, name=f"early{j}_{u}") for u in range(2)] for j in range(SLICES)]
         diff = [[keep.tile([P, HALF], F32, name=f"diff{j}_{u}") for u in range(2)] for j in range(SLICES)]
-        for j in range(SLICES):
-            for u in range(2):
+        def pick(units):
+            for j, u in units:
                 nc.vector.tensor_copy(early[j][u][:], h[j][:].indirect(pos2_t[:, 24 * u : 24 * (u + 1)]))
-            for u in range(2):
+            for j, u in units:
                 nc.vector.tensor_tensor(
                     diff[j][u][:], h[j][:].indirect(pos1_t[:, 24 * u : 24 * (u + 1)]), early[j][u][:], ALU.subtract
                 )
-        for j in range(SLICES):
-            for u in range(2):
-                total = psum.tile([P, HALF], F32, name="total", tag="total")
-                for k in range(HALF // P):
-                    cols = slice(P * k, P * (k + 1))
-                    for n, src in enumerate((early[j][u], early[j][u], diff[j][u])):
-                        nc.tensor.matmul(
-                            total[:, cols], src[:, cols], ident[:], start=(n == 0), stop=(n == 2), is_transpose=True
-                        )
-                root = ring.tile([P, HALF], F32, name="root", tag="root")
-                nc.scalar.activation(root[:], total[:], ACT.Abs_reciprocal_sqrt)
-                back = psum.tile([P, HALF], F32, name="back", tag="back")
-                for k in range(HALF // P):
-                    cols = slice(P * k, P * (k + 1))
-                    nc.tensor.transpose(back[:, cols], root[:, cols], ident[:])
-                nc.scalar.activation(early[j][u][:], back[:], ACT.Square)
+
+        def invert(j, u):
+            total = psum.tile([P, HALF], F32, name="total", tag="total", bufs=3)
+            for k in range(HALF // P):
+                cols = slice(P * k, P * (k + 1))
+                for n, src in enumerate((early[j][u], early[j][u], diff[j][u])):
+                    nc.tensor.matmul(
+                        total[:, cols], src[:, cols], ident[:], start=(n == 0), stop=(n == 2), is_transpose=True
+                    )
+            root = ring.tile([P, HALF], F32, name="root", tag="root", align_bytes=64)
+            nc.scalar.activation(root[:], total[:], ACT.Abs_reciprocal_sqrt)
+            back = psum.tile([P, HALF], F32, name="back", tag="back")
+            for k in range(HALF // P):
+                cols = slice(P * k, P * (k + 1))
+                nc.tensor.transpose(back[:, cols], root[:, cols], ident[:])
+            nc.scalar.activation(early[j][u][:], back[:], ACT.Square)
+
+        units = [(j, u) for j in range(PACK) for u in range(2)] + [(j, u) for u in range(2) for j in range(PACK, SLICES)]
+        for n in range(0, len(units), 2):
+            pick(units[n : n + 2])
+        for n, (j, u) in enumerate(units):
+            invert(j, u)
+            if 2 <= n < 10:
+                round_w2(n - 2)
 
         for b in range(PASSES):
             nc.vector.quantize_mx(out=w2c[b][:].bitcast(FP8X4), scales=w2s[b][:], in_=w2b[b][:])
@@ -174,9 +185,10 @@ def tile_list_vegetation_change_indices_kernel(
                         )
 
         def quantise_z(b, c0, c1):
-            woven = ring.tile([P, 512 * PACK], BF16, name="woven", tag="woven", align_bytes=64)
+            tag, weave = ("root", nc.scalar.copy) if b == 0 else ("woven", nc.vector.tensor_copy)
+            woven = ring.tile([P, 512 * PACK], BF16, name="woven", tag=tag, align_bytes=64)
             w = c1 - c0
-            nc.vector.tensor_copy(
+            weave(
                 woven[:, 0 : w * PACK].rearrange("p (c i t) -> p c t i", i=4, t=PACK),
                 zrow[b][:, :, c0:c1].rearrange("p t (c i) -> p c t i", i=4),
             )
@@ -193,7 +205,7 @@ def tile_list_vegetation_change_indices_kernel(
             yf = ring.tile([P, PACK, 256], F32, name="yf", tag="yf")
             for s0 in range(c0, c1, Y_COLS):
                 cols = slice(s0, s0 + Y_COLS)
-                acc = psum.tile([P, PACK, Y_COLS], F32, name="yacc", tag="acc", bufs=4)
+                acc = psum.tile([P, PACK, Y_COLS], F32, name="yacc", tag="acc", bufs=3)
                 for t in range(PACK):
                     for b in range(PASSES):
                         nc.tensor.matmul_mx(
@@ -213,9 +225,9 @@ def tile_list_vegetation_change_indices_kernel(
             nc.sync.dma_start(out_words[:, c0:c1], yc[:, c0:c1].bitcast(I32))
 
         ratio(0, 0, PAIRS)
-        quantise_z(0, 0, 512)
-        quantise_z(0, 512, PAIRS)
-        for c0, c1 in ((0, 256), (256, 512), (512, 640), (640, 768)):
+        quantise_z(0, 0, 256)
+        quantise_z(0, 256, PAIRS)
+        for c0, c1 in ((0, 256), (256, 384), (384, 640), (640, 768)):
             ratio(1, c0, c1)
             quantise_z(1, c0, c1)
             mix(c0, c1)

@@ -24,6 +24,7 @@ SLICES = H // P
 BANK = 512
 HALF = PAIRS // 2
 Y_COLS = 128
+BY_TENSOR = 4
 
 
 def tile_list_vegetation_change_indices_kernel(
@@ -128,21 +129,31 @@ def tile_list_vegetation_change_indices_kernel(
                 w2_raw[:, b, :].rearrange("p (j m t) -> p m j t", j=PACK, t=PACK)[:, 32 * k : 32 * (k + 1)],
             )
 
-        early = [[keep.tile([P, HALF], F32, name=f"early{j}_{u}") for u in range(2)] for j in range(SLICES)]
-        diff = [[keep.tile([P, HALF], F32, name=f"diff{j}_{u}") for u in range(2)] for j in range(SLICES)]
-        def pick(units):
-            for j, u in units:
-                nc.vector.tensor_copy(early[j][u][:], h[j][:].indirect(pos2_t[:, 24 * u : 24 * (u + 1)]))
-            for j, u in units:
+        units = [(j, u) for j in range(PACK) for u in range(2)] + [(j, u) for u in range(2) for j in range(PACK, SLICES)]
+        early = [keep.tile([P, 2, HALF], F32, name=f"early{n}") for n in range(SLICES)]
+        diff = [keep.tile([P, 2, HALF], F32, name=f"diff{n}") for n in range(SLICES)]
+
+        def of_unit(tiles, j, u):
+            n, side = divmod(units.index((j, u)), 2)
+            return tiles[n][:, side, :]
+
+        def pick(n):
+            for j, u in units[2 * n : 2 * n + 2]:
+                nc.vector.tensor_copy(of_unit(early, j, u), h[j][:].indirect(pos2_t[:, 24 * u : 24 * (u + 1)]))
+            for j, u in units[2 * n : 2 * n + 2]:
                 nc.vector.tensor_tensor(
-                    diff[j][u][:], h[j][:].indirect(pos1_t[:, 24 * u : 24 * (u + 1)]), early[j][u][:], ALU.subtract
+                    of_unit(diff, j, u),
+                    h[j][:].indirect(pos1_t[:, 24 * u : 24 * (u + 1)]),
+                    of_unit(early, j, u),
+                    ALU.subtract,
                 )
 
-        def invert(j, u):
+        def invert_by_tensor(j, u):
+            b_half, d_half = of_unit(early, j, u), of_unit(diff, j, u)
             total = psum.tile([P, HALF], F32, name="total", tag="total", bufs=3)
             for k in range(HALF // P):
                 cols = slice(P * k, P * (k + 1))
-                for n, src in enumerate((early[j][u], early[j][u], diff[j][u])):
+                for n, src in enumerate((b_half, b_half, d_half)):
                     nc.tensor.matmul(
                         total[:, cols], src[:, cols], ident[:], start=(n == 0), stop=(n == 2), is_transpose=True
                     )
@@ -152,45 +163,64 @@ def tile_list_vegetation_change_indices_kernel(
             for k in range(HALF // P):
                 cols = slice(P * k, P * (k + 1))
                 nc.tensor.transpose(back[:, cols], root[:, cols], ident[:])
-            nc.scalar.activation(early[j][u][:], back[:], ACT.Square)
+            nc.scalar.activation(b_half, back[:], ACT.Square)
 
-        units = [(j, u) for j in range(PACK) for u in range(2)] + [(j, u) for u in range(2) for j in range(PACK, SLICES)]
-        for n in range(0, len(units), 2):
-            pick(units[n : n + 2])
-        for n, (j, u) in enumerate(units):
-            invert(j, u)
-            if 2 <= n < 10:
-                round_w2(n - 2)
+        sums = {}
+
+        def add_by_vector(n):
+            sums[n] = keep.tile([P, 2, HALF], F32, name=f"sum{n}")
+            nc.vector.scalar_tensor_tensor(sums[n][:], early[n][:], 2.0, diff[n][:], ALU.mult, ALU.add)
+
+        def invert_sum(n):
+            root = ring.tile([P, 2, HALF], F32, name="root2", tag="root", align_bytes=64)
+            nc.scalar.activation(root[:], sums[n][:], ACT.Abs_reciprocal_sqrt)
+            nc.scalar.activation(early[n][:], root[:], ACT.Square)
+
+        for n in range(SLICES):
+            pick(n)
+            if n - 1 >= BY_TENSOR:
+                add_by_vector(n - 1)
+        add_by_vector(SLICES - 1)
+        for n in range(SLICES):
+            if n < BY_TENSOR:
+                for j, u in units[2 * n : 2 * n + 2]:
+                    invert_by_tensor(j, u)
+            else:
+                invert_sum(n)
+            if 1 <= n < 5:
+                round_w2(2 * n - 2)
+                round_w2(2 * n - 1)
 
         for b in range(PASSES):
             nc.vector.quantize_mx(out=w2c[b][:].bitcast(FP8X4), scales=w2s[b][:], in_=w2b[b][:])
 
         zc = [keep.tile([P, PAIRS], U32, name=f"zc{b}", align_bytes=64) for b in range(PASSES)]
         zs = [keep.tile([P, PAIRS], U8, name=f"zs{b}", align_bytes=64) for b in range(PASSES)]
-        zrow = [keep.tile([P, PACK, PAIRS], BF16, name=f"zrow{b}") for b in range(PASSES)]
 
         def ratio(b, c0, c1):
+            zrow = ring.tile([P, PACK, 256], BF16, name="zrow", tag=f"zrow{b}")
             for t in range(PACK):
                 j = PACK * b + t
                 for u in range(2):
                     lo, hi = max(c0, HALF * u), min(c1, HALF * (u + 1))
                     if lo < hi:
                         nc.vector.scalar_tensor_tensor(
-                            zrow[b][:, t, lo:hi],
-                            diff[j][u][:, lo - HALF * u : hi - HALF * u],
+                            zrow[:, t, lo - c0 : hi - c0],
+                            of_unit(diff, j, u)[:, lo - HALF * u : hi - HALF * u],
                             g_t[:, b, t : t + 1],
-                            early[j][u][:, lo - HALF * u : hi - HALF * u],
+                            of_unit(early, j, u)[:, lo - HALF * u : hi - HALF * u],
                             ALU.mult,
                             ALU.mult,
                         )
+            return zrow
 
-        def quantise_z(b, c0, c1):
-            tag, weave = ("root", nc.scalar.copy) if b == 0 else ("woven", nc.vector.tensor_copy)
-            woven = ring.tile([P, 512 * PACK], BF16, name="woven", tag=tag, align_bytes=64)
+        def quantise_z(zrow, b, c0, c1, on_scalar):
+            tag, weave = ("root", nc.scalar.copy) if on_scalar else ("woven", nc.vector.tensor_copy)
+            woven = ring.tile([P, 256 * PACK], BF16, name="woven", tag=tag, align_bytes=64)
             w = c1 - c0
             weave(
                 woven[:, 0 : w * PACK].rearrange("p (c i t) -> p c t i", i=4, t=PACK),
-                zrow[b][:, :, c0:c1].rearrange("p t (c i) -> p c t i", i=4),
+                zrow[:, :, 0:w].rearrange("p t (c i) -> p c t i", i=4),
             )
             nc.vector.quantize_mx(
                 out=zc[b][:, c0:c1].bitcast(FP8X4), scales=zs[b][:, c0:c1], in_=woven[:, 0 : w * PACK]
@@ -224,14 +254,12 @@ def tile_list_vegetation_change_indices_kernel(
             nc.sync.dma_start(out_rows[:, :, c0:c1], yf[:, :, 0 : c1 - c0])
             nc.sync.dma_start(out_words[:, c0:c1], yc[:, c0:c1].bitcast(I32))
 
-        ratio(0, 0, PAIRS)
-        quantise_z(0, 0, 256)
-        quantise_z(0, 256, PAIRS)
         for c0, c1 in ((0, 256), (256, 384), (384, 640), (640, 768)):
-            ratio(1, c0, c1)
-            quantise_z(1, c0, c1)
+            zrows = [ratio(b, c0, c1) for b in range(PASSES)]
+            quantise_z(zrows[0], 0, c0, c1, c0 < HALF)
+            quantise_z(zrows[1], 1, c0, c1, False)
             mix(c0, c1)
         for q in range(4):
-            nc.scalar.dma_start(
+            (nc.scalar, nc.sync)[q % 2].dma_start(
                 out_2[0, 4 * q : 4 * q + 4, :].bitcast(I32), ys[32 * q : 32 * q + 4, :].bitcast(I32)
             )

@@ -1,7 +1,6 @@
 from contextlib import ExitStack
 
 import concourse.mybir as mybir
-from concourse.masks import make_identity
 
 K, T, S, PAIRS, H, N = 512, 4096, 1536, 768, 1024, 512
 FLOPS = 2 * K * H * S + 2 * H * N * PAIRS
@@ -22,9 +21,8 @@ PACK = 4
 PASSES = H // (P * PACK)
 SLICES = H // P
 BANK = 512
-HALF = PAIRS // 2
 Y_COLS = 128
-BY_TENSOR = 4
+BY_GPSIMD = 6
 
 
 def tile_list_vegetation_change_indices_kernel(
@@ -40,55 +38,54 @@ def tile_list_vegetation_change_indices_kernel(
         pos2_t = keep.tile([P, PAIRS // 16], U16, name="pos2_t")
         tabs = keep.tile([P, T], U8, name="tabs")
         w1s_raw = keep.tile([P, H], U8, name="w1s_raw", tag="then_w2")
-        w1w_raw = [
-            keep.tile([P, H], U8, name="w1w_raw0", tag="then_table"),
-            keep.tile([P, H], U8, name="w1w_raw1"),
-        ]
         g_t = keep.tile([P, PASSES, PACK], F32, name="g_t")
+        zero = ring.tile([P, 1], F32, name="zero", tag="root", align_bytes=64)
+        one = ring.tile([P, 1], F32, name="one", tag="root", align_bytes=64)
+        seed_zero = keep.tile([P, 1], F32, name="seed_zero", tag="then_table")
+        seed_one = keep.tile([P, 1], F32, name="seed_one", tag="then_w1")
         nc.vector.memset(tabs[:].bitcast(I32), 0)
+        nc.vector.memset(seed_zero[:], 0.0)
+        nc.vector.tensor_copy(zero[:], seed_zero[:])
+        nc.vector.memset(seed_one[:], 1.0)
+        nc.vector.tensor_copy(one[:], seed_one[:])
         nc.vector.memset(w1s_raw[:].bitcast(I32), 0)
-        nc.sync.dma_start(w1w_raw[0][:].bitcast(I32), w1_words[0, :, 0:H].bitcast(I32))
         nc.sync.dma_start(offs_t[:], offs)
-        nc.sync.dma_start(w1w_raw[1][:].bitcast(I32), w1_words[0, :, H : 2 * H].bitcast(I32))
         nc.sync.dma_start(pos2_t[:], pos2)
         nc.sync.dma_start(pos1_t[:], pos1)
         for q in range(4):
-            nc.sync.dma_start(
+            (nc.sync, nc.scalar)[q % 2].dma_start(
                 tabs[32 * q : 32 * q + 4, :].bitcast(I32), tab_scales[0, 4 * q : 4 * q + 4, :].bitcast(I32)
             )
+        tabw = keep.tile([P, T], I32, name="tabw", tag="then_table")
+        nc.sync.dma_start(tabw[:], tab_words[0].rearrange("p t i -> p (t i)").bitcast(I32))
+        w1w_raw = keep.tile([P, 2 * H], U8, name="w1w_raw", tag="then_w1")
+        nc.scalar.dma_start(w1w_raw[:].bitcast(I32), w1_words[0].bitcast(I32))
         for q in range(4):
-            nc.sync.dma_start(
+            nc.scalar.dma_start(
                 w1s_raw[32 * q : 32 * q + 4, :].bitcast(I32), w1_scales[0, 4 * q : 4 * q + 4, :].bitcast(I32)
             )
         nc.gpsimd.dma_start(g_t[:], g.rearrange("(b p t) -> p b t", b=PASSES, t=PACK))
 
-        zero = ring.tile([P, 1], F32, name="zero", tag="root", align_bytes=64)
-        one = ring.tile([P, 1], F32, name="one", tag="root", align_bytes=64)
-        nc.gpsimd.memset(zero[:], 0.0)
-        nc.gpsimd.memset(one[:], 1.0)
-        ident = keep.tile([P, P], F32, name="ident")
-        make_identity(nc, ident[:])
-
         w1w = [keep.tile([P, 1024], U8, name=f"w1w{b}", align_bytes=64) for b in range(PASSES)]
         w1s = [keep.tile([P, 512], U8, name=f"w1s{b}", align_bytes=64) for b in range(PASSES)]
-        for b in range(PASSES):
+
+        def deal_w1(b):
             nc.vector.tensor_copy(
                 w1w[b][:].bitcast(U16).rearrange("p (t m) -> p t m", t=PACK),
-                w1w_raw[b][:].bitcast(U16).rearrange("p (m t) -> p t m", t=PACK),
+                w1w_raw[:, H * b : H * (b + 1)].bitcast(U16).rearrange("p (m t) -> p t m", t=PACK),
             )
-        tabw = keep.tile([P, T], I32, name="tabw", tag="then_table")
-        nc.sync.dma_start(tabw[:], tab_words[0].rearrange("p t i -> p (t i)").bitcast(I32))
-
-        vs = keep.tile([P, S], U8, name="vs", align_bytes=64)
-        nc.vector.tensor_copy(vs[:], tabs[:].indirect(offs_t[:]))
-        for b in range(PASSES):
             nc.vector.tensor_copy(
                 w1s[b][:].rearrange("p (t m) -> p t m", t=PACK),
                 w1s_raw[:, 512 * b : 512 * (b + 1)].rearrange("p (m t) -> p t m", t=PACK),
             )
+
+        vs = keep.tile([P, S], U8, name="vs", align_bytes=64)
+        nc.vector.tensor_copy(vs[:], tabs[:].indirect(offs_t[:]))
+        deal_w1(0)
         vw = [keep.tile([P, BANK], U32, name=f"vw{c}", tag=f"vw{c}", align_bytes=64) for c in range(S // BANK)]
         for c in range(S // BANK):
             nc.vector.tensor_copy(vw[c][:], tabw[:].bitcast(U32).indirect(offs_t[:, 32 * c : 32 * (c + 1)]))
+        deal_w1(1)
 
         w2_raw = keep.tile([P, PASSES, PACK * N], F32, name="w2_raw", tag="then_w2")
         nc.sync.dma_start(w2_raw[:], w2.rearrange("(b p j) n -> p b (j n)", b=PASSES, j=PACK))
@@ -116,137 +113,99 @@ def tile_list_vegetation_change_indices_kernel(
             for j in range(2, SLICES):
                 for c in range(S // BANK):
                     respond(first, j, c)
-        psum = ctx.enter_context(tc.psum_pool(name="psum", bufs=2))
+        psum = ctx.enter_context(tc.psum_pool(name="psum", bufs=1))
 
         w2c = [keep.tile([P, N], U32, name=f"w2c{b}", align_bytes=64) for b in range(PASSES)]
         w2s = [keep.tile([P, N], U8, name=f"w2s{b}", align_bytes=64) for b in range(PASSES)]
         w2b = [keep.tile([P, N * PACK], BF16, name=f"w2b{b}", tag=f"vw{b}", align_bytes=64) for b in range(PASSES)]
 
-        def round_w2(piece):
-            b, k = divmod(piece, 4)
+        def round_w2(b):
             nc.scalar.copy(
-                w2b[b][:].rearrange("p (t m j) -> p m j t", t=PACK, j=PACK)[:, 32 * k : 32 * (k + 1)],
-                w2_raw[:, b, :].rearrange("p (j m t) -> p m j t", j=PACK, t=PACK)[:, 32 * k : 32 * (k + 1)],
+                w2b[b][:].rearrange("p (t m j) -> p m j t", t=PACK, j=PACK),
+                w2_raw[:, b, :].rearrange("p (j m t) -> p m j t", j=PACK, t=PACK),
             )
 
-        units = [(j, u) for j in range(PACK) for u in range(2)] + [(j, u) for u in range(2) for j in range(PACK, SLICES)]
-        early = [keep.tile([P, 2, HALF], F32, name=f"early{n}") for n in range(SLICES)]
-        diff = [keep.tile([P, 2, HALF], F32, name=f"diff{n}") for n in range(SLICES)]
-
-        def of_unit(tiles, j, u):
-            n, side = divmod(units.index((j, u)), 2)
-            return tiles[n][:, side, :]
-
-        def pick(n):
-            for j, u in units[2 * n : 2 * n + 2]:
-                nc.vector.tensor_copy(of_unit(early, j, u), h[j][:].indirect(pos2_t[:, 24 * u : 24 * (u + 1)]))
-            for j, u in units[2 * n : 2 * n + 2]:
-                nc.vector.tensor_tensor(
-                    of_unit(diff, j, u),
-                    h[j][:].indirect(pos1_t[:, 24 * u : 24 * (u + 1)]),
-                    of_unit(early, j, u),
-                    ALU.subtract,
-                )
-
-        def invert_by_tensor(j, u):
-            b_half, d_half = of_unit(early, j, u), of_unit(diff, j, u)
-            total = psum.tile([P, HALF], F32, name="total", tag="total", bufs=3)
-            for k in range(HALF // P):
-                cols = slice(P * k, P * (k + 1))
-                for n, src in enumerate((b_half, b_half, d_half)):
-                    nc.tensor.matmul(
-                        total[:, cols], src[:, cols], ident[:], start=(n == 0), stop=(n == 2), is_transpose=True
-                    )
-            root = ring.tile([P, HALF], F32, name="root", tag="root", align_bytes=64)
-            nc.scalar.activation(root[:], total[:], ACT.Abs_reciprocal_sqrt)
-            back = psum.tile([P, HALF], F32, name="back", tag="back")
-            for k in range(HALF // P):
-                cols = slice(P * k, P * (k + 1))
-                nc.tensor.transpose(back[:, cols], root[:, cols], ident[:])
-            nc.scalar.activation(b_half, back[:], ACT.Square)
-
-        sums = {}
-
-        def add_by_vector(n):
-            sums[n] = keep.tile([P, 2, HALF], F32, name=f"sum{n}")
-            nc.vector.scalar_tensor_tensor(sums[n][:], early[n][:], 2.0, diff[n][:], ALU.mult, ALU.add)
-
-        def invert_sum(n):
-            root = ring.tile([P, 2, HALF], F32, name="root2", tag="root", align_bytes=64)
-            nc.scalar.activation(root[:], sums[n][:], ACT.Abs_reciprocal_sqrt)
-            nc.scalar.activation(early[n][:], root[:], ACT.Square)
-
-        for n in range(SLICES):
-            pick(n)
-            if n - 1 >= BY_TENSOR:
-                add_by_vector(n - 1)
-        add_by_vector(SLICES - 1)
-        for n in range(SLICES):
-            if n < BY_TENSOR:
-                for j, u in units[2 * n : 2 * n + 2]:
-                    invert_by_tensor(j, u)
-            else:
-                invert_sum(n)
-            if 1 <= n < 5:
-                round_w2(2 * n - 2)
-                round_w2(2 * n - 1)
-
-        for b in range(PASSES):
-            nc.vector.quantize_mx(out=w2c[b][:].bitcast(FP8X4), scales=w2s[b][:], in_=w2b[b][:])
+        diff = [keep.tile([P, PACK, PAIRS], F32, name=f"diff{b}") for b in range(PASSES)]
+        total = [keep.tile([P, PACK, PAIRS], F32, name=f"total{b}") for b in range(PASSES)]
+        early = {}
+        for j in range(SLICES):
+            b, t = divmod(j, PACK)
+            early[j] = ring.tile([P, PAIRS], F32, name="early", tag="early", bufs=3)
+            nc.vector.tensor_copy(early[j][:], h[j][:].indirect(pos2_t[:]))
+            if j < BY_GPSIMD:
+                late = ring.tile([P, PAIRS], F32, name="late", tag="late", bufs=3)
+                nc.vector.tensor_copy(late[:], h[j][:].indirect(pos1_t[:]))
+                nc.gpsimd.tensor_tensor(total[b][:, t, :], late[:], early[j][:], ALU.add)
+                nc.gpsimd.tensor_tensor(diff[b][:, t, :], late[:], early[j][:], ALU.subtract)
+        for j in range(BY_GPSIMD, SLICES):
+            b, t = divmod(j, PACK)
+            nc.vector.tensor_tensor(diff[b][:, t, :], h[j][:].indirect(pos1_t[:]), early[j][:], ALU.subtract)
+        for j in range(BY_GPSIMD, SLICES):
+            b, t = divmod(j, PACK)
+            nc.vector.scalar_tensor_tensor(total[b][:, t, :], early[j][:], 2.0, diff[b][:, t, :], ALU.mult, ALU.add)
+        for j in range(SLICES):
+            b, t = divmod(j, PACK)
+            root = ring.tile([P, PAIRS], F32, name="root", tag="root", align_bytes=64)
+            nc.scalar.activation(root[:], total[b][:, t, :], ACT.Abs_reciprocal_sqrt)
+            nc.scalar.activation(total[b][:, t, :], root[:], ACT.Square)
+            if PACK - 1 <= j < PACK - 1 + PASSES:
+                round_w2(j - PACK + 1)
 
         zc = [keep.tile([P, PAIRS], U32, name=f"zc{b}", align_bytes=64) for b in range(PASSES)]
         zs = [keep.tile([P, PAIRS], U8, name=f"zs{b}", align_bytes=64) for b in range(PASSES)]
 
         def ratio(b, c0, c1):
-            zrow = ring.tile([P, PACK, 256], BF16, name="zrow", tag=f"zrow{b}")
+            zrow = ring.tile([P, PACK, 256], BF16, name="zrow", tag="zrow")
             for t in range(PACK):
-                j = PACK * b + t
-                for u in range(2):
-                    lo, hi = max(c0, HALF * u), min(c1, HALF * (u + 1))
-                    if lo < hi:
-                        nc.vector.scalar_tensor_tensor(
-                            zrow[:, t, lo - c0 : hi - c0],
-                            of_unit(diff, j, u)[:, lo - HALF * u : hi - HALF * u],
-                            g_t[:, b, t : t + 1],
-                            of_unit(early, j, u)[:, lo - HALF * u : hi - HALF * u],
-                            ALU.mult,
-                            ALU.mult,
-                        )
+                nc.vector.scalar_tensor_tensor(
+                    zrow[:, t, 0 : c1 - c0],
+                    diff[b][:, t, c0:c1],
+                    g_t[:, b, t : t + 1],
+                    total[b][:, t, c0:c1],
+                    ALU.mult,
+                    ALU.mult,
+                )
             return zrow
 
-        def quantise_z(zrow, b, c0, c1, on_scalar):
-            tag, weave = ("root", nc.scalar.copy) if on_scalar else ("woven", nc.vector.tensor_copy)
-            woven = ring.tile([P, 256 * PACK], BF16, name="woven", tag=tag, align_bytes=64)
+        def weave(zrow, c0, c1):
+            woven = ring.tile([P, 256 * PACK], BF16, name="woven", tag="woven", align_bytes=64)
             w = c1 - c0
-            weave(
+            nc.vector.tensor_copy(
                 woven[:, 0 : w * PACK].rearrange("p (c i t) -> p c t i", i=4, t=PACK),
                 zrow[:, :, 0:w].rearrange("p t (c i) -> p c t i", i=4),
             )
+            return woven
+
+        def quantise_z(woven, b, c0, c1):
             nc.vector.quantize_mx(
-                out=zc[b][:, c0:c1].bitcast(FP8X4), scales=zs[b][:, c0:c1], in_=woven[:, 0 : w * PACK]
+                out=zc[b][:, c0:c1].bitcast(FP8X4), scales=zs[b][:, c0:c1], in_=woven[:, 0 : (c1 - c0) * PACK]
             )
 
         yc = keep.tile([P, PAIRS], U32, name="yc", align_bytes=64)
         ys = keep.tile([P, PAIRS], U8, name="ys", align_bytes=64)
         out_rows = out_0.rearrange("(p t) q -> p t q", t=PACK)
         out_words = out_1[0].rearrange("p m t -> p (m t)").bitcast(I32)
+        yacc = [psum.tile([P, PACK, Y_COLS], F32, name=f"yacc{s}") for s in range(PAIRS // Y_COLS)]
 
-        def mix(c0, c1):
+        def mix(b, c0, c1):
+            for s0 in range(c0, c1, Y_COLS):
+                cols = slice(s0, s0 + Y_COLS)
+                for t in range(PACK):
+                    nc.tensor.matmul_mx(
+                        out=yacc[s0 // Y_COLS][:, t, :],
+                        lhsT=w2c[b][:, P * t : P * (t + 1)].bitcast(FP8X4),
+                        lhsT_scale=w2s[b][:, P * t : P * (t + 1)],
+                        rhs=zc[b][:, cols].bitcast(FP8X4),
+                        rhs_scale=zs[b][:, cols],
+                        start=(b == 0 and t == 0),
+                        stop=(b == PASSES - 1 and t == PACK - 1),
+                    )
+
+        def hand_out(c0, c1):
             yf = ring.tile([P, PACK, 256], F32, name="yf", tag="yf")
             for s0 in range(c0, c1, Y_COLS):
                 cols = slice(s0, s0 + Y_COLS)
-                acc = psum.tile([P, PACK, Y_COLS], F32, name="yacc", tag="acc", bufs=3)
-                for t in range(PACK):
-                    for b in range(PASSES):
-                        nc.tensor.matmul_mx(
-                            out=acc[:, t, :],
-                            lhsT=w2c[b][:, P * t : P * (t + 1)].bitcast(FP8X4),
-                            lhsT_scale=w2s[b][:, P * t : P * (t + 1)],
-                            rhs=zc[b][:, cols].bitcast(FP8X4),
-                            rhs_scale=zs[b][:, cols],
-                            start=(b == 0),
-                            stop=(b == PASSES - 1),
-                        )
+                acc = yacc[s0 // Y_COLS]
                 yb = ring.tile([P, Y_COLS * PACK], BF16, name="yb", tag="yb", align_bytes=64)
                 nc.scalar.copy(yb[:].rearrange("p (n t) -> p n t", t=PACK), acc[:].rearrange("p t n -> p n t"))
                 nc.scalar.copy(yf[:, :, s0 - c0 : s0 - c0 + Y_COLS], acc[:])
@@ -254,11 +213,21 @@ def tile_list_vegetation_change_indices_kernel(
             nc.sync.dma_start(out_rows[:, :, c0:c1], yf[:, :, 0 : c1 - c0])
             nc.sync.dma_start(out_words[:, c0:c1], yc[:, c0:c1].bitcast(I32))
 
-        for c0, c1 in ((0, 256), (256, 384), (384, 640), (640, 768)):
-            zrows = [ratio(b, c0, c1) for b in range(PASSES)]
-            quantise_z(zrows[0], 0, c0, c1, c0 < HALF)
-            quantise_z(zrows[1], 1, c0, c1, False)
-            mix(c0, c1)
+        steps = [(0, 0, 256), (0, 256, 512), (0, 512, 768), (1, 0, 256), (1, 256, 512), (1, 512, 640), (1, 640, 768)]
+        zrows, wovens = {}, {}
+        for n in range(len(steps) + 2):
+            if n < len(steps):
+                zrows[n] = ratio(*steps[n])
+            if 0 <= n - 2 < len(steps):
+                b, c0, c1 = steps[n - 2]
+                quantise_z(wovens[n - 2], b, c0, c1)
+                if c0 == 0:
+                    nc.vector.quantize_mx(out=w2c[b][:].bitcast(FP8X4), scales=w2s[b][:], in_=w2b[b][:])
+                mix(b, c0, c1)
+                if b == PASSES - 1:
+                    hand_out(c0, c1)
+            if 0 <= n - 1 < len(steps):
+                wovens[n - 1] = weave(zrows[n - 1], *steps[n - 1][1:])
         for q in range(4):
             (nc.scalar, nc.sync)[q % 2].dma_start(
                 out_2[0, 4 * q : 4 * q + 4, :].bitcast(I32), ys[32 * q : 32 * q + 4, :].bitcast(I32)

@@ -22,7 +22,7 @@ PASSES = H // (P * PACK)
 SLICES = H // P
 BANK = 512
 Y_COLS = 128
-BY_GPSIMD = 6
+BY_GPSIMD = 5
 
 
 def tile_list_vegetation_change_indices_kernel(
@@ -36,8 +36,8 @@ def tile_list_vegetation_change_indices_kernel(
         offs_t = keep.tile([P, S // 16], U16, name="offs_t")
         pos1_t = keep.tile([P, PAIRS // 16], U16, name="pos1_t")
         pos2_t = keep.tile([P, PAIRS // 16], U16, name="pos2_t")
-        tabs = keep.tile([P, T], U8, name="tabs")
-        w1s_raw = keep.tile([P, H], U8, name="w1s_raw", tag="then_w2")
+        tabs = keep.tile([P, T], U8, name="tabs", tag="then_w2")
+        w1s_raw = keep.tile([P, H], U8, name="w1s_raw")
         g_t = keep.tile([P, PASSES, PACK], F32, name="g_t")
         zero = ring.tile([P, 1], F32, name="zero", tag="root", align_bytes=64)
         one = ring.tile([P, 1], F32, name="one", tag="root", align_bytes=64)
@@ -64,6 +64,8 @@ def tile_list_vegetation_change_indices_kernel(
             nc.scalar.dma_start(
                 w1s_raw[32 * q : 32 * q + 4, :].bitcast(I32), w1_scales[0, 4 * q : 4 * q + 4, :].bitcast(I32)
             )
+        warm = keep.tile([P, 1], F32, name="warm")
+        nc.scalar.activation(warm[:], zero[:], ACT.Sigmoid, bias=zero[:], scale=one[:])
         nc.gpsimd.dma_start(g_t[:], g.rearrange("(b p t) -> p b t", b=PASSES, t=PACK))
 
         w1w = [keep.tile([P, 1024], U8, name=f"w1w{b}", align_bytes=64) for b in range(PASSES)]
@@ -117,69 +119,70 @@ def tile_list_vegetation_change_indices_kernel(
 
         w2c = [keep.tile([P, N], U32, name=f"w2c{b}", align_bytes=64) for b in range(PASSES)]
         w2s = [keep.tile([P, N], U8, name=f"w2s{b}", align_bytes=64) for b in range(PASSES)]
-        w2b = [keep.tile([P, N * PACK], BF16, name=f"w2b{b}", tag=f"vw{b}", align_bytes=64) for b in range(PASSES)]
+        w2b = [keep.tile([P, N * PACK], BF16, name=f"w2b{b}", align_bytes=64) for b in range(PASSES)]
 
-        def round_w2(b):
-            nc.scalar.copy(
-                w2b[b][:].rearrange("p (t m j) -> p m j t", t=PACK, j=PACK),
-                w2_raw[:, b, :].rearrange("p (j m t) -> p m j t", j=PACK, t=PACK),
+        for b in range(PASSES):
+            nc.gpsimd.tensor_scalar(
+                w2b[b][:].rearrange("p (t m j) -> p t m j", t=PACK, j=PACK),
+                w2_raw[:, b, :].rearrange("p (j m t) -> p t m j", j=PACK, t=PACK),
+                1.0,
+                0.0,
+                ALU.mult,
+                ALU.add,
             )
 
-        diff = [keep.tile([P, PACK, PAIRS], F32, name=f"diff{b}") for b in range(PASSES)]
-        total = [keep.tile([P, PACK, PAIRS], F32, name=f"total{b}") for b in range(PASSES)]
-        early = {}
+        early, diff, total = {}, {}, {}
         for j in range(SLICES):
-            b, t = divmod(j, PACK)
-            early[j] = ring.tile([P, PAIRS], F32, name="early", tag="early", bufs=3)
+            early[j] = keep.tile([P, PAIRS], F32, name=f"early{j}")
+            total[j] = keep.tile([P, PAIRS], F32, name=f"total{j}")
             nc.vector.tensor_copy(early[j][:], h[j][:].indirect(pos2_t[:]))
             if j < BY_GPSIMD:
-                late = ring.tile([P, PAIRS], F32, name="late", tag="late", bufs=3)
+                late = keep.tile([P, PAIRS], F32, name=f"late{j}", tag=f"late{j}")
+                diff[j] = keep.tile([P, PAIRS], F32, name=f"diff{j}", tag=f"diff{j}")
                 nc.vector.tensor_copy(late[:], h[j][:].indirect(pos1_t[:]))
-                nc.gpsimd.tensor_tensor(total[b][:, t, :], late[:], early[j][:], ALU.add)
-                nc.gpsimd.tensor_tensor(diff[b][:, t, :], late[:], early[j][:], ALU.subtract)
-        for j in range(BY_GPSIMD, SLICES):
-            b, t = divmod(j, PACK)
-            nc.vector.tensor_tensor(diff[b][:, t, :], h[j][:].indirect(pos1_t[:]), early[j][:], ALU.subtract)
-        for j in range(BY_GPSIMD, SLICES):
-            b, t = divmod(j, PACK)
-            nc.vector.scalar_tensor_tensor(total[b][:, t, :], early[j][:], 2.0, diff[b][:, t, :], ALU.mult, ALU.add)
-        for j in range(SLICES):
-            b, t = divmod(j, PACK)
+                nc.gpsimd.tensor_tensor(total[j][:], late[:], early[j][:], ALU.add)
+                nc.gpsimd.tensor_tensor(diff[j][:], late[:], early[j][:], ALU.subtract)
+
+        def invert(j):
             root = ring.tile([P, PAIRS], F32, name="root", tag="root", align_bytes=64)
-            nc.scalar.activation(root[:], total[b][:, t, :], ACT.Abs_reciprocal_sqrt)
-            nc.scalar.activation(total[b][:, t, :], root[:], ACT.Square)
-            if PACK - 1 <= j < PACK - 1 + PASSES:
-                round_w2(j - PACK + 1)
+            nc.scalar.activation(root[:], total[j][:], ACT.Abs_reciprocal_sqrt)
+            nc.scalar.activation(total[j][:], root[:], ACT.Square)
+
+        def ratio(zrow, b, c0, c1):
+            for t in range(PACK):
+                j = PACK * b + t
+                nc.vector.scalar_tensor_tensor(
+                    zrow[:, t, 0 : c1 - c0],
+                    diff[j][:, c0:c1],
+                    g_t[:, b, t : t + 1],
+                    total[j][:, c0:c1],
+                    ALU.mult,
+                    ALU.mult,
+                )
+
+        def weave(copy, woven, zrow, w):
+            copy(
+                woven[:, 0 : w * PACK].rearrange("p (c i t) -> p c t i", i=4, t=PACK),
+                zrow[:, :, 0:w].rearrange("p t (c i) -> p c t i", i=4),
+            )
+
+        for j in range(BY_GPSIMD):
+            invert(j)
+        zrow0 = keep.tile([P, PACK, PAIRS], BF16, name="zrow0", tag=f"late{BY_GPSIMD - 1}")
+        ratio(zrow0, 0, 0, PAIRS)
+        woven0 = keep.tile([P, PAIRS * PACK], BF16, name="woven0", align_bytes=64)
+        weave(nc.scalar.copy, woven0, zrow0, PAIRS)
+        for j in range(BY_GPSIMD, SLICES):
+            diff[j] = keep.tile([P, PAIRS], F32, name=f"diff{j}", tag=f"diff{j - PACK}")
+            nc.vector.tensor_tensor(diff[j][:], h[j][:].indirect(pos1_t[:]), early[j][:], ALU.subtract)
+            nc.vector.scalar_tensor_tensor(total[j][:], early[j][:], 2.0, diff[j][:], ALU.mult, ALU.add)
+            invert(j)
 
         zc = [keep.tile([P, PAIRS], U32, name=f"zc{b}", align_bytes=64) for b in range(PASSES)]
         zs = [keep.tile([P, PAIRS], U8, name=f"zs{b}", align_bytes=64) for b in range(PASSES)]
 
-        def ratio(b, c0, c1):
-            zrow = ring.tile([P, PACK, 256], BF16, name="zrow", tag="zrow")
-            for t in range(PACK):
-                nc.vector.scalar_tensor_tensor(
-                    zrow[:, t, 0 : c1 - c0],
-                    diff[b][:, t, c0:c1],
-                    g_t[:, b, t : t + 1],
-                    total[b][:, t, c0:c1],
-                    ALU.mult,
-                    ALU.mult,
-                )
-            return zrow
-
-        def weave(zrow, c0, c1):
-            woven = ring.tile([P, 256 * PACK], BF16, name="woven", tag="woven", align_bytes=64)
-            w = c1 - c0
-            nc.vector.tensor_copy(
-                woven[:, 0 : w * PACK].rearrange("p (c i t) -> p c t i", i=4, t=PACK),
-                zrow[:, :, 0:w].rearrange("p t (c i) -> p c t i", i=4),
-            )
-            return woven
-
         def quantise_z(woven, b, c0, c1):
-            nc.vector.quantize_mx(
-                out=zc[b][:, c0:c1].bitcast(FP8X4), scales=zs[b][:, c0:c1], in_=woven[:, 0 : (c1 - c0) * PACK]
-            )
+            nc.vector.quantize_mx(out=zc[b][:, c0:c1].bitcast(FP8X4), scales=zs[b][:, c0:c1], in_=woven)
 
         yc = keep.tile([P, PAIRS], U32, name="yc", align_bytes=64)
         ys = keep.tile([P, PAIRS], U8, name="ys", align_bytes=64)
@@ -208,26 +211,33 @@ def tile_list_vegetation_change_indices_kernel(
                 acc = yacc[s0 // Y_COLS]
                 yb = ring.tile([P, Y_COLS * PACK], BF16, name="yb", tag="yb", align_bytes=64)
                 nc.scalar.copy(yb[:].rearrange("p (n t) -> p n t", t=PACK), acc[:].rearrange("p t n -> p n t"))
-                nc.scalar.copy(yf[:, :, s0 - c0 : s0 - c0 + Y_COLS], acc[:])
+                copy_out = nc.vector.tensor_copy if s0 >= PAIRS - 2 * Y_COLS else nc.scalar.copy
+                copy_out(yf[:, :, s0 - c0 : s0 - c0 + Y_COLS], acc[:])
                 nc.vector.quantize_mx(out=yc[:, cols].bitcast(FP8X4), scales=ys[:, cols], in_=yb[:])
             nc.sync.dma_start(out_rows[:, :, c0:c1], yf[:, :, 0 : c1 - c0])
             nc.sync.dma_start(out_words[:, c0:c1], yc[:, c0:c1].bitcast(I32))
 
-        steps = [(0, 0, 256), (0, 256, 512), (0, 512, 768), (1, 0, 256), (1, 256, 512), (1, 512, 640), (1, 640, 768)]
+        for b in range(PASSES):
+            nc.vector.quantize_mx(out=w2c[b][:].bitcast(FP8X4), scales=w2s[b][:], in_=w2b[b][:])
+        for c0, c1 in ((0, 512), (512, 768)):
+            quantise_z(woven0[:, PACK * c0 : PACK * c1], 0, c0, c1)
+        mix(0, 0, PAIRS)
+
+        runs = [(0, 128), (128, 384), (384, 640), (640, 768)]
         zrows, wovens = {}, {}
-        for n in range(len(steps) + 2):
-            if n < len(steps):
-                zrows[n] = ratio(*steps[n])
-            if 0 <= n - 2 < len(steps):
-                b, c0, c1 = steps[n - 2]
-                quantise_z(wovens[n - 2], b, c0, c1)
-                if c0 == 0:
-                    nc.vector.quantize_mx(out=w2c[b][:].bitcast(FP8X4), scales=w2s[b][:], in_=w2b[b][:])
-                mix(b, c0, c1)
-                if b == PASSES - 1:
-                    hand_out(c0, c1)
-            if 0 <= n - 1 < len(steps):
-                wovens[n - 1] = weave(zrows[n - 1], *steps[n - 1][1:])
+        for n in range(len(runs) + 2):
+            if n < len(runs):
+                zrows[n] = ring.tile([P, PACK, 256], BF16, name="zrow", tag="zrow")
+                ratio(zrows[n], 1, *runs[n])
+            if 0 <= n - 2 < len(runs):
+                c0, c1 = runs[n - 2]
+                quantise_z(wovens[n - 2][:, 0 : PACK * (c1 - c0)], 1, c0, c1)
+                mix(1, c0, c1)
+                hand_out(c0, c1)
+            if 0 <= n - 1 < len(runs):
+                c0, c1 = runs[n - 1]
+                wovens[n - 1] = ring.tile([P, 256 * PACK], BF16, name="woven", tag="woven", align_bytes=64)
+                weave(nc.vector.tensor_copy, wovens[n - 1], zrows[n - 1], c1 - c0)
         for q in range(4):
             (nc.scalar, nc.sync)[q % 2].dma_start(
                 out_2[0, 4 * q : 4 * q + 4, :].bitcast(I32), ys[32 * q : 32 * q + 4, :].bitcast(I32)

@@ -36,8 +36,7 @@ def tile_list_vegetation_change_indices_kernel(
         offs_t = keep.tile([P, S // 16], U16, name="offs_t")
         pos1_t = keep.tile([P, PAIRS // 16], U16, name="pos1_t")
         pos2_t = keep.tile([P, PAIRS // 16], U16, name="pos2_t")
-        tabs = keep.tile([P, T], U8, name="tabs", tag="then_w2")
-        w1s_raw = keep.tile([P, H], U8, name="w1s_raw")
+        tabs = keep.tile([P, T], U8, name="tabs", tag="then_w1s", align_bytes=64)
         g_t = keep.tile([P, PASSES, PACK], F32, name="g_t")
         zero = ring.tile([P, 1], F32, name="zero", tag="root", align_bytes=64)
         one = ring.tile([P, 1], F32, name="one", tag="root", align_bytes=64)
@@ -48,7 +47,6 @@ def tile_list_vegetation_change_indices_kernel(
         nc.vector.tensor_copy(zero[:], seed_zero[:])
         nc.vector.memset(seed_one[:], 1.0)
         nc.vector.tensor_copy(one[:], seed_one[:])
-        nc.vector.memset(w1s_raw[:].bitcast(I32), 0)
         nc.sync.dma_start(offs_t[:], offs)
         nc.sync.dma_start(pos2_t[:], pos2)
         nc.sync.dma_start(pos1_t[:], pos1)
@@ -60,36 +58,39 @@ def tile_list_vegetation_change_indices_kernel(
         nc.sync.dma_start(tabw[:], tab_words[0].rearrange("p t i -> p (t i)").bitcast(I32))
         w1w_raw = keep.tile([P, 2 * H], U8, name="w1w_raw", tag="then_w1")
         nc.scalar.dma_start(w1w_raw[:].bitcast(I32), w1_words[0].bitcast(I32))
-        for q in range(4):
-            nc.scalar.dma_start(
-                w1s_raw[32 * q : 32 * q + 4, :].bitcast(I32), w1_scales[0, 4 * q : 4 * q + 4, :].bitcast(I32)
-            )
         warm = keep.tile([P, 1], F32, name="warm")
         nc.scalar.activation(warm[:], zero[:], ACT.Sigmoid, bias=zero[:], scale=one[:])
         nc.gpsimd.dma_start(g_t[:], g.rearrange("(b p t) -> p b t", b=PASSES, t=PACK))
 
         w1w = [keep.tile([P, 1024], U8, name=f"w1w{b}", align_bytes=64) for b in range(PASSES)]
-        w1s = [keep.tile([P, 512], U8, name=f"w1s{b}", align_bytes=64) for b in range(PASSES)]
+        w1s = keep.tile([P, H], U8, name="w1s", align_bytes=64)
 
-        def deal_w1(b):
+        vs = keep.tile([P, S], U8, name="vs", align_bytes=64)
+        nc.vector.tensor_copy(vs[:], tabs[:].indirect(offs_t[:]))
+        w1s_raw = keep.tile([P, H], U8, name="w1s_raw", tag="then_w1s", align_bytes=64)
+        nc.vector.memset(w1s_raw[:].bitcast(I32), 0)
+        for q in range(4):
+            (nc.sync, nc.scalar)[q % 2].dma_start(
+                w1s_raw[32 * q : 32 * q + 4, :].bitcast(I32), w1_scales[0, 4 * q : 4 * q + 4, :].bitcast(I32)
+            )
+        for b in range(PASSES):
             nc.vector.tensor_copy(
                 w1w[b][:].bitcast(U16).rearrange("p (t m) -> p t m", t=PACK),
                 w1w_raw[:, H * b : H * (b + 1)].bitcast(U16).rearrange("p (m t) -> p t m", t=PACK),
             )
-            nc.vector.tensor_copy(
-                w1s[b][:].rearrange("p (t m) -> p t m", t=PACK),
-                w1s_raw[:, 512 * b : 512 * (b + 1)].rearrange("p (m t) -> p t m", t=PACK),
-            )
 
-        vs = keep.tile([P, S], U8, name="vs", align_bytes=64)
-        nc.vector.tensor_copy(vs[:], tabs[:].indirect(offs_t[:]))
-        deal_w1(0)
-        vw = [keep.tile([P, BANK], U32, name=f"vw{c}", tag=f"vw{c}", align_bytes=64) for c in range(S // BANK)]
+        vw = []
         for c in range(S // BANK):
+            last = c == S // BANK - 1
+            if last:
+                nc.vector.tensor_copy(
+                    w1s[:].rearrange("p (b t m) -> p b t m", b=PASSES, t=PACK),
+                    w1s_raw[:].rearrange("p (b m t) -> p b t m", b=PASSES, t=PACK),
+                )
+            vw.append(keep.tile([P, BANK], U32, name=f"vw{c}", tag="then_w1s" if last else f"vw{c}", align_bytes=64))
             nc.vector.tensor_copy(vw[c][:], tabw[:].bitcast(U32).indirect(offs_t[:, 32 * c : 32 * (c + 1)]))
-        deal_w1(1)
 
-        w2_raw = keep.tile([P, PASSES, PACK * N], F32, name="w2_raw", tag="then_w2")
+        w2_raw = keep.tile([P, PASSES, PACK * N], F32, name="w2_raw", tag="then_table")
         nc.sync.dma_start(w2_raw[:], w2.rearrange("(b p j) n -> p b (j n)", b=PASSES, j=PACK))
 
         h = [keep.tile([P, S], F32, name=f"h{j}") for j in range(SLICES)]
@@ -100,7 +101,7 @@ def tile_list_vegetation_change_indices_kernel(
             nc.tensor.matmul_mx(
                 out=acc[:],
                 lhsT=w1w[b][:, 256 * t : 256 * (t + 1)].bitcast(FP4X4),
-                lhsT_scale=w1s[b][:, P * t : P * (t + 1)],
+                lhsT_scale=w1s[:, P * j : P * (j + 1)],
                 rhs=vw[c][:].bitcast(FP8X4),
                 rhs_scale=vs[:, BANK * c : BANK * (c + 1)],
                 start=True,
@@ -109,26 +110,19 @@ def tile_list_vegetation_change_indices_kernel(
             nc.scalar.activation(h[j][:, BANK * c : BANK * (c + 1)], acc[:], ACT.Sigmoid, bias=zero[:], scale=one[:])
 
         with tc.psum_pool(name="first", bufs=8) as first:
-            for c in range(S // BANK):
-                for j in range(2):
-                    respond(first, j, c)
-            for j in range(2, SLICES):
+            for j in range(SLICES):
                 for c in range(S // BANK):
                     respond(first, j, c)
         psum = ctx.enter_context(tc.psum_pool(name="psum", bufs=1))
 
         w2c = [keep.tile([P, N], U32, name=f"w2c{b}", align_bytes=64) for b in range(PASSES)]
         w2s = [keep.tile([P, N], U8, name=f"w2s{b}", align_bytes=64) for b in range(PASSES)]
-        w2b = [keep.tile([P, N * PACK], BF16, name=f"w2b{b}", align_bytes=64) for b in range(PASSES)]
+        w2b = [keep.tile([P, N * PACK], BF16, name=f"w2b{b}", tag=f"vw{b}", align_bytes=64) for b in range(PASSES)]
 
-        for b in range(PASSES):
-            nc.gpsimd.tensor_scalar(
-                w2b[b][:].rearrange("p (t m j) -> p t m j", t=PACK, j=PACK),
-                w2_raw[:, b, :].rearrange("p (j m t) -> p t m j", j=PACK, t=PACK),
-                1.0,
-                0.0,
-                ALU.mult,
-                ALU.add,
+        def round_w2(b):
+            nc.scalar.copy(
+                w2b[b][:].rearrange("p (t m j) -> p m j t", t=PACK, j=PACK),
+                w2_raw[:, b, :].rearrange("p (j m t) -> p m j t", j=PACK, t=PACK),
             )
 
         early, diff, total = {}, {}, {}
@@ -168,15 +162,23 @@ def tile_list_vegetation_change_indices_kernel(
 
         for j in range(BY_GPSIMD):
             invert(j)
+        for b in range(PASSES):
+            round_w2(b)
         zrow0 = keep.tile([P, PACK, PAIRS], BF16, name="zrow0", tag=f"late{BY_GPSIMD - 1}")
         ratio(zrow0, 0, 0, PAIRS)
         woven0 = keep.tile([P, PAIRS * PACK], BF16, name="woven0", align_bytes=64)
         weave(nc.scalar.copy, woven0, zrow0, PAIRS)
-        for j in range(BY_GPSIMD, SLICES):
-            diff[j] = keep.tile([P, PAIRS], F32, name=f"diff{j}", tag=f"diff{j - PACK}")
-            nc.vector.tensor_tensor(diff[j][:], h[j][:].indirect(pos1_t[:]), early[j][:], ALU.subtract)
-            nc.vector.scalar_tensor_tensor(total[j][:], early[j][:], 2.0, diff[j][:], ALU.mult, ALU.add)
-            invert(j)
+        for j in range(BY_GPSIMD, SLICES + 1):
+            if j < SLICES:
+                diff[j] = keep.tile([P, PAIRS], F32, name=f"diff{j}", tag=f"diff{j - PACK}")
+                nc.vector.tensor_tensor(diff[j][:], h[j][:].indirect(pos1_t[:]), early[j][:], ALU.subtract)
+            else:
+                nc.vector.quantize_mx(out=w2c[0][:].bitcast(FP8X4), scales=w2s[0][:], in_=w2b[0][:])
+            if j > BY_GPSIMD:
+                nc.vector.scalar_tensor_tensor(
+                    total[j - 1][:], early[j - 1][:], 2.0, diff[j - 1][:], ALU.mult, ALU.add
+                )
+                invert(j - 1)
 
         zc = [keep.tile([P, PAIRS], U32, name=f"zc{b}", align_bytes=64) for b in range(PASSES)]
         zs = [keep.tile([P, PAIRS], U8, name=f"zs{b}", align_bytes=64) for b in range(PASSES)]
@@ -217,11 +219,10 @@ def tile_list_vegetation_change_indices_kernel(
             nc.sync.dma_start(out_rows[:, :, c0:c1], yf[:, :, 0 : c1 - c0])
             nc.sync.dma_start(out_words[:, c0:c1], yc[:, c0:c1].bitcast(I32))
 
-        for b in range(PASSES):
-            nc.vector.quantize_mx(out=w2c[b][:].bitcast(FP8X4), scales=w2s[b][:], in_=w2b[b][:])
         for c0, c1 in ((0, 512), (512, 768)):
             quantise_z(woven0[:, PACK * c0 : PACK * c1], 0, c0, c1)
         mix(0, 0, PAIRS)
+        nc.vector.quantize_mx(out=w2c[1][:].bitcast(FP8X4), scales=w2s[1][:], in_=w2b[1][:])
 
         runs = [(0, 128), (128, 384), (384, 640), (640, 768)]
         zrows, wovens = {}, {}

@@ -23,6 +23,7 @@ SLICES = H // P
 BANK = 512
 Y_COLS = 128
 BY_GPSIMD = 5
+ROUNDED_BY_SCALAR = 128
 
 
 def tile_list_vegetation_change_indices_kernel(
@@ -115,7 +116,7 @@ def tile_list_vegetation_change_indices_kernel(
                     respond(first, j, c)
         psum = ctx.enter_context(tc.psum_pool(name="psum", bufs=1))
 
-        w2c = [keep.tile([P, N], U32, name=f"w2c{b}", align_bytes=64) for b in range(PASSES)]
+        w2c = [keep.tile([P, N], U32, name="w2c0", align_bytes=64)]
         w2s = [keep.tile([P, N], U8, name=f"w2s{b}", align_bytes=64) for b in range(PASSES)]
         w2b = [keep.tile([P, N * PACK], BF16, name=f"w2b{b}", tag=f"vw{b}", align_bytes=64) for b in range(PASSES)]
 
@@ -127,50 +128,55 @@ def tile_list_vegetation_change_indices_kernel(
 
         early, diff, total = {}, {}, {}
         for j in range(SLICES):
-            early[j] = keep.tile([P, PAIRS], F32, name=f"early{j}")
-            total[j] = keep.tile([P, PAIRS], F32, name=f"total{j}")
+            early[j] = keep.tile([P, PAIRS], F32, name=f"early{j}", tag=f"early{j}", align_bytes=64)
+            total[j] = keep.tile([P, PAIRS], F32, name=f"total{j}", tag=f"total{j}", align_bytes=64)
             nc.vector.tensor_copy(early[j][:], h[j][:].indirect(pos2_t[:]))
             if j < BY_GPSIMD:
                 late = keep.tile([P, PAIRS], F32, name=f"late{j}", tag=f"late{j}")
-                diff[j] = keep.tile([P, PAIRS], F32, name=f"diff{j}", tag=f"diff{j}")
+                diff[j] = keep.tile([P, PAIRS], F32, name=f"diff{j}", tag=f"diff{j}", align_bytes=64)
                 nc.vector.tensor_copy(late[:], h[j][:].indirect(pos1_t[:]))
                 nc.gpsimd.tensor_tensor(total[j][:], late[:], early[j][:], ALU.add)
                 nc.gpsimd.tensor_tensor(diff[j][:], late[:], early[j][:], ALU.subtract)
 
-        def invert(j):
-            root = ring.tile([P, PAIRS], F32, name="root", tag="root", align_bytes=64)
-            nc.scalar.activation(root[:], total[j][:], ACT.Abs_reciprocal_sqrt)
-            nc.scalar.activation(total[j][:], root[:], ACT.Square)
+        roots = {}
 
-        def ratio(zrow, b, c0, c1):
-            for t in range(PACK):
-                j = PACK * b + t
-                nc.vector.scalar_tensor_tensor(
-                    zrow[:, t, 0 : c1 - c0],
-                    diff[j][:, c0:c1],
-                    g_t[:, b, t : t + 1],
-                    total[j][:, c0:c1],
-                    ALU.mult,
-                    ALU.mult,
-                )
+        def take_root(j):
+            roots[j] = ring.tile([P, PAIRS], F32, name="root", tag="root", align_bytes=64)
+            nc.scalar.activation(roots[j][:], total[j][:], ACT.Abs_reciprocal_sqrt)
 
-        def weave(copy, woven, zrow, w):
-            copy(
-                woven[:, 0 : w * PACK].rearrange("p (c i t) -> p c t i", i=4, t=PACK),
-                zrow[:, :, 0:w].rearrange("p t (c i) -> p c t i", i=4),
+        def square(j):
+            nc.scalar.activation(total[j][:], roots[j][:], ACT.Square)
+
+        def ratio(zrow, j, c0, c1):
+            b, t = divmod(j, PACK)
+            nc.vector.scalar_tensor_tensor(
+                zrow[:, t, c0:c1], diff[j][:, c0:c1], g_t[:, b, t : t + 1], total[j][:, c0:c1], ALU.mult, ALU.mult
             )
 
-        for j in range(BY_GPSIMD):
-            invert(j)
-        for b in range(PASSES):
-            round_w2(b)
+        def weave(copy, woven, zrow, c0, c1):
+            copy(
+                woven[:, PACK * c0 : PACK * c1].rearrange("p (c i t) -> p c t i", i=4, t=PACK),
+                zrow[:, :, c0:c1].rearrange("p t (c i) -> p c t i", i=4),
+            )
+
+        for j in range(0, PACK, 2):
+            take_root(j)
+            take_root(j + 1)
+            square(j)
+            square(j + 1)
+        take_root(PACK)
+        round_w2(0)
+        square(PACK)
+        round_w2(1)
         zrow0 = keep.tile([P, PACK, PAIRS], BF16, name="zrow0", tag=f"late{BY_GPSIMD - 1}")
-        ratio(zrow0, 0, 0, PAIRS)
+        for j in range(PACK):
+            ratio(zrow0, j, 0, PAIRS)
         woven0 = keep.tile([P, PAIRS * PACK], BF16, name="woven0", align_bytes=64)
-        weave(nc.scalar.copy, woven0, zrow0, PAIRS)
+        weave(nc.scalar.copy, woven0, zrow0, 0, PAIRS)
+        after = (f"diff{PACK - 1}", f"total{PACK - 1}", f"early{BY_GPSIMD}")
         for j in range(BY_GPSIMD, SLICES + 1):
             if j < SLICES:
-                diff[j] = keep.tile([P, PAIRS], F32, name=f"diff{j}", tag=f"diff{j - PACK}")
+                diff[j] = keep.tile([P, PAIRS], F32, name=f"diff{j}", tag=after[j - BY_GPSIMD], align_bytes=64)
                 nc.vector.tensor_tensor(diff[j][:], h[j][:].indirect(pos1_t[:]), early[j][:], ALU.subtract)
             else:
                 nc.vector.quantize_mx(out=w2c[0][:].bitcast(FP8X4), scales=w2s[0][:], in_=w2b[0][:])
@@ -178,9 +184,13 @@ def tile_list_vegetation_change_indices_kernel(
                 nc.vector.scalar_tensor_tensor(
                     total[j - 1][:], early[j - 1][:], 2.0, diff[j - 1][:], ALU.mult, ALU.add
                 )
-                invert(j - 1)
+                take_root(j - 1)
+                square(j - 1)
 
-        zc = [keep.tile([P, PAIRS], U32, name=f"zc{b}", align_bytes=64) for b in range(PASSES)]
+        zc = [
+            keep.tile([P, PAIRS], U32, name="zc0", tag=f"early{SLICES - 1}", align_bytes=64),
+            keep.tile([P, PAIRS], U32, name="zc1", align_bytes=64),
+        ]
         zs = [keep.tile([P, PAIRS], U8, name=f"zs{b}", align_bytes=64) for b in range(PASSES)]
 
         def quantise_z(woven, b, c0, c1):
@@ -206,39 +216,46 @@ def tile_list_vegetation_change_indices_kernel(
                         stop=(b == PASSES - 1 and t == PACK - 1),
                     )
 
+        yf = keep.tile([P, PACK, PAIRS], F32, name="yf")
+        yb = keep.tile([P, PAIRS * PACK], BF16, name="yb", align_bytes=64)
+
         def hand_out(c0, c1):
-            yf = ring.tile([P, PACK, 256], F32, name="yf", tag="yf")
             for s0 in range(c0, c1, Y_COLS):
                 cols = slice(s0, s0 + Y_COLS)
                 acc = yacc[s0 // Y_COLS]
-                yb = ring.tile([P, Y_COLS * PACK], BF16, name="yb", tag="yb", align_bytes=64)
-                nc.scalar.copy(yb[:].rearrange("p (n t) -> p n t", t=PACK), acc[:].rearrange("p t n -> p n t"))
-                copy_out = nc.vector.tensor_copy if s0 >= PAIRS - 2 * Y_COLS else nc.scalar.copy
-                copy_out(yf[:, :, s0 - c0 : s0 - c0 + Y_COLS], acc[:])
-                nc.vector.quantize_mx(out=yc[:, cols].bitcast(FP8X4), scales=ys[:, cols], in_=yb[:])
-            nc.sync.dma_start(out_rows[:, :, c0:c1], yf[:, :, 0 : c1 - c0])
+                rounded = yb[:, PACK * s0 : PACK * (s0 + Y_COLS)]
+                nc.scalar.copy(yf[:, :, cols], acc[:])
+                if s0 < ROUNDED_BY_SCALAR:
+                    nc.scalar.copy(rounded.rearrange("p (n t) -> p n t", t=PACK), acc[:].rearrange("p t n -> p n t"))
+            if c0 >= ROUNDED_BY_SCALAR:
+                weave(nc.vector.tensor_copy, yb, yf, c0, c1)
+            nc.vector.quantize_mx(
+                out=yc[:, c0:c1].bitcast(FP8X4), scales=ys[:, c0:c1], in_=yb[:, PACK * c0 : PACK * c1]
+            )
+            nc.sync.dma_start(out_rows[:, :, c0:c1], yf[:, :, c0:c1])
             nc.sync.dma_start(out_words[:, c0:c1], yc[:, c0:c1].bitcast(I32))
 
         for c0, c1 in ((0, 512), (512, 768)):
             quantise_z(woven0[:, PACK * c0 : PACK * c1], 0, c0, c1)
         mix(0, 0, PAIRS)
+        w2c.append(keep.tile([P, N], U32, name="w2c1", tag=f"early{BY_GPSIMD - 1}", align_bytes=64))
         nc.vector.quantize_mx(out=w2c[1][:].bitcast(FP8X4), scales=w2s[1][:], in_=w2b[1][:])
 
+        zrow1 = keep.tile([P, PACK, PAIRS], BF16, name="zrow1", tag=f"early{SLICES - 2}", align_bytes=64)
+        woven1 = keep.tile([P, PAIRS * PACK], BF16, name="woven1", align_bytes=64)
+        for j in range(PACK, SLICES - 1):
+            ratio(zrow1, j, 0, PAIRS)
         runs = [(0, 128), (128, 384), (384, 640), (640, 768)]
-        zrows, wovens = {}, {}
         for n in range(len(runs) + 2):
             if n < len(runs):
-                zrows[n] = ring.tile([P, PACK, 256], BF16, name="zrow", tag="zrow")
-                ratio(zrows[n], 1, *runs[n])
+                ratio(zrow1, SLICES - 1, *runs[n])
             if 0 <= n - 2 < len(runs):
                 c0, c1 = runs[n - 2]
-                quantise_z(wovens[n - 2][:, 0 : PACK * (c1 - c0)], 1, c0, c1)
+                quantise_z(woven1[:, PACK * c0 : PACK * c1], 1, c0, c1)
                 mix(1, c0, c1)
                 hand_out(c0, c1)
             if 0 <= n - 1 < len(runs):
-                c0, c1 = runs[n - 1]
-                wovens[n - 1] = ring.tile([P, 256 * PACK], BF16, name="woven", tag="woven", align_bytes=64)
-                weave(nc.vector.tensor_copy, wovens[n - 1], zrows[n - 1], c1 - c0)
+                weave(nc.vector.tensor_copy, woven1, zrow1, *runs[n - 1])
         for q in range(4):
             (nc.scalar, nc.sync)[q % 2].dma_start(
                 out_2[0, 4 * q : 4 * q + 4, :].bitcast(I32), ys[32 * q : 32 * q + 4, :].bitcast(I32)

@@ -23,7 +23,6 @@ SLICES = H // P
 BANK = 512
 Y_COLS = 128
 BY_GPSIMD = 5
-ROUNDED_BY_SCALAR = 128
 
 
 def tile_list_vegetation_change_indices_kernel(
@@ -42,7 +41,7 @@ def tile_list_vegetation_change_indices_kernel(
         zero = ring.tile([P, 1], F32, name="zero", tag="root", align_bytes=64)
         one = ring.tile([P, 1], F32, name="one", tag="root", align_bytes=64)
         seed_zero = keep.tile([P, 1], F32, name="seed_zero", tag="then_table")
-        seed_one = keep.tile([P, 1], F32, name="seed_one", tag="then_w1")
+        seed_one = keep.tile([P, 1], F32, name="seed_one", tag="then_w1", align_bytes=64)
         nc.vector.memset(tabs[:].bitcast(I32), 0)
         nc.vector.memset(seed_zero[:], 0.0)
         nc.vector.tensor_copy(zero[:], seed_zero[:])
@@ -57,63 +56,75 @@ def tile_list_vegetation_change_indices_kernel(
             )
         tabw = keep.tile([P, T], I32, name="tabw", tag="then_table")
         nc.sync.dma_start(tabw[:], tab_words[0].rearrange("p t i -> p (t i)").bitcast(I32))
-        w1w_raw = keep.tile([P, 2 * H], U8, name="w1w_raw", tag="then_w1")
+        w1w_raw = keep.tile([P, 2 * H], U8, name="w1w_raw", tag="then_w1", align_bytes=64)
         nc.scalar.dma_start(w1w_raw[:].bitcast(I32), w1_words[0].bitcast(I32))
         warm = keep.tile([P, 1], F32, name="warm")
         nc.scalar.activation(warm[:], zero[:], ACT.Sigmoid, bias=zero[:], scale=one[:])
         nc.gpsimd.dma_start(g_t[:], g.rearrange("(b p t) -> p b t", b=PASSES, t=PACK))
 
         w1w = [keep.tile([P, 1024], U8, name=f"w1w{b}", align_bytes=64) for b in range(PASSES)]
-        w1s = keep.tile([P, H], U8, name="w1s", align_bytes=64)
+        w1s = [keep.tile([P, 512], U8, name=f"w1s{b}", align_bytes=64) for b in range(PASSES)]
+
+        def load_scales(b, tag):
+            raw = keep.tile([P, 512], U8, name=f"w1s_raw{b}", tag=tag, align_bytes=64)
+            nc.vector.memset(raw[:].bitcast(I32), 0)
+            for q in range(4):
+                (nc.sync, nc.scalar)[q % 2].dma_start(
+                    raw[32 * q : 32 * q + 4, :].bitcast(I32),
+                    w1_scales[0, 4 * q : 4 * q + 4, 512 * b : 512 * (b + 1)].bitcast(I32),
+                )
+            return raw
+
+        def deal_scales(b, raw):
+            nc.vector.tensor_copy(
+                w1s[b][:].rearrange("p (t m) -> p t m", t=PACK), raw[:].rearrange("p (m t) -> p t m", t=PACK)
+            )
 
         vs = keep.tile([P, S], U8, name="vs", align_bytes=64)
         nc.vector.tensor_copy(vs[:], tabs[:].indirect(offs_t[:]))
-        w1s_raw = keep.tile([P, H], U8, name="w1s_raw", tag="then_w1s", align_bytes=64)
-        nc.vector.memset(w1s_raw[:].bitcast(I32), 0)
-        for q in range(4):
-            (nc.sync, nc.scalar)[q % 2].dma_start(
-                w1s_raw[32 * q : 32 * q + 4, :].bitcast(I32), w1_scales[0, 4 * q : 4 * q + 4, :].bitcast(I32)
-            )
+        raw0 = load_scales(0, "then_w1s")
         for b in range(PASSES):
             nc.vector.tensor_copy(
                 w1w[b][:].bitcast(U16).rearrange("p (t m) -> p t m", t=PACK),
                 w1w_raw[:, H * b : H * (b + 1)].bitcast(U16).rearrange("p (m t) -> p t m", t=PACK),
             )
+        raw1 = load_scales(1, "then_w1")
 
         vw = []
         for c in range(S // BANK):
             last = c == S // BANK - 1
             if last:
-                nc.vector.tensor_copy(
-                    w1s[:].rearrange("p (b t m) -> p b t m", b=PASSES, t=PACK),
-                    w1s_raw[:].rearrange("p (b m t) -> p b t m", b=PASSES, t=PACK),
-                )
+                deal_scales(0, raw0)
             vw.append(keep.tile([P, BANK], U32, name=f"vw{c}", tag="then_w1s" if last else f"vw{c}", align_bytes=64))
             nc.vector.tensor_copy(vw[c][:], tabw[:].bitcast(U32).indirect(offs_t[:, 32 * c : 32 * (c + 1)]))
+        deal_scales(1, raw1)
 
         w2_raw = keep.tile([P, PASSES, PACK * N], F32, name="w2_raw", tag="then_table")
         nc.sync.dma_start(w2_raw[:], w2.rearrange("(b p j) n -> p b (j n)", b=PASSES, j=PACK))
 
         h = [keep.tile([P, S], F32, name=f"h{j}") for j in range(SLICES)]
 
-        def respond(psum, j, c):
+        def respond(psum, j, c, lo, hi):
             b, t = divmod(j, PACK)
-            acc = psum.tile([P, BANK], F32, name="acc")
+            cols = slice(BANK * c + lo, BANK * c + hi)
+            acc = psum.tile([P, hi - lo], F32, name="acc")
             nc.tensor.matmul_mx(
                 out=acc[:],
                 lhsT=w1w[b][:, 256 * t : 256 * (t + 1)].bitcast(FP4X4),
-                lhsT_scale=w1s[:, P * j : P * (j + 1)],
-                rhs=vw[c][:].bitcast(FP8X4),
-                rhs_scale=vs[:, BANK * c : BANK * (c + 1)],
+                lhsT_scale=w1s[b][:, P * t : P * (t + 1)],
+                rhs=vw[c][:, lo:hi].bitcast(FP8X4),
+                rhs_scale=vs[:, cols],
                 start=True,
                 stop=True,
             )
-            nc.scalar.activation(h[j][:, BANK * c : BANK * (c + 1)], acc[:], ACT.Sigmoid, bias=zero[:], scale=one[:])
+            nc.scalar.activation(h[j][:, cols], acc[:], ACT.Sigmoid, bias=zero[:], scale=one[:])
 
         with tc.psum_pool(name="first", bufs=8) as first:
             for j in range(SLICES):
                 for c in range(S // BANK):
-                    respond(first, j, c)
+                    width = BANK // 2 if (j, c) == (0, S // BANK - 1) else BANK
+                    for lo in range(0, BANK, width):
+                        respond(first, j, c, lo, lo + width)
         psum = ctx.enter_context(tc.psum_pool(name="psum", bufs=1))
 
         w2c = [keep.tile([P, N], U32, name="w2c0", align_bytes=64)]
@@ -223,16 +234,18 @@ def tile_list_vegetation_change_indices_kernel(
             for s0 in range(c0, c1, Y_COLS):
                 cols = slice(s0, s0 + Y_COLS)
                 acc = yacc[s0 // Y_COLS]
-                rounded = yb[:, PACK * s0 : PACK * (s0 + Y_COLS)]
+                if c1 == PAIRS:
+                    nc.scalar.copy(
+                        yb[:, PACK * c0 : PACK * c1].rearrange("p (n t) -> p n t", t=PACK),
+                        acc[:].rearrange("p t n -> p n t"),
+                    )
                 nc.scalar.copy(yf[:, :, cols], acc[:])
-                if s0 < ROUNDED_BY_SCALAR:
-                    nc.scalar.copy(rounded.rearrange("p (n t) -> p n t", t=PACK), acc[:].rearrange("p t n -> p n t"))
-            if c0 >= ROUNDED_BY_SCALAR:
+            if c1 < PAIRS:
                 weave(nc.vector.tensor_copy, yb, yf, c0, c1)
             nc.vector.quantize_mx(
                 out=yc[:, c0:c1].bitcast(FP8X4), scales=ys[:, c0:c1], in_=yb[:, PACK * c0 : PACK * c1]
             )
-            nc.sync.dma_start(out_rows[:, :, c0:c1], yf[:, :, c0:c1])
+            (nc.scalar if c1 == PAIRS else nc.sync).dma_start(out_rows[:, :, c0:c1], yf[:, :, c0:c1])
             nc.sync.dma_start(out_words[:, c0:c1], yc[:, c0:c1].bitcast(I32))
 
         for c0, c1 in ((0, 512), (512, 768)):

@@ -58,8 +58,6 @@ def tile_list_vegetation_change_indices_kernel(
         nc.sync.dma_start(tabw[:], tab_words[0].rearrange("p t i -> p (t i)").bitcast(I32))
         w1w_raw = keep.tile([P, 2 * H], U8, name="w1w_raw", tag="then_w1", align_bytes=64)
         nc.scalar.dma_start(w1w_raw[:].bitcast(I32), w1_words[0].bitcast(I32))
-        warm = keep.tile([P, 1], F32, name="warm")
-        nc.scalar.activation(warm[:], zero[:], ACT.Sigmoid, bias=zero[:], scale=one[:])
         nc.gpsimd.dma_start(g_t[:], g.rearrange("(b p t) -> p b t", b=PASSES, t=PACK))
 
         w1w = [keep.tile([P, 1024], U8, name=f"w1w{b}", align_bytes=64) for b in range(PASSES)]

@@ -22,7 +22,7 @@ PASSES = H // (P * PACK)
 SLICES = H // P
 BANK = 512
 Y_COLS = 128
-BY_GPSIMD = 5
+BY_GPSIMD = 6
 
 
 def tile_list_vegetation_change_indices_kernel(
@@ -36,71 +36,73 @@ def tile_list_vegetation_change_indices_kernel(
         offs_t = keep.tile([P, S // 16], U16, name="offs_t")
         pos1_t = keep.tile([P, PAIRS // 16], U16, name="pos1_t")
         pos2_t = keep.tile([P, PAIRS // 16], U16, name="pos2_t")
-        tabs = keep.tile([P, T], U8, name="tabs", tag="then_w1s", align_bytes=64)
+        tabs = keep.tile([P, T], U8, name="tabs", tag="then_w2", align_bytes=64)
         g_t = keep.tile([P, PASSES, PACK], F32, name="g_t")
         zero = ring.tile([P, 1], F32, name="zero", tag="root", align_bytes=64)
         one = ring.tile([P, 1], F32, name="one", tag="root", align_bytes=64)
         seed_zero = keep.tile([P, 1], F32, name="seed_zero", tag="then_table")
-        seed_one = keep.tile([P, 1], F32, name="seed_one", tag="then_w1", align_bytes=64)
-        nc.vector.memset(tabs[:].bitcast(I32), 0)
+        w1s_raw = keep.tile([P, H], U8, name="w1s_raw", align_bytes=64)
+        w1s = keep.tile([P, H], U8, name="w1s", align_bytes=64)
+        vs = keep.tile([P, S], U8, name="vs", align_bytes=64)
+        nc.vector.memset(w1s_raw[:].bitcast(I32), 0)
         nc.vector.memset(seed_zero[:], 0.0)
+        nc.vector.memset(tabs[:].bitcast(I32), 0)
         nc.vector.tensor_copy(zero[:], seed_zero[:])
-        nc.vector.memset(seed_one[:], 1.0)
-        nc.vector.tensor_copy(one[:], seed_one[:])
+        nc.vector.memset(one[:], 1.0)
+        nc.vector.memset(w1s[:].bitcast(I32), 0)
+        nc.vector.memset(vs[:].bitcast(I32), 0)
         nc.sync.dma_start(offs_t[:], offs)
-        nc.sync.dma_start(pos2_t[:], pos2)
-        nc.sync.dma_start(pos1_t[:], pos1)
-        for q in range(4):
-            (nc.sync, nc.scalar)[q % 2].dma_start(
-                tabs[32 * q : 32 * q + 4, :].bitcast(I32), tab_scales[0, 4 * q : 4 * q + 4, :].bitcast(I32)
-            )
+        w1w_raw = keep.tile([P, 2 * H], U8, name="w1w_raw", align_bytes=64)
+        nc.scalar.dma_start(w1w_raw[:].bitcast(I32), w1_words[0].bitcast(I32))
+        nc.scalar.dma_start(w1s_raw[0:P:8, :].bitcast(I32), w1_scales[0].bitcast(I32))
+        nc.sync.dma_start(tabs[0:P:8, :].bitcast(I32), tab_scales[0].bitcast(I32))
         tabw = keep.tile([P, T], I32, name="tabw", tag="then_table")
         nc.sync.dma_start(tabw[:], tab_words[0].rearrange("p t i -> p (t i)").bitcast(I32))
-        w1w_raw = keep.tile([P, 2 * H], U8, name="w1w_raw", tag="then_w1", align_bytes=64)
-        nc.scalar.dma_start(w1w_raw[:].bitcast(I32), w1_words[0].bitcast(I32))
-        nc.gpsimd.dma_start(g_t[:], g.rearrange("(b p t) -> p b t", b=PASSES, t=PACK))
+        w2_rows = w2.rearrange("(b p j) n -> b p (j n)", b=PASSES, j=PACK)
+        nc.sync.dma_start(pos2_t[:], pos2)
+        nc.sync.dma_start(pos1_t[:], pos1)
+        nc.scalar.dma_start(g_t[:], g.rearrange("(b p t) -> p b t", b=PASSES, t=PACK))
 
         w1w = [keep.tile([P, 1024], U8, name=f"w1w{b}", align_bytes=64) for b in range(PASSES)]
-        w1s = [keep.tile([P, 512], U8, name=f"w1s{b}", align_bytes=64) for b in range(PASSES)]
-
-        def load_scales(b, tag):
-            raw = keep.tile([P, 512], U8, name=f"w1s_raw{b}", tag=tag, align_bytes=64)
-            nc.vector.memset(raw[:].bitcast(I32), 0)
-            for q in range(4):
-                (nc.sync, nc.scalar)[q % 2].dma_start(
-                    raw[32 * q : 32 * q + 4, :].bitcast(I32),
-                    w1_scales[0, 4 * q : 4 * q + 4, 512 * b : 512 * (b + 1)].bitcast(I32),
-                )
-            return raw
-
-        def deal_scales(b, raw):
-            nc.vector.tensor_copy(
-                w1s[b][:].rearrange("p (t m) -> p t m", t=PACK), raw[:].rearrange("p (m t) -> p t m", t=PACK)
-            )
-
-        vs = keep.tile([P, S], U8, name="vs", align_bytes=64)
-        nc.vector.tensor_copy(vs[:], tabs[:].indirect(offs_t[:]))
-        raw0 = load_scales(0, "then_w1s")
         for b in range(PASSES):
             nc.vector.tensor_copy(
                 w1w[b][:].bitcast(U16).rearrange("p (t m) -> p t m", t=PACK),
                 w1w_raw[:, H * b : H * (b + 1)].bitcast(U16).rearrange("p (m t) -> p t m", t=PACK),
             )
-        raw1 = load_scales(1, "then_w1")
+        w1s_dealt = keep.tile([P, H], U8, name="w1s_dealt", align_bytes=64)
+        nc.vector.tensor_copy(
+            w1s_dealt[:].rearrange("p (b t m) -> p b t m", b=PASSES, t=PACK),
+            w1s_raw[:].rearrange("p (b m t) -> p b t m", b=PASSES, t=PACK),
+        )
+        for q in range(4):
+            nc.scalar.dma_start(
+                w1s[32 * q : 32 * q + 4, :].bitcast(I32), w1s_dealt[32 * q : 32 * (q + 1) : 8, :].bitcast(I32)
+            )
 
+        g_inv = keep.tile([P, PASSES, PACK], F32, name="g_inv")
+        g_pos = keep.tile([P, PASSES, PACK], F32, name="g_pos")
+        g_sign = keep.tile([P, PASSES, PACK], F32, name="g_sign")
+        nc.vector.tensor_scalar(g_pos[:], g_t[:], 0.0, 2.0, ALU.is_ge, ALU.mult)
+        nc.vector.reciprocal(g_inv[:], g_t[:])
+        nc.vector.tensor_scalar(g_sign[:], g_pos[:], -1.0, None, ALU.add)
+
+        vs_spread = keep.tile([P, S], U8, name="vs_spread", align_bytes=64)
+        nc.vector.tensor_copy(vs_spread[:], tabs[:].indirect(offs_t[:]))
+        for q in range(4):
+            nc.sync.dma_start(
+                vs[32 * q : 32 * q + 4, :].bitcast(I32), vs_spread[32 * q : 32 * (q + 1) : 8, :].bitcast(I32)
+            )
+        w2_raw = [keep.tile([P, PACK * N], F32, name="w2_raw0", tag="then_w2", align_bytes=64)]
+        nc.sync.dma_start(w2_raw[0][:], w2_rows[0])
         vw = []
         for c in range(S // BANK):
-            last = c == S // BANK - 1
-            if last:
-                deal_scales(0, raw0)
-            vw.append(keep.tile([P, BANK], U32, name=f"vw{c}", tag="then_w1s" if last else f"vw{c}", align_bytes=64))
+            vw.append(keep.tile([P, BANK], U32, name=f"vw{c}", tag=f"vw{c}", align_bytes=64))
             nc.vector.tensor_copy(vw[c][:], tabw[:].bitcast(U32).indirect(offs_t[:, 32 * c : 32 * (c + 1)]))
-        deal_scales(1, raw1)
 
-        w2_raw = keep.tile([P, PASSES, PACK * N], F32, name="w2_raw", tag="then_table")
-        nc.sync.dma_start(w2_raw[:], w2.rearrange("(b p j) n -> p b (j n)", b=PASSES, j=PACK))
+        w2_raw.append(keep.tile([P, PACK * N], F32, name="w2_raw1", tag="then_table"))
+        nc.sync.dma_start(w2_raw[1][:], w2_rows[1])
 
-        h = [keep.tile([P, S], F32, name=f"h{j}") for j in range(SLICES)]
+        h = [keep.tile([P, S], F32, name=f"h{j}", tag=f"h{j}", align_bytes=64) for j in range(SLICES)]
 
         def respond(psum, j, c, lo, hi):
             b, t = divmod(j, PACK)
@@ -109,7 +111,7 @@ def tile_list_vegetation_change_indices_kernel(
             nc.tensor.matmul_mx(
                 out=acc[:],
                 lhsT=w1w[b][:, 256 * t : 256 * (t + 1)].bitcast(FP4X4),
-                lhsT_scale=w1s[b][:, P * t : P * (t + 1)],
+                lhsT_scale=w1s[:, P * j : P * (j + 1)],
                 rhs=vw[c][:, lo:hi].bitcast(FP8X4),
                 rhs_scale=vs[:, cols],
                 start=True,
@@ -125,41 +127,81 @@ def tile_list_vegetation_change_indices_kernel(
                         respond(first, j, c, lo, lo + width)
         psum = ctx.enter_context(tc.psum_pool(name="psum", bufs=1))
 
-        w2c = [keep.tile([P, N], U32, name="w2c0", align_bytes=64)]
-        w2s = [keep.tile([P, N], U8, name=f"w2s{b}", align_bytes=64) for b in range(PASSES)]
-        w2b = [keep.tile([P, N * PACK], BF16, name=f"w2b{b}", tag=f"vw{b}", align_bytes=64) for b in range(PASSES)]
+        w2p = [
+            keep.tile([P, PACK, N], BF16, name="w2p0", tag="vw2", align_bytes=64),
+            keep.tile([P, PACK, N], BF16, name="w2p1", tag="vw0", align_bytes=64),
+        ]
 
         def round_w2(b):
+            for j in range(PACK):
+                nc.scalar.activation(
+                    w2p[b][:, j, :], w2_raw[b][:, N * j : N * (j + 1)], ACT.Copy, scale=g_sign[:, b, j : j + 1]
+                )
+
+        def weave_w2(w2b, b):
             nc.scalar.copy(
-                w2b[b][:].rearrange("p (t m j) -> p m j t", t=PACK, j=PACK),
-                w2_raw[:, b, :].rearrange("p (j m t) -> p m j t", j=PACK, t=PACK),
+                w2b[:].rearrange("p (t m j) -> p m j t", t=PACK, j=PACK),
+                w2p[b][:].rearrange("p j (m t) -> p m j t", t=PACK),
             )
 
-        early, diff, total = {}, {}, {}
+        diff = [keep.tile([P, PACK, PAIRS], F32, name=f"diff{b}", align_bytes=64) for b in range(PASSES)]
+        total = [keep.tile([P, PACK, PAIRS], F32, name=f"total{b}", align_bytes=64) for b in range(PASSES)]
+
+        def row(tiles, j):
+            return tiles[j // PACK][:, j % PACK, :]
+
+        early = {}
         for j in range(SLICES):
-            early[j] = keep.tile([P, PAIRS], F32, name=f"early{j}", tag=f"early{j}", align_bytes=64)
-            total[j] = keep.tile([P, PAIRS], F32, name=f"total{j}", tag=f"total{j}", align_bytes=64)
-            nc.vector.tensor_copy(early[j][:], h[j][:].indirect(pos2_t[:]))
-            if j < BY_GPSIMD:
-                late = keep.tile([P, PAIRS], F32, name=f"late{j}", tag=f"late{j}")
-                diff[j] = keep.tile([P, PAIRS], F32, name=f"diff{j}", tag=f"diff{j}", align_bytes=64)
-                nc.vector.tensor_copy(late[:], h[j][:].indirect(pos1_t[:]))
-                nc.gpsimd.tensor_tensor(total[j][:], late[:], early[j][:], ALU.add)
-                nc.gpsimd.tensor_tensor(diff[j][:], late[:], early[j][:], ALU.subtract)
+            if j == SLICES - 1:
+                early[j] = row(diff, SLICES - 2)
+            else:
+                early[j] = keep.tile([P, PAIRS], F32, name=f"early{j}", tag=f"early{j}", align_bytes=64)[:]
+            if j == BY_GPSIMD - 1:
+                late = row(diff, SLICES - 1)
+            elif j < BY_GPSIMD:
+                late = keep.tile([P, PAIRS], F32, name=f"late{j}")[:]
+            width = PAIRS // 2 if j == 0 else PAIRS
+            for c0 in range(0, PAIRS, width):
+                cols = slice(c0, c0 + width)
+                entries = slice(c0 // 16, (c0 + width) // 16)
+                nc.vector.tensor_copy(early[j][:, cols], h[j][:].indirect(pos2_t[:, entries]))
+                if j < BY_GPSIMD:
+                    nc.vector.tensor_copy(late[:, cols], h[j][:].indirect(pos1_t[:, entries]))
+                    nc.gpsimd.tensor_tensor(row(total, j)[:, cols], late[:, cols], early[j][:, cols], ALU.add)
+                    nc.gpsimd.tensor_tensor(row(diff, j)[:, cols], late[:, cols], early[j][:, cols], ALU.subtract)
+        for j in range(SLICES - 1, BY_GPSIMD - 1, -1):
+            nc.vector.tensor_tensor(row(diff, j), h[j][:].indirect(pos1_t[:]), early[j], ALU.subtract)
+            nc.vector.scalar_tensor_tensor(row(total, j), early[j], 2.0, row(diff, j), ALU.mult, ALU.add)
 
         roots = {}
 
         def take_root(j):
+            b, t = divmod(j, PACK)
             roots[j] = ring.tile([P, PAIRS], F32, name="root", tag="root", align_bytes=64)
-            nc.scalar.activation(roots[j][:], total[j][:], ACT.Abs_reciprocal_sqrt)
+            nc.scalar.activation(roots[j][:], row(total, j), ACT.Abs_reciprocal_sqrt, scale=g_inv[:, b, t : t + 1])
 
         def square(j):
-            nc.scalar.activation(total[j][:], roots[j][:], ACT.Square)
+            nc.scalar.activation(row(total, j), roots[j][:], ACT.Square)
 
-        def ratio(zrow, j, c0, c1):
-            b, t = divmod(j, PACK)
-            nc.vector.scalar_tensor_tensor(
-                zrow[:, t, c0:c1], diff[j][:, c0:c1], g_t[:, b, t : t + 1], total[j][:, c0:c1], ALU.mult, ALU.mult
+        w2b0 = keep.tile([P, N * PACK], BF16, name="w2b0", tag="vw1", align_bytes=64)
+        for j in (0, 1, 2, 3, 4, 5, 7, 6):
+            take_root(j)
+            square(j)
+            if j == 1:
+                round_w2(0)
+            if j == 2:
+                weave_w2(w2b0, 0)
+            if j == 3:
+                round_w2(1)
+        w2b1 = ring.tile([P, N * PACK], BF16, name="w2b1", tag="root", align_bytes=64)
+        weave_w2(w2b1, 1)
+
+        def ratio(woven, b, c0, c1):
+            nc.vector.tensor_tensor(
+                woven[:, PACK * c0 : PACK * c1].rearrange("p (c i t) -> p c t i", i=4, t=PACK),
+                diff[b][:, :, c0:c1].rearrange("p t (c i) -> p c t i", i=4),
+                total[b][:, :, c0:c1].rearrange("p t (c i) -> p c t i", i=4),
+                ALU.mult,
             )
 
         def weave(copy, woven, zrow, c0, c1):
@@ -168,38 +210,15 @@ def tile_list_vegetation_change_indices_kernel(
                 zrow[:, :, c0:c1].rearrange("p t (c i) -> p c t i", i=4),
             )
 
-        for j in range(0, PACK, 2):
-            take_root(j)
-            take_root(j + 1)
-            square(j)
-            square(j + 1)
-        take_root(PACK)
-        round_w2(0)
-        square(PACK)
-        round_w2(1)
-        zrow0 = keep.tile([P, PACK, PAIRS], BF16, name="zrow0", tag=f"late{BY_GPSIMD - 1}")
-        for j in range(PACK):
-            ratio(zrow0, j, 0, PAIRS)
-        woven0 = keep.tile([P, PAIRS * PACK], BF16, name="woven0", align_bytes=64)
-        weave(nc.scalar.copy, woven0, zrow0, 0, PAIRS)
-        after = (f"diff{PACK - 1}", f"total{PACK - 1}", f"early{BY_GPSIMD}")
-        for j in range(BY_GPSIMD, SLICES + 1):
-            if j < SLICES:
-                diff[j] = keep.tile([P, PAIRS], F32, name=f"diff{j}", tag=after[j - BY_GPSIMD], align_bytes=64)
-                nc.vector.tensor_tensor(diff[j][:], h[j][:].indirect(pos1_t[:]), early[j][:], ALU.subtract)
-            else:
-                nc.vector.quantize_mx(out=w2c[0][:].bitcast(FP8X4), scales=w2s[0][:], in_=w2b[0][:])
-            if j > BY_GPSIMD:
-                nc.vector.scalar_tensor_tensor(
-                    total[j - 1][:], early[j - 1][:], 2.0, diff[j - 1][:], ALU.mult, ALU.add
-                )
-                take_root(j - 1)
-                square(j - 1)
-
-        zc = [
-            keep.tile([P, PAIRS], U32, name="zc0", tag=f"early{SLICES - 1}", align_bytes=64),
-            keep.tile([P, PAIRS], U32, name="zc1", align_bytes=64),
+        woven0 = keep.tile([P, PAIRS * PACK], BF16, name="woven0", tag=f"early{SLICES - 2}", align_bytes=64)
+        ratio(woven0, 0, 0, PAIRS)
+        w2c = [
+            keep.tile([P, N], U32, name="w2c0", tag=f"h{SLICES - 1}", align_bytes=64),
+            keep.tile([P, N], U32, name="w2c1", align_bytes=64),
         ]
+        w2s = [keep.tile([P, N], U8, name=f"w2s{b}", align_bytes=64) for b in range(PASSES)]
+        nc.vector.quantize_mx(out=w2c[0][:].bitcast(FP8X4), scales=w2s[0][:], in_=w2b0[:])
+        zc = [keep.tile([P, PAIRS], U32, name=f"zc{b}", align_bytes=64) for b in range(PASSES)]
         zs = [keep.tile([P, PAIRS], U8, name=f"zs{b}", align_bytes=64) for b in range(PASSES)]
 
         def quantise_z(woven, b, c0, c1):
@@ -249,24 +268,18 @@ def tile_list_vegetation_change_indices_kernel(
         for c0, c1 in ((0, 512), (512, 768)):
             quantise_z(woven0[:, PACK * c0 : PACK * c1], 0, c0, c1)
         mix(0, 0, PAIRS)
-        w2c.append(keep.tile([P, N], U32, name="w2c1", tag=f"early{BY_GPSIMD - 1}", align_bytes=64))
-        nc.vector.quantize_mx(out=w2c[1][:].bitcast(FP8X4), scales=w2s[1][:], in_=w2b[1][:])
-
-        zrow1 = keep.tile([P, PACK, PAIRS], BF16, name="zrow1", tag=f"early{SLICES - 2}", align_bytes=64)
         woven1 = keep.tile([P, PAIRS * PACK], BF16, name="woven1", align_bytes=64)
-        for j in range(PACK, SLICES - 1):
-            ratio(zrow1, j, 0, PAIRS)
         runs = [(0, 128), (128, 384), (384, 640), (640, 768)]
-        for n in range(len(runs) + 2):
+        for n in range(len(runs) + 1):
             if n < len(runs):
-                ratio(zrow1, SLICES - 1, *runs[n])
-            if 0 <= n - 2 < len(runs):
-                c0, c1 = runs[n - 2]
+                ratio(woven1, 1, *runs[n])
+            if n == 0:
+                nc.vector.quantize_mx(out=w2c[1][:].bitcast(FP8X4), scales=w2s[1][:], in_=w2b1[:])
+            if n > 0:
+                c0, c1 = runs[n - 1]
                 quantise_z(woven1[:, PACK * c0 : PACK * c1], 1, c0, c1)
                 mix(1, c0, c1)
                 hand_out(c0, c1)
-            if 0 <= n - 1 < len(runs):
-                weave(nc.vector.tensor_copy, woven1, zrow1, *runs[n - 1])
         for q in range(4):
             (nc.scalar, nc.sync)[q % 2].dma_start(
                 out_2[0, 4 * q : 4 * q + 4, :].bitcast(I32), ys[32 * q : 32 * q + 4, :].bitcast(I32)

@@ -1,6 +1,7 @@
 from contextlib import ExitStack
 
 import concourse.mybir as mybir
+from concourse.masks import make_identity
 
 K, T, S, PAIRS, H, N = 512, 4096, 1536, 768, 1024, 512
 FLOPS = 2 * K * H * S + 2 * H * N * PAIRS
@@ -23,6 +24,7 @@ SLICES = H // P
 BANK = 512
 Y_COLS = 128
 BY_GPSIMD = 6
+TURNED = 4
 
 
 def tile_list_vegetation_change_indices_kernel(
@@ -36,15 +38,15 @@ def tile_list_vegetation_change_indices_kernel(
         offs_t = keep.tile([P, S // 16], U16, name="offs_t")
         pos1_t = keep.tile([P, PAIRS // 16], U16, name="pos1_t")
         pos2_t = keep.tile([P, PAIRS // 16], U16, name="pos2_t")
-        tabs = keep.tile([P, T], U8, name="tabs", tag="then_w2", align_bytes=64)
+        tabs = keep.tile([P, T], U8, name="tabs", align_bytes=64)
         g_t = keep.tile([P, PASSES, PACK], F32, name="g_t")
         zero = ring.tile([P, 1], F32, name="zero", tag="root", align_bytes=64)
         one = ring.tile([P, 1], F32, name="one", tag="root", align_bytes=64)
         seed_zero = keep.tile([P, 1], F32, name="seed_zero", tag="then_table")
-        w1s_raw = keep.tile([P, H], U8, name="w1s_raw", align_bytes=64)
+        w1s_raw = keep.tile([P, H], U8, name="w1s_raw", tag="then_w2", align_bytes=64)
         w1s = keep.tile([P, H], U8, name="w1s", align_bytes=64)
         vs = keep.tile([P, S], U8, name="vs", align_bytes=64)
-        nc.vector.memset(w1s_raw[:].bitcast(I32), 0)
+        nc.gpsimd.memset(w1s_raw[:].bitcast(I32), 0)
         nc.vector.memset(seed_zero[:], 0.0)
         nc.vector.memset(tabs[:].bitcast(I32), 0)
         nc.vector.tensor_copy(zero[:], seed_zero[:])
@@ -75,9 +77,11 @@ def tile_list_vegetation_change_indices_kernel(
             w1s_raw[:].rearrange("p (b m t) -> p b t m", b=PASSES, t=PACK),
         )
         for q in range(4):
-            nc.scalar.dma_start(
+            nc.sync.dma_start(
                 w1s[32 * q : 32 * q + 4, :].bitcast(I32), w1s_dealt[32 * q : 32 * (q + 1) : 8, :].bitcast(I32)
             )
+        w2_raw = [keep.tile([P, PACK * N], F32, name="w2_raw0", tag="then_w2", align_bytes=64)]
+        nc.sync.dma_start(w2_raw[0][:], w2_rows[0])
 
         g_inv = keep.tile([P, PASSES, PACK], F32, name="g_inv")
         g_pos = keep.tile([P, PASSES, PACK], F32, name="g_pos")
@@ -86,14 +90,22 @@ def tile_list_vegetation_change_indices_kernel(
         nc.vector.reciprocal(g_inv[:], g_t[:])
         nc.vector.tensor_scalar(g_sign[:], g_pos[:], -1.0, None, ALU.add)
 
+        late_g = slice(0, PACK)
+        g_abs = keep.tile([P, PACK], F32, name="g_abs")
+        g_root = keep.tile([P, PACK], F32, name="g_root")
+        half = keep.tile([P, PACK], F32, name="half")
+        ident = keep.tile([P, P], F32, name="ident")
+        make_identity(nc, ident[:])
+        nc.gpsimd.memset(half[:, late_g], 0.5)
+        nc.gpsimd.tensor_tensor(g_abs[:, late_g], g_t[:, 1, late_g], g_sign[:, 1, late_g], ALU.mult)
+        nc.gpsimd.tensor_tensor(g_root[:, late_g], g_abs[:, late_g], half[:, late_g], ALU.pow)
+
         vs_spread = keep.tile([P, S], U8, name="vs_spread", align_bytes=64)
         nc.vector.tensor_copy(vs_spread[:], tabs[:].indirect(offs_t[:]))
         for q in range(4):
-            nc.sync.dma_start(
+            nc.scalar.dma_start(
                 vs[32 * q : 32 * q + 4, :].bitcast(I32), vs_spread[32 * q : 32 * (q + 1) : 8, :].bitcast(I32)
             )
-        w2_raw = [keep.tile([P, PACK * N], F32, name="w2_raw0", tag="then_w2", align_bytes=64)]
-        nc.sync.dma_start(w2_raw[0][:], w2_rows[0])
         vw = []
         for c in range(S // BANK):
             vw.append(keep.tile([P, BANK], U32, name=f"vw{c}", tag=f"vw{c}", align_bytes=64))
@@ -128,9 +140,13 @@ def tile_list_vegetation_change_indices_kernel(
         psum = ctx.enter_context(tc.psum_pool(name="psum", bufs=1))
 
         w2p = [
-            keep.tile([P, PACK, N], BF16, name="w2p0", tag="vw2", align_bytes=64),
+            keep.tile([P, PACK, N], BF16, name="w2p0", align_bytes=64),
             keep.tile([P, PACK, N], BF16, name="w2p1", tag="vw0", align_bytes=64),
         ]
+        for j in range(PACK):
+            nc.gpsimd.tensor_scalar(
+                w2p[0][:, j, :], w2_raw[0][:, N * j : N * (j + 1)], g_sign[:, 0, j : j + 1], 0.0, ALU.mult, ALU.add
+            )
 
         def round_w2(b):
             for j in range(PACK):
@@ -150,6 +166,21 @@ def tile_list_vegetation_change_indices_kernel(
         def row(tiles, j):
             return tiles[j // PACK][:, j % PACK, :]
 
+        spans = ((0, BANK), (BANK, PAIRS))
+        turned = {}
+
+        def add_turned(j, src, start, stop):
+            for k, (c0, c1) in enumerate(spans):
+                for c in range(c0, c1, P):
+                    nc.tensor.matmul(
+                        turned[j][k][:, c - c0 : c - c0 + P],
+                        src[:, c : c + P],
+                        ident[:],
+                        start=(start and c == c0),
+                        stop=(stop and c == c1 - P),
+                        is_transpose=True,
+                    )
+
         early = {}
         for j in range(SLICES):
             if j == SLICES - 1:
@@ -159,7 +190,7 @@ def tile_list_vegetation_change_indices_kernel(
             if j == BY_GPSIMD - 1:
                 late = row(diff, SLICES - 1)
             elif j < BY_GPSIMD:
-                late = keep.tile([P, PAIRS], F32, name=f"late{j}")[:]
+                late = keep.tile([P, PAIRS], F32, name=f"late{j}", tag=f"late{j}", align_bytes=64)[:]
             width = PAIRS // 2 if j == 0 else PAIRS
             for c0 in range(0, PAIRS, width):
                 cols = slice(c0, c0 + width)
@@ -167,11 +198,16 @@ def tile_list_vegetation_change_indices_kernel(
                 nc.vector.tensor_copy(early[j][:, cols], h[j][:].indirect(pos2_t[:, entries]))
                 if j < BY_GPSIMD:
                     nc.vector.tensor_copy(late[:, cols], h[j][:].indirect(pos1_t[:, entries]))
-                    nc.gpsimd.tensor_tensor(row(total, j)[:, cols], late[:, cols], early[j][:, cols], ALU.add)
+                    if j != TURNED:
+                        nc.gpsimd.tensor_tensor(row(total, j)[:, cols], late[:, cols], early[j][:, cols], ALU.add)
                     nc.gpsimd.tensor_tensor(row(diff, j)[:, cols], late[:, cols], early[j][:, cols], ALU.subtract)
-        for j in range(SLICES - 1, BY_GPSIMD - 1, -1):
-            nc.vector.tensor_tensor(row(diff, j), h[j][:].indirect(pos1_t[:]), early[j], ALU.subtract)
-            nc.vector.scalar_tensor_tensor(row(total, j), early[j], 2.0, row(diff, j), ALU.mult, ALU.add)
+            if j == TURNED:
+                turned[j] = [
+                    psum.tile([P, c1 - c0], F32, name=f"turned{j}_{k}", tag=f"bank{4 + k}")
+                    for k, (c0, c1) in enumerate(spans)
+                ]
+                add_turned(j, early[j], True, False)
+                add_turned(j, late, False, True)
 
         roots = {}
 
@@ -184,16 +220,51 @@ def tile_list_vegetation_change_indices_kernel(
             nc.scalar.activation(row(total, j), roots[j][:], ACT.Square)
 
         w2b0 = keep.tile([P, N * PACK], BF16, name="w2b0", tag="vw1", align_bytes=64)
-        for j in (0, 1, 2, 3, 4, 5, 7, 6):
+        back = {}
+
+        def turned_root(j, pool, tag, bank):
+            roots[j] = pool.tile([P, PAIRS], F32, name=f"root{j}", tag=tag, align_bytes=64)
+            back[j] = [
+                psum.tile([P, c1 - c0], F32, name=f"back{j}_{k}", tag=f"bank{bank + k}")
+                for k, (c0, c1) in enumerate(spans)
+            ]
+            for k, (c0, c1) in enumerate(spans):
+                nc.scalar.activation(roots[j][:, c0:c1], turned[j][k][:], ACT.Abs_reciprocal_sqrt)
+                for c in range(c0, c1, P):
+                    nc.tensor.transpose(back[j][k][:, c - c0 : c - c0 + P], roots[j][:, c : c + P], ident[:])
+
+        def turned_square(j):
+            for k, (c0, c1) in enumerate(spans):
+                nc.scalar.activation(
+                    row(total, j)[:, c0:c1], back[j][k][:], ACT.Square, scale=g_root[:, j - PACK : j - PACK + 1]
+                )
+
+        for j in range(TURNED):
             take_root(j)
             square(j)
-            if j == 1:
-                round_w2(0)
             if j == 2:
                 weave_w2(w2b0, 0)
-            if j == 3:
-                round_w2(1)
-        w2b1 = ring.tile([P, N * PACK], BF16, name="w2b1", tag="root", align_bytes=64)
+        turned_root(TURNED, ring, "root", 6)
+        round_w2(1)
+        turned_square(TURNED)
+        for j in range(BY_GPSIMD, SLICES):
+            turned[j] = [
+                psum.tile([P, c1 - c0], F32, name=f"turned{j}_{k}", tag=f"bank{4 + 2 * (j - BY_GPSIMD) + k}")
+                for k, (c0, c1) in enumerate(spans)
+            ]
+            add_turned(j, early[j], True, False)
+            add_turned(j, early[j], False, False)
+        for j in range(SLICES - 1, BY_GPSIMD - 1, -1):
+            nc.vector.tensor_tensor(row(diff, j), h[j][:].indirect(pos1_t[:]), early[j], ALU.subtract)
+            add_turned(j, row(diff, j), False, True)
+
+        take_root(BY_GPSIMD - 1)
+        square(BY_GPSIMD - 1)
+        for j in range(SLICES - 1, BY_GPSIMD - 1, -1):
+            turned_root(j, keep, f"root{j}", 2 * (SLICES - 1 - j))
+        for j in range(SLICES - 1, BY_GPSIMD - 1, -1):
+            turned_square(j)
+        w2b1 = keep.tile([P, N * PACK], BF16, name="w2b1", tag=f"root{SLICES - 1}", align_bytes=64)
         weave_w2(w2b1, 1)
 
         def ratio(woven, b, c0, c1):
@@ -210,14 +281,13 @@ def tile_list_vegetation_change_indices_kernel(
                 zrow[:, :, c0:c1].rearrange("p t (c i) -> p c t i", i=4),
             )
 
-        woven0 = keep.tile([P, PAIRS * PACK], BF16, name="woven0", tag=f"early{SLICES - 2}", align_bytes=64)
+        woven0 = keep.tile([P, PAIRS * PACK], BF16, name="woven0", tag=f"h{SLICES - 2}", align_bytes=64)
         ratio(woven0, 0, 0, PAIRS)
         w2c = [
-            keep.tile([P, N], U32, name="w2c0", tag=f"h{SLICES - 1}", align_bytes=64),
+            keep.tile([P, N], U32, name="w2c0", tag=f"root{SLICES - 2}", align_bytes=64),
             keep.tile([P, N], U32, name="w2c1", align_bytes=64),
         ]
         w2s = [keep.tile([P, N], U8, name=f"w2s{b}", align_bytes=64) for b in range(PASSES)]
-        nc.vector.quantize_mx(out=w2c[0][:].bitcast(FP8X4), scales=w2s[0][:], in_=w2b0[:])
         zc = [keep.tile([P, PAIRS], U32, name=f"zc{b}", align_bytes=64) for b in range(PASSES)]
         zs = [keep.tile([P, PAIRS], U8, name=f"zs{b}", align_bytes=64) for b in range(PASSES)]
 
@@ -228,7 +298,7 @@ def tile_list_vegetation_change_indices_kernel(
         ys = keep.tile([P, PAIRS], U8, name="ys", align_bytes=64)
         out_rows = out_0.rearrange("(p t) q -> p t q", t=PACK)
         out_words = out_1[0].rearrange("p m t -> p (m t)").bitcast(I32)
-        yacc = [psum.tile([P, PACK, Y_COLS], F32, name=f"yacc{s}") for s in range(PAIRS // Y_COLS)]
+        yacc = [psum.tile([P, PACK, Y_COLS], F32, name=f"yacc{s}", tag=f"bank{(6, 7, 4, 5, 0, 1)[s]}") for s in range(PAIRS // Y_COLS)]
 
         def mix(b, c0, c1):
             for s0 in range(c0, c1, Y_COLS):
@@ -267,6 +337,7 @@ def tile_list_vegetation_change_indices_kernel(
 
         for c0, c1 in ((0, 512), (512, 768)):
             quantise_z(woven0[:, PACK * c0 : PACK * c1], 0, c0, c1)
+        nc.vector.quantize_mx(out=w2c[0][:].bitcast(FP8X4), scales=w2s[0][:], in_=w2b0[:])
         mix(0, 0, PAIRS)
         woven1 = keep.tile([P, PAIRS * PACK], BF16, name="woven1", align_bytes=64)
         runs = [(0, 128), (128, 384), (384, 640), (640, 768)]

@@ -23,8 +23,7 @@ PASSES = H // (P * PACK)
 SLICES = H // P
 BANK = 512
 Y_COLS = 128
-BY_GPSIMD = 6
-TURNED = 4
+BY_GPSIMD = 5
 
 
 def tile_list_vegetation_change_indices_kernel(
@@ -90,7 +89,7 @@ def tile_list_vegetation_change_indices_kernel(
         nc.vector.reciprocal(g_inv[:], g_t[:])
         nc.vector.tensor_scalar(g_sign[:], g_pos[:], -1.0, None, ALU.add)
 
-        late_g = slice(0, PACK)
+        late_g = slice(1, PACK)
         g_abs = keep.tile([P, PACK], F32, name="g_abs")
         g_root = keep.tile([P, PACK], F32, name="g_root")
         half = keep.tile([P, PACK], F32, name="half")
@@ -132,7 +131,7 @@ def tile_list_vegetation_change_indices_kernel(
             nc.scalar.activation(h[j][:, cols], acc[:], ACT.Sigmoid, bias=zero[:], scale=one[:])
 
         with tc.psum_pool(name="first", bufs=8) as first:
-            for j in range(SLICES):
+            for j in (0, 1, 2, 3, 4, 6, 7, 5):
                 for c in range(S // BANK):
                     width = BANK // 2 if (j, c) == (0, S // BANK - 1) else BANK
                     for lo in range(0, BANK, width):
@@ -181,33 +180,44 @@ def tile_list_vegetation_change_indices_kernel(
                         is_transpose=True,
                     )
 
-        early = {}
-        for j in range(SLICES):
-            if j == SLICES - 1:
-                early[j] = row(diff, SLICES - 2)
-            else:
-                early[j] = keep.tile([P, PAIRS], F32, name=f"early{j}", tag=f"early{j}", align_bytes=64)[:]
-            if j == BY_GPSIMD - 1:
-                late = row(diff, SLICES - 1)
-            elif j < BY_GPSIMD:
-                late = keep.tile([P, PAIRS], F32, name=f"late{j}", tag=f"late{j}", align_bytes=64)[:]
+        def open_turned(j, bank):
+            turned[j] = [
+                psum.tile([P, c1 - c0], F32, name=f"turned{j}_{k}", tag=f"bank{bank + k}")
+                for k, (c0, c1) in enumerate(spans)
+            ]
+
+        for j in range(BY_GPSIMD):
+            early = keep.tile([P, PAIRS], F32, name=f"early{j}", align_bytes=64)
+            late = keep.tile([P, PAIRS], F32, name=f"late{j}", align_bytes=64)
             width = PAIRS // 2 if j == 0 else PAIRS
             for c0 in range(0, PAIRS, width):
                 cols = slice(c0, c0 + width)
                 entries = slice(c0 // 16, (c0 + width) // 16)
-                nc.vector.tensor_copy(early[j][:, cols], h[j][:].indirect(pos2_t[:, entries]))
-                if j < BY_GPSIMD:
-                    nc.vector.tensor_copy(late[:, cols], h[j][:].indirect(pos1_t[:, entries]))
-                    if j != TURNED:
-                        nc.gpsimd.tensor_tensor(row(total, j)[:, cols], late[:, cols], early[j][:, cols], ALU.add)
-                    nc.gpsimd.tensor_tensor(row(diff, j)[:, cols], late[:, cols], early[j][:, cols], ALU.subtract)
-            if j == TURNED:
-                turned[j] = [
-                    psum.tile([P, c1 - c0], F32, name=f"turned{j}_{k}", tag=f"bank{4 + k}")
-                    for k, (c0, c1) in enumerate(spans)
-                ]
-                add_turned(j, early[j], True, False)
-                add_turned(j, late, False, True)
+                nc.vector.tensor_copy(early[:, cols], h[j][:].indirect(pos2_t[:, entries]))
+                nc.vector.tensor_copy(late[:, cols], h[j][:].indirect(pos1_t[:, entries]))
+                nc.gpsimd.tensor_tensor(row(total, j)[:, cols], late[:, cols], early[:, cols], ALU.add)
+                nc.gpsimd.tensor_tensor(row(diff, j)[:, cols], late[:, cols], early[:, cols], ALU.subtract)
+
+        early6, late5 = row(diff, 7), row(diff, 6)
+        nc.vector.tensor_copy(early6, h[6][:].indirect(pos2_t[:]))
+        open_turned(6, 4)
+        add_turned(6, early6, True, False)
+        add_turned(6, early6, False, False)
+        early5 = keep.tile([P, PAIRS], F32, name="early5", align_bytes=64)
+        nc.vector.tensor_copy(early5[:], h[5][:].indirect(pos2_t[:]))
+        nc.vector.tensor_copy(late5, h[5][:].indirect(pos1_t[:]))
+        nc.gpsimd.tensor_tensor(row(diff, 5), late5, early5[:], ALU.subtract)
+        open_turned(5, 6)
+        add_turned(5, early5[:], True, False)
+        add_turned(5, late5, False, True)
+        early7 = keep.tile([P, PAIRS], F32, name="early7", tag="h5", align_bytes=64)
+        nc.vector.tensor_copy(early7[:], h[7][:].indirect(pos2_t[:]))
+        open_turned(7, 0)
+        add_turned(7, early7[:], True, False)
+        add_turned(7, early7[:], False, False)
+        for j, early in ((6, early6), (7, early7[:])):
+            nc.vector.tensor_tensor(row(diff, j), h[j][:].indirect(pos1_t[:]), early, ALU.subtract)
+            add_turned(j, row(diff, j), False, True)
 
         roots = {}
 
@@ -219,57 +229,35 @@ def tile_list_vegetation_change_indices_kernel(
         def square(j):
             nc.scalar.activation(row(total, j), roots[j][:], ACT.Square)
 
-        w2b0 = keep.tile([P, N * PACK], BF16, name="w2b0", tag="vw1", align_bytes=64)
-        back = {}
-
-        def turned_root(j, pool, tag, bank):
+        def turned_root(j, pool, tag):
             roots[j] = pool.tile([P, PAIRS], F32, name=f"root{j}", tag=tag, align_bytes=64)
-            back[j] = [
-                psum.tile([P, c1 - c0], F32, name=f"back{j}_{k}", tag=f"bank{bank + k}")
-                for k, (c0, c1) in enumerate(spans)
-            ]
             for k, (c0, c1) in enumerate(spans):
                 nc.scalar.activation(roots[j][:, c0:c1], turned[j][k][:], ACT.Abs_reciprocal_sqrt)
-                for c in range(c0, c1, P):
-                    nc.tensor.transpose(back[j][k][:, c - c0 : c - c0 + P], roots[j][:, c : c + P], ident[:])
 
-        def turned_square(j):
-            for k, (c0, c1) in enumerate(spans):
-                nc.scalar.activation(
-                    row(total, j)[:, c0:c1], back[j][k][:], ACT.Square, scale=g_root[:, j - PACK : j - PACK + 1]
-                )
-
-        for j in range(TURNED):
+        w2b = [keep.tile([P, N * PACK], BF16, name=f"w2b{b}", tag=f"vw{b + 1}", align_bytes=64) for b in range(PASSES)]
+        for j in range(BY_GPSIMD):
             take_root(j)
             square(j)
             if j == 2:
-                weave_w2(w2b0, 0)
-        turned_root(TURNED, ring, "root", 6)
-        round_w2(1)
-        turned_square(TURNED)
-        for j in range(BY_GPSIMD, SLICES):
-            turned[j] = [
-                psum.tile([P, c1 - c0], F32, name=f"turned{j}_{k}", tag=f"bank{4 + 2 * (j - BY_GPSIMD) + k}")
-                for k, (c0, c1) in enumerate(spans)
-            ]
-            add_turned(j, early[j], True, False)
-            add_turned(j, early[j], False, False)
-        for j in range(SLICES - 1, BY_GPSIMD - 1, -1):
-            nc.vector.tensor_tensor(row(diff, j), h[j][:].indirect(pos1_t[:]), early[j], ALU.subtract)
-            add_turned(j, row(diff, j), False, True)
-
-        take_root(BY_GPSIMD - 1)
-        square(BY_GPSIMD - 1)
-        for j in range(SLICES - 1, BY_GPSIMD - 1, -1):
-            turned_root(j, keep, f"root{j}", 2 * (SLICES - 1 - j))
-        for j in range(SLICES - 1, BY_GPSIMD - 1, -1):
-            turned_square(j)
-        w2b1 = keep.tile([P, N * PACK], BF16, name="w2b1", tag=f"root{SLICES - 1}", align_bytes=64)
-        weave_w2(w2b1, 1)
+                weave_w2(w2b[0], 0)
+            if j == 3:
+                round_w2(1)
+        turned_root(5, ring, "root")
+        weave_w2(w2b[1], 1)
+        turned_root(6, keep, "root6")
+        turned_root(7, keep, "root7")
+        for k, (c0, c1) in enumerate(spans):
+            for j, bank in ((5, 2), (6, 6), (7, 4)):
+                back = psum.tile([P, c1 - c0], F32, name=f"back{j}_{k}", tag=f"bank{bank + k}")
+                for c in range(c0, c1, P):
+                    nc.tensor.transpose(back[:, c - c0 : c - c0 + P], roots[j][:, c : c + P], ident[:])
+                nc.scalar.activation(
+                    row(total, j)[:, c0:c1], back[:], ACT.Square, scale=g_root[:, j - PACK : j - PACK + 1]
+                )
 
         def ratio(woven, b, c0, c1):
             nc.vector.tensor_tensor(
-                woven[:, PACK * c0 : PACK * c1].rearrange("p (c i t) -> p c t i", i=4, t=PACK),
+                woven.rearrange("p (c i t) -> p c t i", i=4, t=PACK),
                 diff[b][:, :, c0:c1].rearrange("p t (c i) -> p c t i", i=4),
                 total[b][:, :, c0:c1].rearrange("p t (c i) -> p c t i", i=4),
                 ALU.mult,
@@ -281,10 +269,13 @@ def tile_list_vegetation_change_indices_kernel(
                 zrow[:, :, c0:c1].rearrange("p t (c i) -> p c t i", i=4),
             )
 
-        woven0 = keep.tile([P, PAIRS * PACK], BF16, name="woven0", tag=f"h{SLICES - 2}", align_bytes=64)
-        ratio(woven0, 0, 0, PAIRS)
+        FIRST = 512
+        woven0 = [
+            keep.tile([P, FIRST * PACK], BF16, name="woven0a", tag="h7", align_bytes=64),
+            keep.tile([P, (PAIRS - FIRST) * PACK], BF16, name="woven0b", tag="root7", align_bytes=64),
+        ]
         w2c = [
-            keep.tile([P, N], U32, name="w2c0", tag=f"root{SLICES - 2}", align_bytes=64),
+            keep.tile([P, N], U32, name="w2c0", tag="root6", align_bytes=64),
             keep.tile([P, N], U32, name="w2c1", align_bytes=64),
         ]
         w2s = [keep.tile([P, N], U8, name=f"w2s{b}", align_bytes=64) for b in range(PASSES)]
@@ -298,7 +289,7 @@ def tile_list_vegetation_change_indices_kernel(
         ys = keep.tile([P, PAIRS], U8, name="ys", align_bytes=64)
         out_rows = out_0.rearrange("(p t) q -> p t q", t=PACK)
         out_words = out_1[0].rearrange("p m t -> p (m t)").bitcast(I32)
-        yacc = [psum.tile([P, PACK, Y_COLS], F32, name=f"yacc{s}", tag=f"bank{(6, 7, 4, 5, 0, 1)[s]}") for s in range(PAIRS // Y_COLS)]
+        yacc = [psum.tile([P, PACK, Y_COLS], F32, name=f"yacc{s}", tag=f"bank{(0, 1, 2, 6, 4, 3)[s]}") for s in range(PAIRS // Y_COLS)]
 
         def mix(b, c0, c1):
             for s0 in range(c0, c1, Y_COLS):
@@ -317,40 +308,52 @@ def tile_list_vegetation_change_indices_kernel(
         yf = keep.tile([P, PACK, PAIRS], F32, name="yf")
         yb = keep.tile([P, PAIRS * PACK], BF16, name="yb", align_bytes=64)
 
-        def hand_out(c0, c1):
+        def hand_out(c0, c1, by_vector):
             for s0 in range(c0, c1, Y_COLS):
                 cols = slice(s0, s0 + Y_COLS)
                 acc = yacc[s0 // Y_COLS]
-                if c1 == PAIRS:
+                if not by_vector:
                     nc.scalar.copy(
-                        yb[:, PACK * c0 : PACK * c1].rearrange("p (n t) -> p n t", t=PACK),
+                        yb[:, PACK * s0 : PACK * (s0 + Y_COLS)].rearrange("p (n t) -> p n t", t=PACK),
                         acc[:].rearrange("p t n -> p n t"),
                     )
                 nc.scalar.copy(yf[:, :, cols], acc[:])
-            if c1 < PAIRS:
+            (nc.scalar if c1 == PAIRS else nc.sync).dma_start(out_rows[:, :, c0:c1], yf[:, :, c0:c1])
+
+        def finish(c0, c1, by_vector):
+            if by_vector:
                 weave(nc.vector.tensor_copy, yb, yf, c0, c1)
             nc.vector.quantize_mx(
                 out=yc[:, c0:c1].bitcast(FP8X4), scales=ys[:, c0:c1], in_=yb[:, PACK * c0 : PACK * c1]
             )
-            (nc.scalar if c1 == PAIRS else nc.sync).dma_start(out_rows[:, :, c0:c1], yf[:, :, c0:c1])
-            nc.sync.dma_start(out_words[:, c0:c1], yc[:, c0:c1].bitcast(I32))
 
-        for c0, c1 in ((0, 512), (512, 768)):
-            quantise_z(woven0[:, PACK * c0 : PACK * c1], 0, c0, c1)
-        nc.vector.quantize_mx(out=w2c[0][:].bitcast(FP8X4), scales=w2s[0][:], in_=w2b0[:])
-        mix(0, 0, PAIRS)
+        ratio(woven0[0][:], 0, 0, FIRST)
+        nc.vector.quantize_mx(out=w2c[1][:].bitcast(FP8X4), scales=w2s[1][:], in_=w2b[1][:])
+        quantise_z(woven0[0][:], 0, 0, FIRST)
+        nc.vector.quantize_mx(out=w2c[0][:].bitcast(FP8X4), scales=w2s[0][:], in_=w2b[0][:])
         woven1 = keep.tile([P, PAIRS * PACK], BF16, name="woven1", align_bytes=64)
-        runs = [(0, 128), (128, 384), (384, 640), (640, 768)]
+        runs = [(0, 128), (128, 256), (256, 512), (512, 640), (640, 768)]
+        by_vector = (2, 3)
         for n in range(len(runs) + 1):
             if n < len(runs):
-                ratio(woven1, 1, *runs[n])
-            if n == 0:
-                nc.vector.quantize_mx(out=w2c[1][:].bitcast(FP8X4), scales=w2s[1][:], in_=w2b1[:])
-            if n > 0:
+                c0, c1 = runs[n]
+                ratio(woven1[:, PACK * c0 : PACK * c1], 1, c0, c1)
+            if 0 <= n - 1 < len(runs):
                 c0, c1 = runs[n - 1]
                 quantise_z(woven1[:, PACK * c0 : PACK * c1], 1, c0, c1)
+                mix(0, c0, c1)
                 mix(1, c0, c1)
-                hand_out(c0, c1)
+                hand_out(c0, c1, n - 1 in by_vector)
+            if n == 1:
+                ratio(woven0[1][:], 0, FIRST, PAIRS)
+            if n == 2:
+                quantise_z(woven0[1][:], 0, FIRST, PAIRS)
+        finish(0, 256, False)
+        finish(256, 512, True)
+        nc.sync.dma_start(out_words[:, :BANK], yc[:, :BANK].bitcast(I32))
+        finish(512, 640, True)
+        finish(640, 768, False)
+        nc.sync.dma_start(out_words[:, BANK:], yc[:, BANK:].bitcast(I32))
         for q in range(4):
             (nc.scalar, nc.sync)[q % 2].dma_start(
                 out_2[0, 4 * q : 4 * q + 4, :].bitcast(I32), ys[32 * q : 32 * q + 4, :].bitcast(I32)

@@ -37,12 +37,12 @@ def tile_list_vegetation_change_indices_kernel(
         offs_t = keep.tile([P, S // 16], U16, name="offs_t")
         pos1_t = keep.tile([P, PAIRS // 16], U16, name="pos1_t")
         pos2_t = keep.tile([P, PAIRS // 16], U16, name="pos2_t")
-        tabs = keep.tile([P, T], U8, name="tabs", align_bytes=64)
+        tabs = keep.tile([P, T], U8, name="tabs", tag="then_w2", align_bytes=64)
         g_t = keep.tile([P, PASSES, PACK], F32, name="g_t")
         zero = ring.tile([P, 1], F32, name="zero", tag="root", align_bytes=64)
         one = ring.tile([P, 1], F32, name="one", tag="root", align_bytes=64)
         seed_zero = keep.tile([P, 1], F32, name="seed_zero", tag="then_table")
-        w1s_raw = keep.tile([P, H], U8, name="w1s_raw", tag="then_w2", align_bytes=64)
+        w1s_raw = keep.tile([P, H], U8, name="w1s_raw", align_bytes=64)
         w1s = keep.tile([P, H], U8, name="w1s", align_bytes=64)
         vs = keep.tile([P, S], U8, name="vs", align_bytes=64)
         nc.gpsimd.memset(w1s_raw[:].bitcast(I32), 0)
@@ -79,8 +79,6 @@ def tile_list_vegetation_change_indices_kernel(
             nc.sync.dma_start(
                 w1s[32 * q : 32 * q + 4, :].bitcast(I32), w1s_dealt[32 * q : 32 * (q + 1) : 8, :].bitcast(I32)
             )
-        w2_raw = [keep.tile([P, PACK * N], F32, name="w2_raw0", tag="then_w2", align_bytes=64)]
-        nc.sync.dma_start(w2_raw[0][:], w2_rows[0])
 
         g_inv = keep.tile([P, PASSES, PACK], F32, name="g_inv")
         g_pos = keep.tile([P, PASSES, PACK], F32, name="g_pos")
@@ -102,9 +100,11 @@ def tile_list_vegetation_change_indices_kernel(
         vs_spread = keep.tile([P, S], U8, name="vs_spread", align_bytes=64)
         nc.vector.tensor_copy(vs_spread[:], tabs[:].indirect(offs_t[:]))
         for q in range(4):
-            nc.scalar.dma_start(
+            nc.sync.dma_start(
                 vs[32 * q : 32 * q + 4, :].bitcast(I32), vs_spread[32 * q : 32 * (q + 1) : 8, :].bitcast(I32)
             )
+        w2_raw = [keep.tile([P, PACK * N], F32, name="w2_raw0", tag="then_w2", align_bytes=64)]
+        nc.sync.dma_start(w2_raw[0][:], w2_rows[0])
         vw = []
         for c in range(S // BANK):
             vw.append(keep.tile([P, BANK], U32, name=f"vw{c}", tag=f"vw{c}", align_bytes=64))
@@ -272,7 +272,6 @@ def tile_list_vegetation_change_indices_kernel(
         FIRST = 512
         woven0 = [
             keep.tile([P, FIRST * PACK], BF16, name="woven0a", tag="h7", align_bytes=64),
-            keep.tile([P, (PAIRS - FIRST) * PACK], BF16, name="woven0b", tag="root7", align_bytes=64),
         ]
         w2c = [
             keep.tile([P, N], U32, name="w2c0", tag="root6", align_bytes=64),
@@ -317,7 +316,7 @@ def tile_list_vegetation_change_indices_kernel(
                         yb[:, PACK * s0 : PACK * (s0 + Y_COLS)].rearrange("p (n t) -> p n t", t=PACK),
                         acc[:].rearrange("p t n -> p n t"),
                     )
-                nc.scalar.copy(yf[:, :, cols], acc[:])
+                (nc.vector.tensor_copy if s0 == PAIRS - 2 * Y_COLS else nc.scalar.copy)(yf[:, :, cols], acc[:])
             (nc.scalar if c1 == PAIRS else nc.sync).dma_start(out_rows[:, :, c0:c1], yf[:, :, c0:c1])
 
         def finish(c0, c1, by_vector):
@@ -331,28 +330,32 @@ def tile_list_vegetation_change_indices_kernel(
         nc.vector.quantize_mx(out=w2c[1][:].bitcast(FP8X4), scales=w2s[1][:], in_=w2b[1][:])
         quantise_z(woven0[0][:], 0, 0, FIRST)
         nc.vector.quantize_mx(out=w2c[0][:].bitcast(FP8X4), scales=w2s[0][:], in_=w2b[0][:])
-        woven1 = keep.tile([P, PAIRS * PACK], BF16, name="woven1", align_bytes=64)
+        woven1 = {}
         runs = [(0, 128), (128, 256), (256, 512), (512, 640), (640, 768)]
         by_vector = (2, 3)
         for n in range(len(runs) + 1):
             if n < len(runs):
                 c0, c1 = runs[n]
-                ratio(woven1[:, PACK * c0 : PACK * c1], 1, c0, c1)
+                woven1[n] = keep.tile([P, (c1 - c0) * PACK], BF16, name=f"woven1_{n}", tag=f"woven1_{n}", align_bytes=64)
+                ratio(woven1[n][:], 1, c0, c1)
             if 0 <= n - 1 < len(runs):
                 c0, c1 = runs[n - 1]
-                quantise_z(woven1[:, PACK * c0 : PACK * c1], 1, c0, c1)
+                quantise_z(woven1[n - 1][:], 1, c0, c1)
                 mix(0, c0, c1)
                 mix(1, c0, c1)
                 hand_out(c0, c1, n - 1 in by_vector)
-            if n == 1:
-                ratio(woven0[1][:], 0, FIRST, PAIRS)
             if n == 2:
+                woven0.append(
+                    keep.tile([P, (PAIRS - FIRST) * PACK], BF16, name="woven0b", tag="woven1_1", align_bytes=64)
+                )
+                ratio(woven0[1][:], 0, FIRST, PAIRS)
+            if n == 3:
                 quantise_z(woven0[1][:], 0, FIRST, PAIRS)
         finish(0, 256, False)
         finish(256, 512, True)
         nc.sync.dma_start(out_words[:, :BANK], yc[:, :BANK].bitcast(I32))
-        finish(512, 640, True)
-        finish(640, 768, False)
+        weave(nc.vector.tensor_copy, yb, yf, 512, 640)
+        finish(512, 768, False)
         nc.sync.dma_start(out_words[:, BANK:], yc[:, BANK:].bitcast(I32))
         for q in range(4):
             (nc.scalar, nc.sync)[q % 2].dma_start(

@@ -24,6 +24,7 @@ SLICES = H // P
 BANK = 512
 Y_COLS = 128
 BY_GPSIMD = 5
+ROUNDED_BY_SCALAR = 2
 
 
 def tile_list_vegetation_change_indices_kernel(
@@ -97,21 +98,23 @@ def tile_list_vegetation_change_indices_kernel(
         nc.gpsimd.tensor_tensor(g_abs[:, late_g], g_t[:, 1, late_g], g_sign[:, 1, late_g], ALU.mult)
         nc.gpsimd.tensor_tensor(g_root[:, late_g], g_abs[:, late_g], half[:, late_g], ALU.pow)
 
-        vs_spread = keep.tile([P, S], U8, name="vs_spread", align_bytes=64)
+        vs_spread = keep.tile([P, S], U8, name="vs_spread", tag="then_w2_last", align_bytes=64)
         nc.vector.tensor_copy(vs_spread[:], tabs[:].indirect(offs_t[:]))
         for q in range(4):
             nc.sync.dma_start(
                 vs[32 * q : 32 * q + 4, :].bitcast(I32), vs_spread[32 * q : 32 * (q + 1) : 8, :].bitcast(I32)
             )
-        w2_raw = [keep.tile([P, PACK * N], F32, name="w2_raw0", tag="then_w2", align_bytes=64)]
-        nc.sync.dma_start(w2_raw[0][:], w2_rows[0])
+        lead = (PACK - ROUNDED_BY_SCALAR) * N
+        w2_both = keep.tile([P, PACK * N + lead], F32, name="w2_both", tag="then_w2", align_bytes=64)
+        w2_raw = [w2_both[:, : PACK * N], w2_both[:, PACK * N :]]
+        nc.sync.dma_start(w2_raw[0], w2_rows[0])
+        nc.sync.dma_start(w2_raw[1], w2_rows[1][:, :lead])
+        w2_last = keep.tile([P, ROUNDED_BY_SCALAR * N], F32, name="w2_last", tag="then_w2_last", align_bytes=64)
+        nc.sync.dma_start(w2_last[:], w2_rows[1][:, lead:])
         vw = []
         for c in range(S // BANK):
             vw.append(keep.tile([P, BANK], U32, name=f"vw{c}", tag=f"vw{c}", align_bytes=64))
             nc.vector.tensor_copy(vw[c][:], tabw[:].bitcast(U32).indirect(offs_t[:, 32 * c : 32 * (c + 1)]))
-
-        w2_raw.append(keep.tile([P, PACK * N], F32, name="w2_raw1", tag="then_table"))
-        nc.sync.dma_start(w2_raw[1][:], w2_rows[1])
 
         h = [keep.tile([P, S], F32, name=f"h{j}", tag=f"h{j}", align_bytes=64) for j in range(SLICES)]
 
@@ -138,19 +141,11 @@ def tile_list_vegetation_change_indices_kernel(
                         respond(first, j, c, lo, lo + width)
         psum = ctx.enter_context(tc.psum_pool(name="psum", bufs=1))
 
-        w2p = [
-            keep.tile([P, PACK, N], BF16, name="w2p0", align_bytes=64),
-            keep.tile([P, PACK, N], BF16, name="w2p1", tag="vw0", align_bytes=64),
-        ]
-        for j in range(PACK):
-            nc.gpsimd.tensor_scalar(
-                w2p[0][:, j, :], w2_raw[0][:, N * j : N * (j + 1)], g_sign[:, 0, j : j + 1], 0.0, ALU.mult, ALU.add
-            )
-
-        def round_w2(b):
-            for j in range(PACK):
-                nc.scalar.activation(
-                    w2p[b][:, j, :], w2_raw[b][:, N * j : N * (j + 1)], ACT.Copy, scale=g_sign[:, b, j : j + 1]
+        w2p = [keep.tile([P, PACK, N], BF16, name=f"w2p{b}", align_bytes=64) for b in range(PASSES)]
+        for b in range(PASSES):
+            for j in range(PACK - b * ROUNDED_BY_SCALAR):
+                nc.gpsimd.tensor_scalar(
+                    w2p[b][:, j, :], w2_raw[b][:, N * j : N * (j + 1)], g_sign[:, b, j : j + 1], 0.0, ALU.mult, ALU.add
                 )
 
         def weave_w2(w2b, b):
@@ -159,8 +154,10 @@ def tile_list_vegetation_change_indices_kernel(
                 w2p[b][:].rearrange("p j (m t) -> p m j t", t=PACK),
             )
 
-        diff = [keep.tile([P, PACK, PAIRS], F32, name=f"diff{b}", align_bytes=64) for b in range(PASSES)]
-        total = [keep.tile([P, PACK, PAIRS], F32, name=f"total{b}", align_bytes=64) for b in range(PASSES)]
+        first_pass = keep.tile([P, 2 * PACK * PAIRS], F32, name="first_pass", tag="then_w2", align_bytes=64)
+        first_rows = first_pass[:].rearrange("p (u t c) -> p u t c", u=2, t=PACK)
+        diff = [first_rows[:, 0], keep.tile([P, PACK, PAIRS], F32, name="diff1", align_bytes=64)[:]]
+        total = [first_rows[:, 1], keep.tile([P, PACK, PAIRS], F32, name="total1", align_bytes=64)[:]]
 
         def row(tiles, j):
             return tiles[j // PACK][:, j % PACK, :]
@@ -234,15 +231,23 @@ def tile_list_vegetation_change_indices_kernel(
             for k, (c0, c1) in enumerate(spans):
                 nc.scalar.activation(roots[j][:, c0:c1], turned[j][k][:], ACT.Abs_reciprocal_sqrt)
 
-        w2b = [keep.tile([P, N * PACK], BF16, name=f"w2b{b}", tag=f"vw{b + 1}", align_bytes=64) for b in range(PASSES)]
+        w2b = [keep.tile([P, N * PACK], BF16, name="w2b0", tag="vw1", align_bytes=64)]
         for j in range(BY_GPSIMD):
             take_root(j)
             square(j)
             if j == 2:
                 weave_w2(w2b[0], 0)
             if j == 3:
-                round_w2(1)
+                for i in range(ROUNDED_BY_SCALAR):
+                    plane = PACK - ROUNDED_BY_SCALAR + i
+                    nc.scalar.activation(
+                        w2p[1][:, plane, :],
+                        w2_last[:, N * i : N * (i + 1)],
+                        ACT.Copy,
+                        scale=g_sign[:, 1, plane : plane + 1],
+                    )
         turned_root(5, ring, "root")
+        w2b.append(ring.tile([P, N * PACK], BF16, name="w2b1", tag="root", align_bytes=64))
         weave_w2(w2b[1], 1)
         turned_root(6, keep, "root6")
         turned_root(7, keep, "root7")
@@ -275,7 +280,7 @@ def tile_list_vegetation_change_indices_kernel(
         ]
         w2c = [
             keep.tile([P, N], U32, name="w2c0", tag="root6", align_bytes=64),
-            keep.tile([P, N], U32, name="w2c1", align_bytes=64),
+            keep.tile([P, N], U32, name="w2c1", tag="h5", align_bytes=64),
         ]
         w2s = [keep.tile([P, N], U8, name=f"w2s{b}", align_bytes=64) for b in range(PASSES)]
         zc = [keep.tile([P, PAIRS], U32, name=f"zc{b}", align_bytes=64) for b in range(PASSES)]

@@ -42,7 +42,7 @@ def tile_list_vegetation_change_indices_kernel(
         g_t = keep.tile([P, PASSES, PACK], F32, name="g_t")
         zero = ring.tile([P, 1], F32, name="zero", tag="root", align_bytes=64)
         one = ring.tile([P, 1], F32, name="one", tag="root", align_bytes=64)
-        seed_zero = keep.tile([P, 1], F32, name="seed_zero", tag="then_table")
+        seed_zero = keep.tile([P, 1], F32, name="seed_zero", tag="then_table", align_bytes=64)
         w1s_raw = keep.tile([P, H], U8, name="w1s_raw", align_bytes=64)
         w1s = keep.tile([P, H], U8, name="w1s", align_bytes=64)
         vs = keep.tile([P, S], U8, name="vs", align_bytes=64)
@@ -58,26 +58,30 @@ def tile_list_vegetation_change_indices_kernel(
         nc.scalar.dma_start(w1w_raw[:].bitcast(I32), w1_words[0].bitcast(I32))
         nc.scalar.dma_start(w1s_raw[0:P:8, :].bitcast(I32), w1_scales[0].bitcast(I32))
         nc.sync.dma_start(tabs[0:P:8, :].bitcast(I32), tab_scales[0].bitcast(I32))
-        tabw = keep.tile([P, T], I32, name="tabw", tag="then_table")
+        tabw = keep.tile([P, T], I32, name="tabw", tag="then_table", align_bytes=64)
         nc.sync.dma_start(tabw[:], tab_words[0].rearrange("p t i -> p (t i)").bitcast(I32))
         w2_rows = w2.rearrange("(b p j) n -> b p (j n)", b=PASSES, j=PACK)
         nc.sync.dma_start(pos2_t[:], pos2)
         nc.sync.dma_start(pos1_t[:], pos1)
         nc.scalar.dma_start(g_t[:], g.rearrange("(b p t) -> p b t", b=PASSES, t=PACK))
 
-        w1w = [keep.tile([P, 1024], U8, name=f"w1w{b}", align_bytes=64) for b in range(PASSES)]
-        for b in range(PASSES):
+        w1w = {}
+
+        def deal_w1(b, tag):
+            w1w[b] = keep.tile([P, 1024], U8, name=f"w1w{b}", tag=tag, align_bytes=64)
             nc.vector.tensor_copy(
                 w1w[b][:].bitcast(U16).rearrange("p (t m) -> p t m", t=PACK),
                 w1w_raw[:, H * b : H * (b + 1)].bitcast(U16).rearrange("p (m t) -> p t m", t=PACK),
             )
-        w1s_dealt = keep.tile([P, H], U8, name="w1s_dealt", align_bytes=64)
+
+        deal_w1(0, "w1w0")
+        w1s_dealt = keep.tile([P, H], U8, name="w1s_dealt", tag="then_g", align_bytes=64)
         nc.vector.tensor_copy(
             w1s_dealt[:].rearrange("p (b t m) -> p b t m", b=PASSES, t=PACK),
             w1s_raw[:].rearrange("p (b m t) -> p b t m", b=PASSES, t=PACK),
         )
         for q in range(4):
-            nc.sync.dma_start(
+            (nc.gpsimd if q < 2 else nc.sync).dma_start(
                 w1s[32 * q : 32 * q + 4, :].bitcast(I32), w1s_dealt[32 * q : 32 * (q + 1) : 8, :].bitcast(I32)
             )
 
@@ -89,7 +93,7 @@ def tile_list_vegetation_change_indices_kernel(
         nc.vector.tensor_scalar(g_sign[:], g_pos[:], -1.0, None, ALU.add)
 
         late_g = slice(1, PACK)
-        g_abs = keep.tile([P, PACK], F32, name="g_abs")
+        g_abs = keep.tile([P, PACK], F32, name="g_abs", tag="then_g", align_bytes=64)
         g_root = keep.tile([P, PACK], F32, name="g_root")
         half = keep.tile([P, PACK], F32, name="half")
         ident = keep.tile([P, P], F32, name="ident")
@@ -98,23 +102,33 @@ def tile_list_vegetation_change_indices_kernel(
         nc.gpsimd.tensor_tensor(g_abs[:, late_g], g_t[:, 1, late_g], g_sign[:, 1, late_g], ALU.mult)
         nc.gpsimd.tensor_tensor(g_root[:, late_g], g_abs[:, late_g], half[:, late_g], ALU.pow)
 
-        vs_spread = keep.tile([P, S], U8, name="vs_spread", tag="then_w2_last", align_bytes=64)
-        nc.vector.tensor_copy(vs_spread[:], tabs[:].indirect(offs_t[:]))
-        for q in range(4):
-            nc.sync.dma_start(
-                vs[32 * q : 32 * q + 4, :].bitcast(I32), vs_spread[32 * q : 32 * (q + 1) : 8, :].bitcast(I32)
+        for c0, c1 in ((0, 2 * BANK), (2 * BANK, S)):
+            vs_spread = keep.tile(
+                [P, c1 - c0], U8, name=f"vs_spread{c0}", tag="then_w2_last" if c1 == S else "spread", align_bytes=64
             )
+            nc.vector.tensor_copy(vs_spread[:], tabs[:].indirect(offs_t[:, c0 // 16 : c1 // 16]))
+            for q in range(4):
+                nc.sync.dma_start(
+                    vs[32 * q : 32 * q + 4, c0:c1].bitcast(I32),
+                    vs_spread[32 * q : 32 * (q + 1) : 8, :].bitcast(I32),
+                )
         lead = (PACK - ROUNDED_BY_SCALAR) * N
         w2_both = keep.tile([P, PACK * N + lead], F32, name="w2_both", tag="then_w2", align_bytes=64)
         w2_raw = [w2_both[:, : PACK * N], w2_both[:, PACK * N :]]
-        nc.sync.dma_start(w2_raw[0], w2_rows[0])
+        for c0 in (0, 2 * N):
+            nc.sync.dma_start(w2_raw[0][:, c0 : c0 + 2 * N], w2_rows[0][:, c0 : c0 + 2 * N])
         nc.sync.dma_start(w2_raw[1], w2_rows[1][:, :lead])
         w2_last = keep.tile([P, ROUNDED_BY_SCALAR * N], F32, name="w2_last", tag="then_w2_last", align_bytes=64)
         nc.sync.dma_start(w2_last[:], w2_rows[1][:, lead:])
         vw = []
         for c in range(S // BANK):
             vw.append(keep.tile([P, BANK], U32, name=f"vw{c}", tag=f"vw{c}", align_bytes=64))
-            nc.vector.tensor_copy(vw[c][:], tabw[:].bitcast(U32).indirect(offs_t[:, 32 * c : 32 * (c + 1)]))
+            width = BANK // 2 if c == S // BANK - 1 else BANK
+            for lo in range(0, BANK, width):
+                entries = slice((BANK * c + lo) // 16, (BANK * c + lo + width) // 16)
+                nc.vector.tensor_copy(vw[c][:, lo : lo + width], tabw[:].bitcast(U32).indirect(offs_t[:, entries]))
+
+        deal_w1(1, "then_table")
 
         h = [keep.tile([P, S], F32, name=f"h{j}", tag=f"h{j}", align_bytes=64) for j in range(SLICES)]
 
@@ -136,9 +150,9 @@ def tile_list_vegetation_change_indices_kernel(
         with tc.psum_pool(name="first", bufs=8) as first:
             for j in (0, 1, 2, 3, 4, 6, 7, 5):
                 for c in range(S // BANK):
-                    width = BANK // 2 if (j, c) == (0, S // BANK - 1) else BANK
-                    for lo in range(0, BANK, width):
-                        respond(first, j, c, lo, lo + width)
+                    cuts = (0, 256, 384, BANK) if (j, c) == (0, S // BANK - 1) else (0, BANK)
+                    for lo, hi in zip(cuts, cuts[1:]):
+                        respond(first, j, c, lo, hi)
         psum = ctx.enter_context(tc.psum_pool(name="psum", bufs=1))
 
         w2p = [keep.tile([P, PACK, N], BF16, name=f"w2p{b}", align_bytes=64) for b in range(PASSES)]

@@ -25,6 +25,7 @@ BANK = 512
 Y_COLS = 128
 BY_GPSIMD = 5
 ROUNDED_BY_SCALAR = 2
+EARLY = 512
 
 
 def tile_list_vegetation_change_indices_kernel(
@@ -39,31 +40,32 @@ def tile_list_vegetation_change_indices_kernel(
         pos1_t = keep.tile([P, PAIRS // 16], U16, name="pos1_t")
         pos2_t = keep.tile([P, PAIRS // 16], U16, name="pos2_t")
         tabs = keep.tile([P, T], U8, name="tabs", tag="then_w2", align_bytes=64)
-        g_t = keep.tile([P, PASSES, PACK], F32, name="g_t")
         zero = ring.tile([P, 1], F32, name="zero", tag="root", align_bytes=64)
         one = ring.tile([P, 1], F32, name="one", tag="root", align_bytes=64)
-        seed_zero = keep.tile([P, 1], F32, name="seed_zero", tag="then_table", align_bytes=64)
+        tabw = keep.tile([P, T], I32, name="tabw", tag="then_table", align_bytes=64)
+        zeros = tabw[:, T - 8 :]
         w1s_raw = keep.tile([P, H], U8, name="w1s_raw", align_bytes=64)
         w1s = keep.tile([P, H], U8, name="w1s", align_bytes=64)
         vs = keep.tile([P, S], U8, name="vs", align_bytes=64)
         nc.gpsimd.memset(w1s_raw[:].bitcast(I32), 0)
-        nc.vector.memset(seed_zero[:], 0.0)
+        nc.vector.memset(zeros, 0)
         nc.vector.memset(tabs[:].bitcast(I32), 0)
-        nc.vector.tensor_copy(zero[:], seed_zero[:])
+        nc.vector.tensor_copy(vs[:, :32].bitcast(I32), zeros)
+        nc.vector.memset(zero[:], 0.0)
         nc.vector.memset(one[:], 1.0)
         nc.vector.memset(w1s[:].bitcast(I32), 0)
-        nc.vector.memset(vs[:].bitcast(I32), 0)
+        nc.vector.memset(vs[:, 32:].bitcast(I32), 0)
         nc.sync.dma_start(offs_t[:], offs)
+        tab_rows = tab_words[0].rearrange("p t i -> p (t i)").bitcast(I32)
+        nc.sync.dma_start(tabw[:, :EARLY], tab_rows[:, :EARLY])
         w1w_raw = keep.tile([P, 2 * H], U8, name="w1w_raw", align_bytes=64)
         nc.scalar.dma_start(w1w_raw[:].bitcast(I32), w1_words[0].bitcast(I32))
         nc.scalar.dma_start(w1s_raw[0:P:8, :].bitcast(I32), w1_scales[0].bitcast(I32))
         nc.sync.dma_start(tabs[0:P:8, :].bitcast(I32), tab_scales[0].bitcast(I32))
-        tabw = keep.tile([P, T], I32, name="tabw", tag="then_table", align_bytes=64)
-        nc.sync.dma_start(tabw[:], tab_words[0].rearrange("p t i -> p (t i)").bitcast(I32))
+        nc.sync.dma_start(tabw[:, EARLY:], tab_rows[:, EARLY:])
         w2_rows = w2.rearrange("(b p j) n -> b p (j n)", b=PASSES, j=PACK)
         nc.sync.dma_start(pos2_t[:], pos2)
         nc.sync.dma_start(pos1_t[:], pos1)
-        nc.scalar.dma_start(g_t[:], g.rearrange("(b p t) -> p b t", b=PASSES, t=PACK))
 
         w1w = {}
 
@@ -75,7 +77,7 @@ def tile_list_vegetation_change_indices_kernel(
             )
 
         deal_w1(0, "w1w0")
-        w1s_dealt = keep.tile([P, H], U8, name="w1s_dealt", tag="then_g", align_bytes=64)
+        w1s_dealt = keep.tile([P, H], U8, name="w1s_dealt", align_bytes=64)
         nc.vector.tensor_copy(
             w1s_dealt[:].rearrange("p (b t m) -> p b t m", b=PASSES, t=PACK),
             w1s_raw[:].rearrange("p (b m t) -> p b t m", b=PASSES, t=PACK),
@@ -85,38 +87,35 @@ def tile_list_vegetation_change_indices_kernel(
                 w1s[32 * q : 32 * q + 4, :].bitcast(I32), w1s_dealt[32 * q : 32 * (q + 1) : 8, :].bitcast(I32)
             )
 
-        g_inv = keep.tile([P, PASSES, PACK], F32, name="g_inv")
-        g_pos = keep.tile([P, PASSES, PACK], F32, name="g_pos")
-        g_sign = keep.tile([P, PASSES, PACK], F32, name="g_sign")
-        nc.vector.tensor_scalar(g_pos[:], g_t[:], 0.0, 2.0, ALU.is_ge, ALU.mult)
-        nc.vector.reciprocal(g_inv[:], g_t[:])
-        nc.vector.tensor_scalar(g_sign[:], g_pos[:], -1.0, None, ALU.add)
-
-        late_g = slice(1, PACK)
-        g_abs = keep.tile([P, PACK], F32, name="g_abs", tag="then_g", align_bytes=64)
-        g_root = keep.tile([P, PACK], F32, name="g_root")
-        half = keep.tile([P, PACK], F32, name="half")
         ident = keep.tile([P, P], F32, name="ident")
         make_identity(nc, ident[:])
-        nc.gpsimd.memset(half[:, late_g], 0.5)
-        nc.gpsimd.tensor_tensor(g_abs[:, late_g], g_t[:, 1, late_g], g_sign[:, 1, late_g], ALU.mult)
-        nc.gpsimd.tensor_tensor(g_root[:, late_g], g_abs[:, late_g], half[:, late_g], ALU.pow)
 
+        spread = {}
         for c0, c1 in ((0, 2 * BANK), (2 * BANK, S)):
-            vs_spread = keep.tile(
+            spread[c0] = keep.tile(
                 [P, c1 - c0], U8, name=f"vs_spread{c0}", tag="then_w2_last" if c1 == S else "spread", align_bytes=64
             )
-            nc.vector.tensor_copy(vs_spread[:], tabs[:].indirect(offs_t[:, c0 // 16 : c1 // 16]))
+            nc.vector.tensor_copy(spread[c0][:], tabs[:].indirect(offs_t[:, c0 // 16 : c1 // 16]))
+
+        def place_scales(c0, c1):
             for q in range(4):
                 nc.sync.dma_start(
                     vs[32 * q : 32 * q + 4, c0:c1].bitcast(I32),
-                    vs_spread[32 * q : 32 * (q + 1) : 8, :].bitcast(I32),
+                    spread[c0][32 * q : 32 * (q + 1) : 8, :].bitcast(I32),
                 )
+
         lead = (PACK - ROUNDED_BY_SCALAR) * N
-        w2_both = keep.tile([P, PACK * N + lead], F32, name="w2_both", tag="then_w2", align_bytes=64)
-        w2_raw = [w2_both[:, : PACK * N], w2_both[:, PACK * N :]]
-        for c0 in (0, 2 * N):
-            nc.sync.dma_start(w2_raw[0][:, c0 : c0 + 2 * N], w2_rows[0][:, c0 : c0 + 2 * N])
+        w2_both = keep.tile([P, PACK * N + lead + SLICES], F32, name="w2_both", tag="then_w2", align_bytes=64)
+        w2_raw = [w2_both[:, : PACK * N], w2_both[:, PACK * N : PACK * N + lead]]
+        g_t = w2_both[:, PACK * N + lead :]
+        place_scales(0, 2 * BANK)
+        nc.sync.dma_start(
+            g_t.rearrange("p (b t) -> p b t", b=PASSES), g.rearrange("(b p t) -> p b t", b=PASSES, t=PACK)
+        )
+        nc.sync.dma_start(w2_raw[0][:, :N], w2_rows[0][:, :N])
+        place_scales(2 * BANK, S)
+        for c0, c1 in ((N, 2 * N), (2 * N, PACK * N)):
+            nc.sync.dma_start(w2_raw[0][:, c0:c1], w2_rows[0][:, c0:c1])
         nc.sync.dma_start(w2_raw[1], w2_rows[1][:, :lead])
         w2_last = keep.tile([P, ROUNDED_BY_SCALAR * N], F32, name="w2_last", tag="then_w2_last", align_bytes=64)
         nc.sync.dma_start(w2_last[:], w2_rows[1][:, lead:])
@@ -128,7 +127,14 @@ def tile_list_vegetation_change_indices_kernel(
                 entries = slice((BANK * c + lo) // 16, (BANK * c + lo + width) // 16)
                 nc.vector.tensor_copy(vw[c][:, lo : lo + width], tabw[:].bitcast(U32).indirect(offs_t[:, entries]))
 
+        g_pos = keep.tile([P, SLICES], F32, name="g_pos")
+        g_sign = keep.tile([P, PASSES, PACK], F32, name="g_sign")
+        g_inv = keep.tile([P, PASSES, PACK], F32, name="g_inv")
+        signs = g_sign[:].rearrange("p b t -> p (b t)")
+        nc.gpsimd.tensor_scalar(g_pos[:], g_t, 0.0, 2.0, ALU.is_ge, ALU.mult)
+        nc.gpsimd.tensor_scalar(signs, g_pos[:], 1.0, -1.0, ALU.mult, ALU.add)
         deal_w1(1, "then_table")
+        nc.vector.reciprocal(g_inv[:].rearrange("p b t -> p (b t)"), g_t)
 
         h = [keep.tile([P, S], F32, name=f"h{j}", tag=f"h{j}", align_bytes=64) for j in range(SLICES)]
 
@@ -198,7 +204,7 @@ def tile_list_vegetation_change_indices_kernel(
             ]
 
         for j in range(BY_GPSIMD):
-            early = keep.tile([P, PAIRS], F32, name=f"early{j}", align_bytes=64)
+            early = keep.tile([P, PAIRS], F32, name=f"early{j}", tag=f"early{j}", align_bytes=64)
             late = keep.tile([P, PAIRS], F32, name=f"late{j}", align_bytes=64)
             width = PAIRS // 2 if j == 0 else PAIRS
             for c0 in range(0, PAIRS, width):
@@ -260,6 +266,8 @@ def tile_list_vegetation_change_indices_kernel(
                         ACT.Copy,
                         scale=g_sign[:, 1, plane : plane + 1],
                     )
+        g_root = keep.tile([P, PACK], F32, name="g_root", tag="early3", align_bytes=64)
+        nc.scalar.activation(g_root[:, 1:], g_inv[:, 1, 1:], ACT.Abs_reciprocal_sqrt)
         turned_root(5, ring, "root")
         w2b.append(ring.tile([P, N * PACK], BF16, name="w2b1", tag="root", align_bytes=64))
         weave_w2(w2b[1], 1)

@@ -44,7 +44,7 @@ def tile_list_vegetation_change_indices_kernel(
         one = ring.tile([P, 1], F32, name="one", tag="root", align_bytes=64)
         tabw = keep.tile([P, T], I32, name="tabw", tag="then_table", align_bytes=64)
         zeros = tabw[:, T - 8 :]
-        w1s_raw = keep.tile([P, H], U8, name="w1s_raw", align_bytes=64)
+        w1s_raw = keep.tile([P, H], U8, name="w1s_raw", tag="then_ident", align_bytes=64)
         w1s = keep.tile([P, H], U8, name="w1s", align_bytes=64)
         vs = keep.tile([P, S], U8, name="vs", align_bytes=64)
         nc.gpsimd.memset(w1s_raw[:].bitcast(I32), 0)
@@ -69,25 +69,28 @@ def tile_list_vegetation_change_indices_kernel(
 
         w1w = {}
 
-        def deal_w1(b, tag):
-            w1w[b] = keep.tile([P, 1024], U8, name=f"w1w{b}", tag=tag, align_bytes=64)
+        def deal_w1(tile, j0, j1):
+            b, t0 = divmod(j0, PACK)
             nc.vector.tensor_copy(
-                w1w[b][:].bitcast(U16).rearrange("p (t m) -> p t m", t=PACK),
-                w1w_raw[:, H * b : H * (b + 1)].bitcast(U16).rearrange("p (m t) -> p t m", t=PACK),
+                tile.bitcast(U16).rearrange("p (t m) -> p t m", t=j1 - j0),
+                w1w_raw[:, H * b : H * (b + 1)].bitcast(U16).rearrange("p (m t) -> p t m", t=PACK)[:, t0 : t0 + j1 - j0],
             )
+            for j in range(j0, j1):
+                w1w[j] = tile[:, 2 * P * (j - j0) : 2 * P * (j - j0 + 1)]
 
-        deal_w1(0, "w1w0")
         w1s_dealt = keep.tile([P, H], U8, name="w1s_dealt", align_bytes=64)
         nc.vector.tensor_copy(
             w1s_dealt[:].rearrange("p (b t m) -> p b t m", b=PASSES, t=PACK),
             w1s_raw[:].rearrange("p (b m t) -> p b t m", b=PASSES, t=PACK),
         )
+        w1w_first = keep.tile([P, 2 * P], U8, name="w1w_first", align_bytes=64)
+        deal_w1(w1w_first[:], 0, 1)
         for q in range(4):
             (nc.gpsimd if q < 2 else nc.sync).dma_start(
                 w1s[32 * q : 32 * q + 4, :].bitcast(I32), w1s_dealt[32 * q : 32 * (q + 1) : 8, :].bitcast(I32)
             )
 
-        ident = keep.tile([P, P], F32, name="ident")
+        ident = keep.tile([P, P], F32, name="ident", tag="then_ident", align_bytes=64)
         make_identity(nc, ident[:])
 
         spread = {}
@@ -133,18 +136,19 @@ def tile_list_vegetation_change_indices_kernel(
         signs = g_sign[:].rearrange("p b t -> p (b t)")
         nc.gpsimd.tensor_scalar(g_pos[:], g_t, 0.0, 2.0, ALU.is_ge, ALU.mult)
         nc.gpsimd.tensor_scalar(signs, g_pos[:], 1.0, -1.0, ALU.mult, ALU.add)
-        deal_w1(1, "then_table")
+        w1w_rest = keep.tile([P, 2 * P * (SLICES - 1)], U8, name="w1w_rest", tag="then_table", align_bytes=64)
+        deal_w1(w1w_rest[:, : 2 * P * (PACK - 1)], 1, PACK)
+        deal_w1(w1w_rest[:, 2 * P * (PACK - 1) :], PACK, SLICES)
         nc.vector.reciprocal(g_inv[:].rearrange("p b t -> p (b t)"), g_t)
 
         h = [keep.tile([P, S], F32, name=f"h{j}", tag=f"h{j}", align_bytes=64) for j in range(SLICES)]
 
         def respond(psum, j, c, lo, hi):
-            b, t = divmod(j, PACK)
             cols = slice(BANK * c + lo, BANK * c + hi)
             acc = psum.tile([P, hi - lo], F32, name="acc")
             nc.tensor.matmul_mx(
                 out=acc[:],
-                lhsT=w1w[b][:, 256 * t : 256 * (t + 1)].bitcast(FP4X4),
+                lhsT=w1w[j].bitcast(FP4X4),
                 lhsT_scale=w1s[:, P * j : P * (j + 1)],
                 rhs=vw[c][:, lo:hi].bitcast(FP8X4),
                 rhs_scale=vs[:, cols],
@@ -343,7 +347,7 @@ def tile_list_vegetation_change_indices_kernel(
                         yb[:, PACK * s0 : PACK * (s0 + Y_COLS)].rearrange("p (n t) -> p n t", t=PACK),
                         acc[:].rearrange("p t n -> p n t"),
                     )
-                (nc.vector.tensor_copy if s0 == PAIRS - 2 * Y_COLS else nc.scalar.copy)(yf[:, :, cols], acc[:])
+                nc.scalar.copy(yf[:, :, cols], acc[:])
             (nc.scalar if c1 == PAIRS else nc.sync).dma_start(out_rows[:, :, c0:c1], yf[:, :, c0:c1])
 
         def finish(c0, c1, by_vector):
@@ -359,7 +363,7 @@ def tile_list_vegetation_change_indices_kernel(
         nc.vector.quantize_mx(out=w2c[0][:].bitcast(FP8X4), scales=w2s[0][:], in_=w2b[0][:])
         woven1 = {}
         runs = [(0, 128), (128, 256), (256, 512), (512, 640), (640, 768)]
-        by_vector = (2, 3)
+        by_vector = (2, 3, 4)
         for n in range(len(runs) + 1):
             if n < len(runs):
                 c0, c1 = runs[n]
@@ -380,10 +384,10 @@ def tile_list_vegetation_change_indices_kernel(
                 quantise_z(woven0[1][:], 0, FIRST, PAIRS)
         finish(0, 256, False)
         finish(256, 512, True)
-        nc.sync.dma_start(out_words[:, :BANK], yc[:, :BANK].bitcast(I32))
-        weave(nc.vector.tensor_copy, yb, yf, 512, 640)
-        finish(512, 768, False)
-        nc.sync.dma_start(out_words[:, BANK:], yc[:, BANK:].bitcast(I32))
+        finish(512, 640, True)
+        nc.sync.dma_start(out_words[:, :640], yc[:, :640].bitcast(I32))
+        finish(640, 768, True)
+        nc.sync.dma_start(out_words[:, 640:], yc[:, 640:].bitcast(I32))
         for q in range(4):
             (nc.scalar, nc.sync)[q % 2].dma_start(
                 out_2[0, 4 * q : 4 * q + 4, :].bitcast(I32), ys[32 * q : 32 * q + 4, :].bitcast(I32)

@@ -16,15 +16,19 @@ FP8X4 = mybir.dt.float8_e4m3fn_x4
 FP4X4 = mybir.dt.float4_e2m1fn_x4
 ACT = mybir.ActivationFunctionType
 ALU = mybir.AluOpType
+SIZE = {F32: 4, BF16: 2, I32: 4, U32: 4, U16: 2, U8: 1}
 
 P = 128
 PACK = 4
 PASSES = H // (P * PACK)
 SLICES = H // P
 BANK = 512
+BANKS = 8
 Y_COLS = 128
-BY_GPSIMD = 5
-ROUNDED_BY_SCALAR = 2
+SPLIT = 256
+PARTS = ((0, SPLIT), (SPLIT, PAIRS))
+WIDEST = max(SPLIT, PAIRS - SPLIT)
+SUMS_BY_GPSIMD = 2
 EARLY = 512
 
 
@@ -33,20 +37,45 @@ def tile_list_vegetation_change_indices_kernel(
 ):
     nc = tc.nc
     with ExitStack() as ctx:
-        keep = ctx.enter_context(tc.tile_pool(name="keep", bufs=1))
-        ring = ctx.enter_context(tc.tile_pool(name="ring", bufs=2))
+        lists = ctx.enter_context(tc.tile_pool(name="lists", bufs=1))
+        arena = ctx.enter_context(tc.tile_pool(name="arena", bufs=1))
+        psum = ctx.enter_context(tc.psum_pool(name="psum", bufs=1))
+        free = [0]
 
-        offs_t = keep.tile([P, S // 16], U16, name="offs_t")
-        pos1_t = keep.tile([P, PAIRS // 16], U16, name="pos1_t")
-        pos2_t = keep.tile([P, PAIRS // 16], U16, name="pos2_t")
-        tabs = keep.tile([P, T], U8, name="tabs", tag="then_w2", align_bytes=64)
-        zero = ring.tile([P, 1], F32, name="zero", tag="root", align_bytes=64)
-        one = ring.tile([P, 1], F32, name="one", tag="root", align_bytes=64)
-        tabw = keep.tile([P, T], I32, name="tabw", tag="then_table", align_bytes=64)
+        def room(width):
+            at = free[0]
+            free[0] = at + -(-width // 64) * 64
+            return at
+
+        def place(name, cols, dtype, at=None):
+            at = room(cols * SIZE[dtype]) if at is None else at
+            return arena.tile([P, cols], dtype, name=name, align_bytes=64, offset=at)
+
+        def bank(name, cols, number):
+            return psum.tile([P, cols], F32, name=name, offset=4 * BANK * number)
+
+        at_table = room(4 * T)
+        at_w2_late = room(4 * PACK * N)
+        at_gain = room(64)
+        at_w2 = [room(4 * PACK * N), at_w2_late]
+        at_w1_rest = room(2 * P * (SLICES - 1))
+        at_h = [room(4 * S) for j in range(SLICES)]
+        at_roots = [room(4 * WIDEST) for j in range(4)]
+        at_w2b = [room(2 * PACK * N) for b in range(PASSES)]
+        at_ident = room(H)
+        at_zero = room(64)
+
+        offs_t = lists.tile([P, S // 16], U16, name="offs_t")
+        pos1_t = lists.tile([P, PAIRS // 16], U16, name="pos1_t")
+        pos2_t = lists.tile([P, PAIRS // 16], U16, name="pos2_t")
+        tabs = place("tabs", T, U8, at_gain - T // 2)
+        zero = place("zero", 1, F32, at_zero)
+        one = place("one", 1, F32, at_roots[0])
+        tabw = place("tabw", T, I32, at_table)
         zeros = tabw[:, T - 8 :]
-        w1s_raw = keep.tile([P, H], U8, name="w1s_raw", tag="then_ident", align_bytes=64)
-        w1s = keep.tile([P, H], U8, name="w1s", align_bytes=64)
-        vs = keep.tile([P, S], U8, name="vs", align_bytes=64)
+        w1s_raw = place("w1s_raw", H, U8, at_ident)
+        w1s = place("w1s", H, U8)
+        vs = place("vs", S, U8)
         nc.gpsimd.memset(w1s_raw[:].bitcast(I32), 0)
         nc.vector.memset(zeros, 0)
         nc.vector.memset(tabs[:].bitcast(I32), 0)
@@ -58,7 +87,7 @@ def tile_list_vegetation_change_indices_kernel(
         nc.sync.dma_start(offs_t[:], offs)
         tab_rows = tab_words[0].rearrange("p t i -> p (t i)").bitcast(I32)
         nc.sync.dma_start(tabw[:, :EARLY], tab_rows[:, :EARLY])
-        w1w_raw = keep.tile([P, 2 * H], U8, name="w1w_raw", align_bytes=64)
+        w1w_raw = place("w1w_raw", 2 * H, U8)
         nc.scalar.dma_start(w1w_raw[:].bitcast(I32), w1_words[0].bitcast(I32))
         nc.scalar.dma_start(w1s_raw[0:P:8, :].bitcast(I32), w1_scales[0].bitcast(I32))
         nc.sync.dma_start(tabs[0:P:8, :].bitcast(I32), tab_scales[0].bitcast(I32))
@@ -78,26 +107,24 @@ def tile_list_vegetation_change_indices_kernel(
             for j in range(j0, j1):
                 w1w[j] = tile[:, 2 * P * (j - j0) : 2 * P * (j - j0 + 1)]
 
-        w1s_dealt = keep.tile([P, H], U8, name="w1s_dealt", align_bytes=64)
+        w1s_dealt = place("w1s_dealt", H, U8)
         nc.vector.tensor_copy(
             w1s_dealt[:].rearrange("p (b t m) -> p b t m", b=PASSES, t=PACK),
             w1s_raw[:].rearrange("p (b m t) -> p b t m", b=PASSES, t=PACK),
         )
-        w1w_first = keep.tile([P, 2 * P], U8, name="w1w_first", align_bytes=64)
+        w1w_first = place("w1w_first", 2 * P, U8)
         deal_w1(w1w_first[:], 0, 1)
         for q in range(4):
             (nc.gpsimd if q < 2 else nc.sync).dma_start(
                 w1s[32 * q : 32 * q + 4, :].bitcast(I32), w1s_dealt[32 * q : 32 * (q + 1) : 8, :].bitcast(I32)
             )
 
-        ident = keep.tile([P, P], F32, name="ident", tag="then_ident", align_bytes=64)
+        ident = place("ident", P, F32, at_ident)
         make_identity(nc, ident[:])
 
         spread = {}
         for c0, c1 in ((0, 2 * BANK), (2 * BANK, S)):
-            spread[c0] = keep.tile(
-                [P, c1 - c0], U8, name=f"vs_spread{c0}", tag="then_w2_last" if c1 == S else "spread", align_bytes=64
-            )
+            spread[c0] = place(f"vs_spread{c0}", c1 - c0, U8, at_w1_rest + 2 * P * (PACK - 2) if c1 == S else None)
             nc.vector.tensor_copy(spread[c0][:], tabs[:].indirect(offs_t[:, c0 // 16 : c1 // 16]))
 
         def place_scales(c0, c1):
@@ -107,45 +134,45 @@ def tile_list_vegetation_change_indices_kernel(
                     spread[c0][32 * q : 32 * (q + 1) : 8, :].bitcast(I32),
                 )
 
-        lead = (PACK - ROUNDED_BY_SCALAR) * N
-        w2_both = keep.tile([P, PACK * N + lead + SLICES], F32, name="w2_both", tag="then_w2", align_bytes=64)
-        w2_raw = [w2_both[:, : PACK * N], w2_both[:, PACK * N : PACK * N + lead]]
-        g_t = w2_both[:, PACK * N + lead :]
+        g_t = place("g_t", SLICES, F32, at_gain)
+        w2_raw = [place(f"w2_raw{b}", PACK * N, F32, at_w2[b]) for b in range(PASSES)]
         place_scales(0, 2 * BANK)
         nc.sync.dma_start(
-            g_t.rearrange("p (b t) -> p b t", b=PASSES), g.rearrange("(b p t) -> p b t", b=PASSES, t=PACK)
+            g_t[:].rearrange("p (b t) -> p b t", b=PASSES), g.rearrange("(b p t) -> p b t", b=PASSES, t=PACK)
         )
         nc.sync.dma_start(w2_raw[0][:, :N], w2_rows[0][:, :N])
         place_scales(2 * BANK, S)
         for c0, c1 in ((N, 2 * N), (2 * N, PACK * N)):
             nc.sync.dma_start(w2_raw[0][:, c0:c1], w2_rows[0][:, c0:c1])
-        nc.sync.dma_start(w2_raw[1], w2_rows[1][:, :lead])
-        w2_last = keep.tile([P, ROUNDED_BY_SCALAR * N], F32, name="w2_last", tag="then_w2_last", align_bytes=64)
-        nc.sync.dma_start(w2_last[:], w2_rows[1][:, lead:])
+        for c0, c1 in ((0, 2 * N), (2 * N, PACK * N)):
+            nc.sync.dma_start(w2_raw[1][:, c0:c1], w2_rows[1][:, c0:c1])
         vw = []
         for c in range(S // BANK):
-            vw.append(keep.tile([P, BANK], U32, name=f"vw{c}", tag=f"vw{c}", align_bytes=64))
+            vw.append(place(f"vw{c}", BANK, U32))
             width = BANK // 2 if c == S // BANK - 1 else BANK
             for lo in range(0, BANK, width):
                 entries = slice((BANK * c + lo) // 16, (BANK * c + lo + width) // 16)
                 nc.vector.tensor_copy(vw[c][:, lo : lo + width], tabw[:].bitcast(U32).indirect(offs_t[:, entries]))
 
-        g_pos = keep.tile([P, SLICES], F32, name="g_pos")
-        g_sign = keep.tile([P, PASSES, PACK], F32, name="g_sign")
-        g_inv = keep.tile([P, PASSES, PACK], F32, name="g_inv")
-        signs = g_sign[:].rearrange("p b t -> p (b t)")
-        nc.gpsimd.tensor_scalar(g_pos[:], g_t, 0.0, 2.0, ALU.is_ge, ALU.mult)
-        nc.gpsimd.tensor_scalar(signs, g_pos[:], 1.0, -1.0, ALU.mult, ALU.add)
-        w1w_rest = keep.tile([P, 2 * P * (SLICES - 1)], U8, name="w1w_rest", tag="then_table", align_bytes=64)
+        g_pos = place("g_pos", SLICES, F32)
+        g_sign = place("g_sign", SLICES, F32)
+        g_inv = place("g_inv", SLICES, F32)
+        nc.gpsimd.tensor_scalar(g_pos[:], g_t[:], 0.0, 2.0, ALU.is_ge, ALU.mult)
+        nc.gpsimd.tensor_scalar(g_sign[:], g_pos[:], 1.0, -1.0, ALU.mult, ALU.add)
+        w1w_rest = place("w1w_rest", 2 * P * (SLICES - 1), U8, at_w1_rest)
         deal_w1(w1w_rest[:, : 2 * P * (PACK - 1)], 1, PACK)
         deal_w1(w1w_rest[:, 2 * P * (PACK - 1) :], PACK, SLICES)
-        nc.vector.reciprocal(g_inv[:].rearrange("p b t -> p (b t)"), g_t)
+        nc.vector.reciprocal(g_inv[:], g_t[:])
 
-        h = [keep.tile([P, S], F32, name=f"h{j}", tag=f"h{j}", align_bytes=64) for j in range(SLICES)]
-
-        def respond(psum, j, c, lo, hi):
+        h = [place(f"h{j}", S, F32, at_h[j]) for j in range(SLICES)]
+        pieces = []
+        for j in range(SLICES):
+            for c in range(S // BANK):
+                cuts = (0, 256, 384, BANK) if (j, c) == (0, S // BANK - 1) else (0, BANK)
+                pieces.extend((j, c, lo, hi) for lo, hi in zip(cuts, cuts[1:]))
+        for n, (j, c, lo, hi) in enumerate(pieces):
             cols = slice(BANK * c + lo, BANK * c + hi)
-            acc = psum.tile([P, hi - lo], F32, name="acc")
+            acc = bank(f"acc{n}", hi - lo, n % BANKS)
             nc.tensor.matmul_mx(
                 out=acc[:],
                 lhsT=w1w[j].bitcast(FP4X4),
@@ -157,176 +184,186 @@ def tile_list_vegetation_change_indices_kernel(
             )
             nc.scalar.activation(h[j][:, cols], acc[:], ACT.Sigmoid, bias=zero[:], scale=one[:])
 
-        with tc.psum_pool(name="first", bufs=8) as first:
-            for j in (0, 1, 2, 3, 4, 6, 7, 5):
-                for c in range(S // BANK):
-                    cuts = (0, 256, 384, BANK) if (j, c) == (0, S // BANK - 1) else (0, BANK)
-                    for lo, hi in zip(cuts, cuts[1:]):
-                        respond(first, j, c, lo, hi)
-        psum = ctx.enter_context(tc.psum_pool(name="psum", bufs=1))
-
-        w2p = [keep.tile([P, PACK, N], BF16, name=f"w2p{b}", align_bytes=64) for b in range(PASSES)]
+        w2_pairs = [place(f"w2_pairs{b}", PACK * N, BF16) for b in range(PASSES)]
         for b in range(PASSES):
-            for j in range(PACK - b * ROUNDED_BY_SCALAR):
+            pairs = w2_pairs[b][:].rearrange("p (u n e) -> p u n e", u=2, e=2)
+            for j in range(PACK):
                 nc.gpsimd.tensor_scalar(
-                    w2p[b][:, j, :], w2_raw[b][:, N * j : N * (j + 1)], g_sign[:, b, j : j + 1], 0.0, ALU.mult, ALU.add
+                    pairs[:, j // 2, :, j % 2],
+                    w2_raw[b][:, N * j : N * (j + 1)],
+                    g_sign[:, PACK * b + j : PACK * b + j + 1],
+                    0.0,
+                    ALU.mult,
+                    ALU.add,
                 )
 
-        def weave_w2(w2b, b):
+        def weave_w2(b):
+            woven = place(f"w2b{b}", PACK * N, BF16, at_w2b[b])
             nc.scalar.copy(
-                w2b[:].rearrange("p (t m j) -> p m j t", t=PACK, j=PACK),
-                w2p[b][:].rearrange("p j (m t) -> p m j t", t=PACK),
+                woven[:].bitcast(U32).rearrange("p (t m u) -> p m u t", t=PACK, u=2),
+                w2_pairs[b][:].bitcast(U32).rearrange("p (u m t) -> p m u t", u=2, t=PACK),
             )
+            return woven
 
-        first_pass = keep.tile([P, 2 * PACK * PAIRS], F32, name="first_pass", tag="then_w2", align_bytes=64)
-        first_rows = first_pass[:].rearrange("p (u t c) -> p u t c", u=2, t=PACK)
-        diff = [first_rows[:, 0], keep.tile([P, PACK, PAIRS], F32, name="diff1", align_bytes=64)[:]]
-        total = [first_rows[:, 1], keep.tile([P, PACK, PAIRS], F32, name="total1", align_bytes=64)[:]]
+        halves = [slice(c0, c1) for c0, c1 in PARTS]
+        widths = [c1 - c0 for c0, c1 in PARTS]
+        work = place("work", 17 * PAIRS, F32)
+        rows = work[:].rearrange("p (r c) -> p r c", c=PAIRS)
+        diff0, diff1 = rows[:, 1:8:2, :], rows[:, 9:16:2, :]
+        early_row = (0, 5, 7, 4, 11, 13, 15, 16)
+        late_row = (1, 3, 2, 6, 10, 12, 14)
+        inverse0 = [
+            work[:, 10 * PAIRS - PACK * SPLIT : 10 * PAIRS].rearrange("p (t c) -> p t c", t=PACK),
+            place("inverse0b", PACK * widths[1], F32)[:].rearrange("p (t c) -> p t c", t=PACK),
+        ]
+        inverse1 = place("inverse1", PACK * PAIRS, F32)[:].rearrange("p (t c) -> p t c", t=PACK)
+        early, late, total, turned, roots = {}, {}, {}, {}, {}
 
-        def row(tiles, j):
-            return tiles[j // PACK][:, j % PACK, :]
+        def entries_of(k):
+            return slice(PARTS[k][0] // 16, PARTS[k][1] // 16)
 
-        spans = ((0, BANK), (BANK, PAIRS))
-        turned = {}
+        def pick(j, split):
+            early[j], late[j] = rows[:, early_row[j], :], rows[:, late_row[j], :]
+            nc.vector.tensor_copy(early[j], h[j][:].indirect(pos2_t[:]))
+            if split:
+                for k in range(2):
+                    nc.vector.tensor_copy(late[j][:, halves[k]], h[j][:].indirect(pos1_t[:, entries_of(k)]))
+            else:
+                nc.vector.tensor_copy(late[j], h[j][:].indirect(pos1_t[:]))
 
-        def add_turned(j, src, start, stop):
-            for k, (c0, c1) in enumerate(spans):
-                for c in range(c0, c1, P):
+        def turn(j, k, number, terms):
+            turned[j, k] = bank(f"turned{j}_{k}", widths[k], number)
+            for i, term in enumerate(terms):
+                for c in range(0, widths[k], P):
                     nc.tensor.matmul(
-                        turned[j][k][:, c - c0 : c - c0 + P],
-                        src[:, c : c + P],
+                        turned[j, k][:, c : c + P],
+                        term[:, PARTS[k][0] + c : PARTS[k][0] + c + P],
                         ident[:],
-                        start=(start and c == c0),
-                        stop=(stop and c == c1 - P),
+                        start=(i == 0 and c == 0),
+                        stop=(i == len(terms) - 1 and c == widths[k] - P),
                         is_transpose=True,
                     )
 
-        def open_turned(j, bank):
-            turned[j] = [
-                psum.tile([P, c1 - c0], F32, name=f"turned{j}_{k}", tag=f"bank{bank + k}")
-                for k, (c0, c1) in enumerate(spans)
-            ]
-
-        for j in range(BY_GPSIMD):
-            early = keep.tile([P, PAIRS], F32, name=f"early{j}", tag=f"early{j}", align_bytes=64)
-            late = keep.tile([P, PAIRS], F32, name=f"late{j}", align_bytes=64)
-            width = PAIRS // 2 if j == 0 else PAIRS
-            for c0 in range(0, PAIRS, width):
-                cols = slice(c0, c0 + width)
-                entries = slice(c0 // 16, (c0 + width) // 16)
-                nc.vector.tensor_copy(early[:, cols], h[j][:].indirect(pos2_t[:, entries]))
-                nc.vector.tensor_copy(late[:, cols], h[j][:].indirect(pos1_t[:, entries]))
-                nc.gpsimd.tensor_tensor(row(total, j)[:, cols], late[:, cols], early[:, cols], ALU.add)
-                nc.gpsimd.tensor_tensor(row(diff, j)[:, cols], late[:, cols], early[:, cols], ALU.subtract)
-
-        early6, late5 = row(diff, 7), row(diff, 6)
-        nc.vector.tensor_copy(early6, h[6][:].indirect(pos2_t[:]))
-        open_turned(6, 4)
-        add_turned(6, early6, True, False)
-        add_turned(6, early6, False, False)
-        early5 = keep.tile([P, PAIRS], F32, name="early5", align_bytes=64)
-        nc.vector.tensor_copy(early5[:], h[5][:].indirect(pos2_t[:]))
-        nc.vector.tensor_copy(late5, h[5][:].indirect(pos1_t[:]))
-        nc.gpsimd.tensor_tensor(row(diff, 5), late5, early5[:], ALU.subtract)
-        open_turned(5, 6)
-        add_turned(5, early5[:], True, False)
-        add_turned(5, late5, False, True)
-        early7 = keep.tile([P, PAIRS], F32, name="early7", tag="h5", align_bytes=64)
-        nc.vector.tensor_copy(early7[:], h[7][:].indirect(pos2_t[:]))
-        open_turned(7, 0)
-        add_turned(7, early7[:], True, False)
-        add_turned(7, early7[:], False, False)
-        for j, early in ((6, early6), (7, early7[:])):
-            nc.vector.tensor_tensor(row(diff, j), h[j][:].indirect(pos1_t[:]), early, ALU.subtract)
-            add_turned(j, row(diff, j), False, True)
-
-        roots = {}
-
-        def take_root(j):
-            b, t = divmod(j, PACK)
-            roots[j] = ring.tile([P, PAIRS], F32, name="root", tag="root", align_bytes=64)
-            nc.scalar.activation(roots[j][:], row(total, j), ACT.Abs_reciprocal_sqrt, scale=g_inv[:, b, t : t + 1])
-
-        def square(j):
-            nc.scalar.activation(row(total, j), roots[j][:], ACT.Square)
-
-        def turned_root(j, pool, tag):
-            roots[j] = pool.tile([P, PAIRS], F32, name=f"root{j}", tag=tag, align_bytes=64)
-            for k, (c0, c1) in enumerate(spans):
-                nc.scalar.activation(roots[j][:, c0:c1], turned[j][k][:], ACT.Abs_reciprocal_sqrt)
-
-        w2b = [keep.tile([P, N * PACK], BF16, name="w2b0", tag="vw1", align_bytes=64)]
-        for j in range(BY_GPSIMD):
-            take_root(j)
-            square(j)
-            if j == 2:
-                weave_w2(w2b[0], 0)
-            if j == 3:
-                for i in range(ROUNDED_BY_SCALAR):
-                    plane = PACK - ROUNDED_BY_SCALAR + i
-                    nc.scalar.activation(
-                        w2p[1][:, plane, :],
-                        w2_last[:, N * i : N * (i + 1)],
-                        ACT.Copy,
-                        scale=g_sign[:, 1, plane : plane + 1],
-                    )
-        g_root = keep.tile([P, PACK], F32, name="g_root", tag="early3", align_bytes=64)
-        nc.scalar.activation(g_root[:, 1:], g_inv[:, 1, 1:], ACT.Abs_reciprocal_sqrt)
-        turned_root(5, ring, "root")
-        w2b.append(ring.tile([P, N * PACK], BF16, name="w2b1", tag="root", align_bytes=64))
-        weave_w2(w2b[1], 1)
-        turned_root(6, keep, "root6")
-        turned_root(7, keep, "root7")
-        for k, (c0, c1) in enumerate(spans):
-            for j, bank in ((5, 2), (6, 6), (7, 4)):
-                back = psum.tile([P, c1 - c0], F32, name=f"back{j}_{k}", tag=f"bank{bank + k}")
-                for c in range(c0, c1, P):
-                    nc.tensor.transpose(back[:, c - c0 : c - c0 + P], roots[j][:, c : c + P], ident[:])
+        def take_root(j, k, at):
+            roots[j, k] = place(f"root{j}_{k}", widths[k], F32, at)
+            if j < SUMS_BY_GPSIMD:
                 nc.scalar.activation(
-                    row(total, j)[:, c0:c1], back[:], ACT.Square, scale=g_root[:, j - PACK : j - PACK + 1]
+                    roots[j, k][:], total[j][:, halves[k]], ACT.Abs_reciprocal_sqrt, scale=g_inv[:, j : j + 1]
                 )
+            else:
+                nc.scalar.activation(roots[j, k][:], turned[j, k][:], ACT.Abs_reciprocal_sqrt)
 
-        def ratio(woven, b, c0, c1):
-            nc.vector.tensor_tensor(
+        backs = {}
+
+        def turn_back(j, k, number):
+            backs[j, k] = bank(f"back{j}_{k}", widths[k], number)
+            for c in range(0, widths[k], P):
+                nc.tensor.transpose(backs[j, k][:, c : c + P], roots[j, k][:, c : c + P], ident[:])
+
+        def square(j, k):
+            into = inverse0[k][:, j, :] if j < PACK else inverse1[:, j - PACK, halves[k]]
+            if j < SUMS_BY_GPSIMD:
+                nc.scalar.activation(into, roots[j, k][:], ACT.Square)
+            else:
+                nc.scalar.activation(into, backs[j, k][:], ACT.Square, scale=g_root[:, j : j + 1])
+
+        def ratio(engine, woven, diff, inverse):
+            engine.tensor_tensor(
                 woven.rearrange("p (c i t) -> p c t i", i=4, t=PACK),
-                diff[b][:, :, c0:c1].rearrange("p t (c i) -> p c t i", i=4),
-                total[b][:, :, c0:c1].rearrange("p t (c i) -> p c t i", i=4),
+                diff.rearrange("p t (c i) -> p c t i", i=4),
+                inverse.rearrange("p t (c i) -> p c t i", i=4),
                 ALU.mult,
             )
 
-        def weave(copy, woven, zrow, c0, c1):
-            copy(
-                woven[:, PACK * c0 : PACK * c1].rearrange("p (c i t) -> p c t i", i=4, t=PACK),
-                zrow[:, :, c0:c1].rearrange("p t (c i) -> p c t i", i=4),
-            )
+        sum_banks = {}
+        for j in range(2, SLICES):
+            sum_banks[j, 0], sum_banks[j, 1] = ((2, 3), (4, 5))[j % 2] if j < PACK else ((2, 4), (3, 5))[j % 2]
+        for j in range(PACK):
+            pick(j, j == PACK - 1)
+            if j < SUMS_BY_GPSIMD:
+                total[j] = early[j - 1] if j else place("total0", PAIRS, F32, at_w2[1] + 4 * (PACK * N - PAIRS))[:]
+                nc.gpsimd.tensor_tensor(total[j], late[j], early[j], ALU.add)
+            else:
+                for k in range(2):
+                    turn(j, k, sum_banks[j, k], (early[j], late[j]))
+            nc.gpsimd.tensor_tensor(diff0[:, j, :], late[j], early[j], ALU.subtract)
 
-        FIRST = 512
-        woven0 = [
-            keep.tile([P, FIRST * PACK], BF16, name="woven0a", tag="h7", align_bytes=64),
-        ]
-        w2c = [
-            keep.tile([P, N], U32, name="w2c0", tag="root6", align_bytes=64),
-            keep.tile([P, N], U32, name="w2c1", tag="h5", align_bytes=64),
-        ]
-        w2s = [keep.tile([P, N], U8, name=f"w2s{b}", align_bytes=64) for b in range(PASSES)]
-        zc = [keep.tile([P, PAIRS], U32, name=f"zc{b}", align_bytes=64) for b in range(PASSES)]
-        zs = [keep.tile([P, PAIRS], U8, name=f"zs{b}", align_bytes=64) for b in range(PASSES)]
+        g_root = place("g_root", SLICES, F32, at_zero)
+        nc.scalar.activation(g_root[:], g_inv[:], ACT.Abs_reciprocal_sqrt)
+        for j in range(PACK):
+            take_root(j, 0, at_roots[j])
+        for j in range(SUMS_BY_GPSIMD, PACK):
+            turn_back(j, 0, sum_banks[j, 0])
+        for j in range(PACK):
+            square(j, 0)
+        woven0 = [place("woven0a", PACK * SPLIT, BF16)]
+        ratio(nc.gpsimd, woven0[0][:], diff0[:, :, halves[0]], inverse0[0])
+
+        for j, at in ((2, at_roots[0]), (3, at_w2b[0]), (0, at_roots[2]), (1, at_roots[3])):
+            take_root(j, 1, at)
+        for j in range(SUMS_BY_GPSIMD, PACK):
+            turn_back(j, 1, sum_banks[j, 1])
+        for j in range(PACK):
+            square(j, 1)
+
+        w2b = []
+        for j in range(PACK, SLICES - 1):
+            pick(j, False)
+            for k in range(2):
+                turn(j, k, sum_banks[j, k], (early[j], late[j]))
+            nc.gpsimd.tensor_tensor(diff1[:, j - PACK, :], late[j], early[j], ALU.subtract)
+            for k in range(2):
+                take_root(j, k, at_w2b[1] if (j, k) == (PACK, 1) else at_roots[2 * (j % 2) + k])
+            if j < PACK + PASSES:
+                for k in range(2):
+                    turn_back(j, k, sum_banks[j, k])
+                w2b.append(weave_w2(j - PACK))
+                for k in range(2):
+                    square(j, k)
+        last = SLICES - 1
+        early[last] = rows[:, early_row[last], :]
+        nc.vector.tensor_copy(early[last], h[last][:].indirect(pos2_t[:]))
+        for k in range(2):
+            nc.vector.tensor_tensor(
+                diff1[:, PACK - 1, halves[k]],
+                h[last][:].indirect(pos1_t[:, entries_of(k)]),
+                early[last][:, halves[k]],
+                ALU.subtract,
+            )
+            turn(last, k, sum_banks[last, k], (early[last], early[last], diff1[:, PACK - 1, :]))
+        for k in range(2):
+            take_root(last, k, at_roots[2 + k])
+        for k in range(2):
+            for j in (last - 1, last):
+                turn_back(j, k, (6 + 2 * k + j - (last - 1)) % BANKS)
+        for k in range(2):
+            for j in (last - 1, last):
+                square(j, k)
+
+        w2c = [place(f"w2c{b}", N, U32) for b in range(PASSES)]
+        w2s = [place(f"w2s{b}", N, U8, at_h[last] + N * b) for b in range(PASSES)]
+        zc = [place(f"zc{b}", PAIRS, U32) for b in range(PASSES)]
+        zs = [place("zs0", PAIRS, U8, at_h[last] + 2 * N), place("zs1", PAIRS, U8)]
+        woven0.append(place("woven0b", PACK * widths[1], BF16, at_h[last] + 4 * N))
 
         def quantise_z(woven, b, c0, c1):
             nc.vector.quantize_mx(out=zc[b][:, c0:c1].bitcast(FP8X4), scales=zs[b][:, c0:c1], in_=woven)
 
-        yc = keep.tile([P, PAIRS], U32, name="yc", align_bytes=64)
-        ys = keep.tile([P, PAIRS], U8, name="ys", align_bytes=64)
+        yc = place("yc", PAIRS, U32)
+        ys = place("ys", PAIRS, U8)
         out_rows = out_0.rearrange("(p t) q -> p t q", t=PACK)
         out_words = out_1[0].rearrange("p m t -> p (m t)").bitcast(I32)
-        yacc = [psum.tile([P, PACK, Y_COLS], F32, name=f"yacc{s}", tag=f"bank{(0, 1, 2, 6, 4, 3)[s]}") for s in range(PAIRS // Y_COLS)]
+        y_banks = (5, 6, 7, 0, 1, 5)
+        yacc = {}
 
         def mix(b, c0, c1):
             for s0 in range(c0, c1, Y_COLS):
                 cols = slice(s0, s0 + Y_COLS)
+                if b == 0:
+                    yacc[s0] = bank(f"yacc{s0}", BANK, y_banks[s0 // Y_COLS])[:].rearrange("p (t n) -> p t n", t=PACK)
                 for t in range(PACK):
                     nc.tensor.matmul_mx(
-                        out=yacc[s0 // Y_COLS][:, t, :],
+                        out=yacc[s0][:, t, :],
                         lhsT=w2c[b][:, P * t : P * (t + 1)].bitcast(FP8X4),
                         lhsT_scale=w2s[b][:, P * t : P * (t + 1)],
                         rhs=zc[b][:, cols].bitcast(FP8X4),
@@ -335,53 +372,49 @@ def tile_list_vegetation_change_indices_kernel(
                         stop=(b == PASSES - 1 and t == PACK - 1),
                     )
 
-        yf = keep.tile([P, PACK, PAIRS], F32, name="yf")
-        yb = keep.tile([P, PAIRS * PACK], BF16, name="yb", align_bytes=64)
+        yf = place("yf", PACK * PAIRS, F32, at_table + 2048)[:].rearrange("p (t c) -> p t c", t=PACK)
+        yb = place("yb", PAIRS * PACK, BF16)
 
         def hand_out(c0, c1, by_vector):
             for s0 in range(c0, c1, Y_COLS):
                 cols = slice(s0, s0 + Y_COLS)
-                acc = yacc[s0 // Y_COLS]
                 if not by_vector:
                     nc.scalar.copy(
                         yb[:, PACK * s0 : PACK * (s0 + Y_COLS)].rearrange("p (n t) -> p n t", t=PACK),
-                        acc[:].rearrange("p t n -> p n t"),
+                        yacc[s0].rearrange("p t n -> p n t"),
                     )
-                nc.scalar.copy(yf[:, :, cols], acc[:])
+                nc.scalar.copy(yf[:, :, cols], yacc[s0])
             (nc.scalar if c1 == PAIRS else nc.sync).dma_start(out_rows[:, :, c0:c1], yf[:, :, c0:c1])
 
         def finish(c0, c1, by_vector):
             if by_vector:
-                weave(nc.vector.tensor_copy, yb, yf, c0, c1)
+                nc.vector.tensor_copy(
+                    yb[:, PACK * c0 : PACK * c1].rearrange("p (c i t) -> p c t i", i=4, t=PACK),
+                    yf[:, :, c0:c1].rearrange("p t (c i) -> p c t i", i=4),
+                )
             nc.vector.quantize_mx(
                 out=yc[:, c0:c1].bitcast(FP8X4), scales=ys[:, c0:c1], in_=yb[:, PACK * c0 : PACK * c1]
             )
 
-        ratio(woven0[0][:], 0, 0, FIRST)
-        nc.vector.quantize_mx(out=w2c[1][:].bitcast(FP8X4), scales=w2s[1][:], in_=w2b[1][:])
-        quantise_z(woven0[0][:], 0, 0, FIRST)
         nc.vector.quantize_mx(out=w2c[0][:].bitcast(FP8X4), scales=w2s[0][:], in_=w2b[0][:])
+        ratio(nc.vector, woven0[1][:], diff0[:, :, halves[1]], inverse0[1])
+        quantise_z(woven0[0][:], 0, 0, SPLIT)
+        nc.vector.quantize_mx(out=w2c[1][:].bitcast(FP8X4), scales=w2s[1][:], in_=w2b[1][:])
+        quantise_z(woven0[1][:], 0, SPLIT, PAIRS)
         woven1 = {}
         runs = [(0, 128), (128, 256), (256, 512), (512, 640), (640, 768)]
         by_vector = (2, 3, 4)
         for n in range(len(runs) + 1):
             if n < len(runs):
                 c0, c1 = runs[n]
-                woven1[n] = keep.tile([P, (c1 - c0) * PACK], BF16, name=f"woven1_{n}", tag=f"woven1_{n}", align_bytes=64)
-                ratio(woven1[n][:], 1, c0, c1)
-            if 0 <= n - 1 < len(runs):
+                woven1[n] = place(f"woven1_{n}", (c1 - c0) * PACK, BF16)
+                ratio(nc.vector, woven1[n][:], diff1[:, :, c0:c1], inverse1[:, :, c0:c1])
+            if n > 0:
                 c0, c1 = runs[n - 1]
                 quantise_z(woven1[n - 1][:], 1, c0, c1)
                 mix(0, c0, c1)
                 mix(1, c0, c1)
                 hand_out(c0, c1, n - 1 in by_vector)
-            if n == 2:
-                woven0.append(
-                    keep.tile([P, (PAIRS - FIRST) * PACK], BF16, name="woven0b", tag="woven1_1", align_bytes=64)
-                )
-                ratio(woven0[1][:], 0, FIRST, PAIRS)
-            if n == 3:
-                quantise_z(woven0[1][:], 0, FIRST, PAIRS)
         finish(0, 256, False)
         finish(256, 512, True)
         finish(512, 640, True)

@@ -26,9 +26,10 @@ BANK = 512
 BANKS = 8
 Y_COLS = 128
 SPLIT = 256
-PARTS = ((0, SPLIT), (SPLIT, PAIRS))
+PARTS = ((PAIRS - SPLIT, PAIRS), (0, PAIRS - SPLIT))
 WIDEST = max(SPLIT, PAIRS - SPLIT)
-SUMS_BY_GPSIMD = 2
+SUMS_BY_GPSIMD = 1
+DEALT_FIRST = 1
 EARLY = 512
 
 
@@ -58,7 +59,7 @@ def tile_list_vegetation_change_indices_kernel(
         at_w2_late = room(4 * PACK * N)
         at_gain = room(64)
         at_w2 = [room(4 * PACK * N), at_w2_late]
-        at_w1_rest = room(2 * P * (SLICES - 1))
+        at_w1_rest = room(2 * P * (SLICES - DEALT_FIRST))
         at_h = [room(4 * S) for j in range(SLICES)]
         at_roots = [room(4 * WIDEST) for j in range(4)]
         at_w2b = [room(2 * PACK * N) for b in range(PASSES)]
@@ -112,8 +113,8 @@ def tile_list_vegetation_change_indices_kernel(
             w1s_dealt[:].rearrange("p (b t m) -> p b t m", b=PASSES, t=PACK),
             w1s_raw[:].rearrange("p (b m t) -> p b t m", b=PASSES, t=PACK),
         )
-        w1w_first = place("w1w_first", 2 * P, U8)
-        deal_w1(w1w_first[:], 0, 1)
+        w1w_first = place("w1w_first", 2 * P * DEALT_FIRST, U8)
+        deal_w1(w1w_first[:], 0, DEALT_FIRST)
         for q in range(4):
             (nc.gpsimd if q < 2 else nc.sync).dma_start(
                 w1s[32 * q : 32 * q + 4, :].bitcast(I32), w1s_dealt[32 * q : 32 * (q + 1) : 8, :].bitcast(I32)
@@ -124,7 +125,7 @@ def tile_list_vegetation_change_indices_kernel(
 
         spread = {}
         for c0, c1 in ((0, 2 * BANK), (2 * BANK, S)):
-            spread[c0] = place(f"vs_spread{c0}", c1 - c0, U8, at_w1_rest + 2 * P * (PACK - 2) if c1 == S else None)
+            spread[c0] = place(f"vs_spread{c0}", c1 - c0, U8, at_w1_rest + 2 * P * (PACK - DEALT_FIRST - 1) if c1 == S else None)
             nc.vector.tensor_copy(spread[c0][:], tabs[:].indirect(offs_t[:, c0 // 16 : c1 // 16]))
 
         def place_scales(c0, c1):
@@ -159,9 +160,9 @@ def tile_list_vegetation_change_indices_kernel(
         g_inv = place("g_inv", SLICES, F32)
         nc.gpsimd.tensor_scalar(g_pos[:], g_t[:], 0.0, 2.0, ALU.is_ge, ALU.mult)
         nc.gpsimd.tensor_scalar(g_sign[:], g_pos[:], 1.0, -1.0, ALU.mult, ALU.add)
-        w1w_rest = place("w1w_rest", 2 * P * (SLICES - 1), U8, at_w1_rest)
-        deal_w1(w1w_rest[:, : 2 * P * (PACK - 1)], 1, PACK)
-        deal_w1(w1w_rest[:, 2 * P * (PACK - 1) :], PACK, SLICES)
+        w1w_rest = place("w1w_rest", 2 * P * (SLICES - DEALT_FIRST), U8, at_w1_rest)
+        deal_w1(w1w_rest[:, : 2 * P * (PACK - DEALT_FIRST)], DEALT_FIRST, PACK)
+        deal_w1(w1w_rest[:, 2 * P * (PACK - DEALT_FIRST) :], PACK, SLICES)
         nc.vector.reciprocal(g_inv[:], g_t[:])
 
         h = [place(f"h{j}", S, F32, at_h[j]) for j in range(SLICES)]
@@ -170,9 +171,10 @@ def tile_list_vegetation_change_indices_kernel(
             for c in range(S // BANK):
                 cuts = (0, 256, 384, BANK) if (j, c) == (0, S // BANK - 1) else (0, BANK)
                 pieces.extend((j, c, lo, hi) for lo, hi in zip(cuts, cuts[1:]))
+        first_banks = [n % BANKS for n in range(22)] + [0, 1, 2, 3]
         for n, (j, c, lo, hi) in enumerate(pieces):
             cols = slice(BANK * c + lo, BANK * c + hi)
-            acc = bank(f"acc{n}", hi - lo, n % BANKS)
+            acc = bank(f"acc{n}", hi - lo, first_banks[n])
             nc.tensor.matmul_mx(
                 out=acc[:],
                 lhsT=w1w[j].bitcast(FP4X4),
@@ -207,13 +209,15 @@ def tile_list_vegetation_change_indices_kernel(
 
         halves = [slice(c0, c1) for c0, c1 in PARTS]
         widths = [c1 - c0 for c0, c1 in PARTS]
-        work = place("work", 17 * PAIRS, F32)
+        work = place("work", 16 * PAIRS, F32)
         rows = work[:].rearrange("p (r c) -> p r c", c=PAIRS)
-        diff0, diff1 = rows[:, 1:8:2, :], rows[:, 9:16:2, :]
-        early_row = (0, 5, 7, 4, 11, 13, 15, 16)
-        late_row = (1, 3, 2, 6, 10, 12, 14)
+        diff0 = rows[:, 1:8:2, :]
+        shifted = work[:, 2 * PAIRS - SPLIT : 10 * PAIRS - SPLIT].rearrange("p (t c) -> p t c", t=PACK)
+        diff1 = shifted[:, :, :PAIRS]
+        early_row = (3, 5, 7, 4, 9, 11, 13, 15)
+        late_row = (1, 0, 2, 6, 10, 12, 14)
         inverse0 = [
-            work[:, 10 * PAIRS - PACK * SPLIT : 10 * PAIRS].rearrange("p (t c) -> p t c", t=PACK),
+            place("inverse0a", PACK * SPLIT, F32)[:].rearrange("p (t c) -> p t c", t=PACK),
             place("inverse0b", PACK * widths[1], F32)[:].rearrange("p (t c) -> p t c", t=PACK),
         ]
         inverse1 = place("inverse1", PACK * PAIRS, F32)[:].rearrange("p (t c) -> p t c", t=PACK)
@@ -222,11 +226,11 @@ def tile_list_vegetation_change_indices_kernel(
         def entries_of(k):
             return slice(PARTS[k][0] // 16, PARTS[k][1] // 16)
 
-        def pick(j, split):
+        def pick(j, order):
             early[j], late[j] = rows[:, early_row[j], :], rows[:, late_row[j], :]
             nc.vector.tensor_copy(early[j], h[j][:].indirect(pos2_t[:]))
-            if split:
-                for k in range(2):
+            if order:
+                for k in order:
                     nc.vector.tensor_copy(late[j][:, halves[k]], h[j][:].indirect(pos1_t[:, entries_of(k)]))
             else:
                 nc.vector.tensor_copy(late[j], h[j][:].indirect(pos1_t[:]))
@@ -275,16 +279,19 @@ def tile_list_vegetation_change_indices_kernel(
                 ALU.mult,
             )
 
-        sum_banks = {}
-        for j in range(2, SLICES):
-            sum_banks[j, 0], sum_banks[j, 1] = ((2, 3), (4, 5))[j % 2] if j < PACK else ((2, 4), (3, 5))[j % 2]
+        sum_banks = {(1, 0): 6, (1, 1): 7, (2, 0): 4, (2, 1): 5, (3, 0): 0, (3, 1): 0}
+        back_banks = dict(sum_banks)
+        back_banks[3, 0], back_banks[3, 1] = 1, 2
+        for j in range(PACK, SLICES):
+            sum_banks[j, 1], sum_banks[j, 0] = ((0, 7), (7, 0))[j % 2]
+            back_banks[j, 1], back_banks[j, 0] = sum_banks[j, 1], 4
         for j in range(PACK):
-            pick(j, j == PACK - 1)
+            pick(j, (0, 1) if j == PACK - 1 else ())
             if j < SUMS_BY_GPSIMD:
-                total[j] = early[j - 1] if j else place("total0", PAIRS, F32, at_w2[1] + 4 * (PACK * N - PAIRS))[:]
+                total[j] = place("total0", PAIRS, F32, at_w2[1] + 4 * (PACK * N - PAIRS))[:]
                 nc.gpsimd.tensor_tensor(total[j], late[j], early[j], ALU.add)
             else:
-                for k in range(2):
+                for k in range(1 if j == PACK - 1 else 2):
                     turn(j, k, sum_banks[j, k], (early[j], late[j]))
             nc.gpsimd.tensor_tensor(diff0[:, j, :], late[j], early[j], ALU.subtract)
 
@@ -293,52 +300,49 @@ def tile_list_vegetation_change_indices_kernel(
         for j in range(PACK):
             take_root(j, 0, at_roots[j])
         for j in range(SUMS_BY_GPSIMD, PACK):
-            turn_back(j, 0, sum_banks[j, 0])
+            turn_back(j, 0, back_banks[j, 0])
+        turn(PACK - 1, 1, sum_banks[PACK - 1, 1], (early[PACK - 1], late[PACK - 1]))
         for j in range(PACK):
             square(j, 0)
         woven0 = [place("woven0a", PACK * SPLIT, BF16)]
         ratio(nc.gpsimd, woven0[0][:], diff0[:, :, halves[0]], inverse0[0])
 
-        for j, at in ((2, at_roots[0]), (3, at_w2b[0]), (0, at_roots[2]), (1, at_roots[3])):
+        for j, at in ((1, at_roots[0]), (2, at_roots[1]), (3, at_w2b[0]), (0, at_roots[2])):
             take_root(j, 1, at)
         for j in range(SUMS_BY_GPSIMD, PACK):
-            turn_back(j, 1, sum_banks[j, 1])
+            turn_back(j, 1, back_banks[j, 1])
         for j in range(PACK):
             square(j, 1)
 
         w2b = []
-        for j in range(PACK, SLICES - 1):
-            pick(j, False)
-            for k in range(2):
-                turn(j, k, sum_banks[j, k], (early[j], late[j]))
-            nc.gpsimd.tensor_tensor(diff1[:, j - PACK, :], late[j], early[j], ALU.subtract)
-            for k in range(2):
-                take_root(j, k, at_w2b[1] if (j, k) == (PACK, 1) else at_roots[2 * (j % 2) + k])
-            if j < PACK + PASSES:
-                for k in range(2):
-                    turn_back(j, k, sum_banks[j, k])
-                w2b.append(weave_w2(j - PACK))
-                for k in range(2):
-                    square(j, k)
         last = SLICES - 1
-        early[last] = rows[:, early_row[last], :]
-        nc.vector.tensor_copy(early[last], h[last][:].indirect(pos2_t[:]))
-        for k in range(2):
-            nc.vector.tensor_tensor(
-                diff1[:, PACK - 1, halves[k]],
-                h[last][:].indirect(pos1_t[:, entries_of(k)]),
-                early[last][:, halves[k]],
-                ALU.subtract,
-            )
-            turn(last, k, sum_banks[last, k], (early[last], early[last], diff1[:, PACK - 1, :]))
-        for k in range(2):
-            take_root(last, k, at_roots[2 + k])
-        for k in range(2):
-            for j in (last - 1, last):
-                turn_back(j, k, (6 + 2 * k + j - (last - 1)) % BANKS)
-        for k in range(2):
-            for j in (last - 1, last):
+        wide_first = (1, 0)
+        for j in range(PACK, SLICES):
+            if j < last:
+                pick(j, ())
+                nc.gpsimd.tensor_tensor(diff1[:, j - PACK, :], late[j], early[j], ALU.subtract)
+                terms = (early[j], late[j])
+            else:
+                early[j] = rows[:, early_row[j], :]
+                nc.vector.tensor_copy(early[j], h[j][:].indirect(pos2_t[:]))
+                for k in wide_first:
+                    nc.vector.tensor_tensor(
+                        diff1[:, j - PACK, halves[k]],
+                        h[j][:].indirect(pos1_t[:, entries_of(k)]),
+                        early[j][:, halves[k]],
+                        ALU.subtract,
+                    )
+                terms = (early[j], early[j], diff1[:, j - PACK, :])
+            for k in wide_first:
+                turn(j, k, sum_banks[j, k], terms)
+            for k in wide_first:
+                take_root(j, k, (at_w2b[1], at_roots[3])[k] if j == PACK else at_roots[2 * (1 - j % 2) + k])
+            for k in wide_first:
+                turn_back(j, k, back_banks[j, k])
+            for k in wide_first:
                 square(j, k)
+            if j < PACK + PASSES:
+                w2b.append(weave_w2(j - PACK))
 
         w2c = [place(f"w2c{b}", N, U32) for b in range(PASSES)]
         w2s = [place(f"w2s{b}", N, U8, at_h[last] + N * b) for b in range(PASSES)]
@@ -353,13 +357,13 @@ def tile_list_vegetation_change_indices_kernel(
         ys = place("ys", PAIRS, U8)
         out_rows = out_0.rearrange("(p t) q -> p t q", t=PACK)
         out_words = out_1[0].rearrange("p m t -> p (m t)").bitcast(I32)
-        y_banks = (5, 6, 7, 0, 1, 5)
+        y_banks = (2, 3, 5, 6, 0, 7)
         yacc = {}
 
-        def mix(b, c0, c1):
+        def mix(b, c0, c1, opens):
             for s0 in range(c0, c1, Y_COLS):
                 cols = slice(s0, s0 + Y_COLS)
-                if b == 0:
+                if opens:
                     yacc[s0] = bank(f"yacc{s0}", BANK, y_banks[s0 // Y_COLS])[:].rearrange("p (t n) -> p t n", t=PACK)
                 for t in range(PACK):
                     nc.tensor.matmul_mx(
@@ -368,8 +372,8 @@ def tile_list_vegetation_change_indices_kernel(
                         lhsT_scale=w2s[b][:, P * t : P * (t + 1)],
                         rhs=zc[b][:, cols].bitcast(FP8X4),
                         rhs_scale=zs[b][:, cols],
-                        start=(b == 0 and t == 0),
-                        stop=(b == PASSES - 1 and t == PACK - 1),
+                        start=(opens and t == 0),
+                        stop=(not opens and t == PACK - 1),
                     )
 
         yf = place("yf", PACK * PAIRS, F32, at_table + 2048)[:].rearrange("p (t c) -> p t c", t=PACK)
@@ -398,9 +402,9 @@ def tile_list_vegetation_change_indices_kernel(
 
         nc.vector.quantize_mx(out=w2c[0][:].bitcast(FP8X4), scales=w2s[0][:], in_=w2b[0][:])
         ratio(nc.vector, woven0[1][:], diff0[:, :, halves[1]], inverse0[1])
-        quantise_z(woven0[0][:], 0, 0, SPLIT)
+        quantise_z(woven0[0][:], 0, *PARTS[0])
         nc.vector.quantize_mx(out=w2c[1][:].bitcast(FP8X4), scales=w2s[1][:], in_=w2b[1][:])
-        quantise_z(woven0[1][:], 0, SPLIT, PAIRS)
+        quantise_z(woven0[1][:], 0, *PARTS[1])
         woven1 = {}
         runs = [(0, 128), (128, 256), (256, 512), (512, 640), (640, 768)]
         by_vector = (2, 3, 4)
@@ -412,8 +416,9 @@ def tile_list_vegetation_change_indices_kernel(
             if n > 0:
                 c0, c1 = runs[n - 1]
                 quantise_z(woven1[n - 1][:], 1, c0, c1)
-                mix(0, c0, c1)
-                mix(1, c0, c1)
+                opener = 1 if c1 <= BANK else 0
+                mix(opener, c0, c1, True)
+                mix(1 - opener, c0, c1, False)
                 hand_out(c0, c1, n - 1 in by_vector)
         finish(0, 256, False)
         finish(256, 512, True)

@@ -31,6 +31,7 @@ WIDEST = max(SPLIT, PAIRS - SPLIT)
 SUMS_BY_GPSIMD = 1
 DEALT_FIRST = 1
 EARLY = 512
+WOVEN_BY_SCALAR = 3
 
 
 def tile_list_vegetation_change_indices_kernel(
@@ -61,7 +62,7 @@ def tile_list_vegetation_change_indices_kernel(
         at_w2 = [room(4 * PACK * N), at_w2_late]
         at_w1_rest = room(2 * P * (SLICES - DEALT_FIRST))
         at_h = [room(4 * S) for j in range(SLICES)]
-        at_roots = [room(4 * WIDEST) for j in range(4)]
+        at_roots = [room(4 * PAIRS)] + [room(4 * WIDEST) for j in range(3)]
         at_w2b = [room(2 * PACK * N) for b in range(PASSES)]
         at_ident = room(H)
         at_zero = room(64)
@@ -285,6 +286,7 @@ def tile_list_vegetation_change_indices_kernel(
         for j in range(PACK, SLICES):
             sum_banks[j, 1], sum_banks[j, 0] = ((0, 7), (7, 0))[j % 2]
             back_banks[j, 1], back_banks[j, 0] = sum_banks[j, 1], 4
+        back_banks[SLICES - 1, 1] = 3
         for j in range(PACK):
             pick(j, (0, 1) if j == PACK - 1 else ())
             if j < SUMS_BY_GPSIMD:
@@ -317,6 +319,8 @@ def tile_list_vegetation_change_indices_kernel(
         w2b = []
         last = SLICES - 1
         wide_first = (1, 0)
+        late_roots = {(j, k): at_roots[2 * (1 - j % 2) + k] for j in range(PACK, SLICES) for k in range(2)}
+        late_roots[last, 0] = at_roots[0] + 2 * SPLIT
         for j in range(PACK, SLICES):
             if j < last:
                 pick(j, ())
@@ -336,7 +340,7 @@ def tile_list_vegetation_change_indices_kernel(
             for k in wide_first:
                 turn(j, k, sum_banks[j, k], terms)
             for k in wide_first:
-                take_root(j, k, (at_w2b[1], at_roots[3])[k] if j == PACK else at_roots[2 * (1 - j % 2) + k])
+                take_root(j, k, (at_w2b[1], at_roots[3])[k] if j == PACK else late_roots[j, k])
             for k in wide_first:
                 turn_back(j, k, back_banks[j, k])
             for k in wide_first:
@@ -346,9 +350,10 @@ def tile_list_vegetation_change_indices_kernel(
 
         w2c = [place(f"w2c{b}", N, U32) for b in range(PASSES)]
         w2s = [place(f"w2s{b}", N, U8, at_h[last] + N * b) for b in range(PASSES)]
-        zc = [place(f"zc{b}", PAIRS, U32) for b in range(PASSES)]
+        zc = [place("zc0", PAIRS, U32, at_roots[0]), place("zc1", PAIRS, U32)]
         zs = [place("zs0", PAIRS, U8, at_h[last] + 2 * N), place("zs1", PAIRS, U8)]
-        woven0.append(place("woven0b", PACK * widths[1], BF16, at_h[last] + 4 * N))
+        woven0.append(place("woven0b", PACK * SPLIT, BF16, at_h[last] + 4 * N))
+        at_woven = room(2 * PACK * SPLIT)
 
         def quantise_z(woven, b, c0, c1):
             nc.vector.quantize_mx(out=zc[b][:, c0:c1].bitcast(FP8X4), scales=zs[b][:, c0:c1], in_=woven)
@@ -357,7 +362,7 @@ def tile_list_vegetation_change_indices_kernel(
         ys = place("ys", PAIRS, U8)
         out_rows = out_0.rearrange("(p t) q -> p t q", t=PACK)
         out_words = out_1[0].rearrange("p m t -> p (m t)").bitcast(I32)
-        y_banks = (2, 3, 5, 6, 0, 7)
+        y_banks = (1, 2, 5, 6, 7, 0)
         yacc = {}
 
         def mix(b, c0, c1, opens):
@@ -400,32 +405,52 @@ def tile_list_vegetation_change_indices_kernel(
                 out=yc[:, c0:c1].bitcast(FP8X4), scales=ys[:, c0:c1], in_=yb[:, PACK * c0 : PACK * c1]
             )
 
-        nc.vector.quantize_mx(out=w2c[0][:].bitcast(FP8X4), scales=w2s[0][:], in_=w2b[0][:])
-        ratio(nc.vector, woven0[1][:], diff0[:, :, halves[1]], inverse0[1])
-        quantise_z(woven0[0][:], 0, *PARTS[0])
-        nc.vector.quantize_mx(out=w2c[1][:].bitcast(FP8X4), scales=w2s[1][:], in_=w2b[1][:])
-        quantise_z(woven0[1][:], 0, *PARTS[1])
+        def first_pass(woven, c0):
+            ratio(
+                nc.vector,
+                woven[:],
+                diff0[:, :, c0 : c0 + SPLIT],
+                inverse0[1][:, :, c0 : c0 + SPLIT],
+            )
+
         woven1 = {}
-        runs = [(0, 128), (128, 256), (256, 512), (512, 640), (640, 768)]
-        by_vector = (2, 3, 4)
-        for n in range(len(runs) + 1):
-            if n < len(runs):
-                c0, c1 = runs[n]
-                woven1[n] = place(f"woven1_{n}", (c1 - c0) * PACK, BF16)
-                ratio(nc.vector, woven1[n][:], diff1[:, :, c0:c1], inverse1[:, :, c0:c1])
-            if n > 0:
-                c0, c1 = runs[n - 1]
-                quantise_z(woven1[n - 1][:], 1, c0, c1)
-                opener = 1 if c1 <= BANK else 0
-                mix(opener, c0, c1, True)
-                mix(1 - opener, c0, c1, False)
-                hand_out(c0, c1, n - 1 in by_vector)
+
+        def second_pass(n):
+            cols = slice(Y_COLS * n, Y_COLS * (n + 1))
+            woven1[n] = place(f"woven1_{n}", Y_COLS * PACK, BF16, at_woven if n == 0 else None)
+            ratio(nc.vector, woven1[n][:], diff1[:, :, cols], inverse1[:, :, cols])
+
+        def close(n):
+            c0, c1 = Y_COLS * n, Y_COLS * (n + 1)
+            quantise_z(woven1[n][:], 1, c0, c1)
+            mix(0, c0, c1, True)
+            mix(1, c0, c1, False)
+            hand_out(c0, c1, n >= WOVEN_BY_SCALAR)
+
+        nc.vector.quantize_mx(out=w2c[0][:].bitcast(FP8X4), scales=w2s[0][:], in_=w2b[0][:])
+        quantise_z(woven0[0][:], 0, *PARTS[0])
+        first_pass(woven0[1], 0)
+        nc.vector.quantize_mx(out=w2c[1][:].bitcast(FP8X4), scales=w2s[1][:], in_=w2b[1][:])
+        quantise_z(woven0[1][:], 0, 0, SPLIT)
+        second_pass(0)
+        second_pass(1)
+        close(0)
+        woven0.append(place("woven0c", PACK * SPLIT, BF16, at_woven))
+        first_pass(woven0[2], SPLIT)
+        close(1)
+        second_pass(2)
+        quantise_z(woven0[2][:], 0, SPLIT, 2 * SPLIT)
+        for n in range(3, PAIRS // Y_COLS):
+            second_pass(n)
+            close(n - 1)
         finish(0, 256, False)
-        finish(256, 512, True)
+        close(PAIRS // Y_COLS - 1)
+        finish(256, 384, False)
+        finish(384, 512, True)
+        nc.sync.dma_start(out_words[:, :512], yc[:, :512].bitcast(I32))
         finish(512, 640, True)
-        nc.sync.dma_start(out_words[:, :640], yc[:, :640].bitcast(I32))
         finish(640, 768, True)
-        nc.sync.dma_start(out_words[:, 640:], yc[:, 640:].bitcast(I32))
+        nc.sync.dma_start(out_words[:, 512:], yc[:, 512:].bitcast(I32))
         for q in range(4):
             (nc.scalar, nc.sync)[q % 2].dma_start(
                 out_2[0, 4 * q : 4 * q + 4, :].bitcast(I32), ys[32 * q : 32 * q + 4, :].bitcast(I32)

@@ -62,7 +62,7 @@ def tile_list_vegetation_change_indices_kernel(
         at_w2 = [room(4 * PACK * N), at_w2_late]
         at_w1_rest = room(2 * P * (SLICES - DEALT_FIRST))
         at_h = [room(4 * S) for j in range(SLICES)]
-        at_roots = [room(4 * PAIRS)] + [room(4 * WIDEST) for j in range(3)]
+        at_roots = [room(4 * PAIRS) for j in range(4)]
         at_w2b = [room(2 * PACK * N) for b in range(PASSES)]
         at_ident = room(H)
         at_zero = room(64)
@@ -272,21 +272,18 @@ def tile_list_vegetation_change_indices_kernel(
             else:
                 nc.scalar.activation(into, backs[j, k][:], ACT.Square, scale=g_root[:, j : j + 1])
 
-        def ratio(engine, woven, diff, inverse):
+        def ratio(engine, woven, diff, inverse, step=4):
             engine.tensor_tensor(
-                woven.rearrange("p (c i t) -> p c t i", i=4, t=PACK),
-                diff.rearrange("p t (c i) -> p c t i", i=4),
-                inverse.rearrange("p t (c i) -> p c t i", i=4),
+                woven.rearrange("p (c i t) -> p c t i", i=step, t=PACK),
+                diff.rearrange("p t (c i) -> p c t i", i=step),
+                inverse.rearrange("p t (c i) -> p c t i", i=step),
                 ALU.mult,
             )
 
         sum_banks = {(1, 0): 6, (1, 1): 7, (2, 0): 4, (2, 1): 5, (3, 0): 0, (3, 1): 0}
+        sum_banks.update({(4, 1): 6, (4, 0): 4, (5, 1): 0, (5, 0): 7, (6, 1): 7, (6, 0): 6, (7, 1): 4, (7, 0): 4})
         back_banks = dict(sum_banks)
-        back_banks[3, 0], back_banks[3, 1] = 1, 2
-        for j in range(PACK, SLICES):
-            sum_banks[j, 1], sum_banks[j, 0] = ((0, 7), (7, 0))[j % 2]
-            back_banks[j, 1], back_banks[j, 0] = sum_banks[j, 1], 4
-        back_banks[SLICES - 1, 1] = 3
+        back_banks.update({(3, 0): 1, (3, 1): 2, (5, 0): 3, (7, 1): 5})
         for j in range(PACK):
             pick(j, (0, 1) if j == PACK - 1 else ())
             if j < SUMS_BY_GPSIMD:
@@ -307,50 +304,67 @@ def tile_list_vegetation_change_indices_kernel(
         for j in range(PACK):
             square(j, 0)
         woven0 = [place("woven0a", PACK * SPLIT, BF16)]
-        ratio(nc.gpsimd, woven0[0][:], diff0[:, :, halves[0]], inverse0[0])
+        ratio(nc.gpsimd, woven0[0][:], diff0[:, :, halves[0]], inverse0[0], 2)
 
-        for j, at in ((1, at_roots[0]), (2, at_roots[1]), (3, at_w2b[0]), (0, at_roots[2])):
-            take_root(j, 1, at)
+        last = SLICES - 1
+        wide_first = (1, 0)
+
+        def pick_late(j):
+            pick(j, ())
+            nc.gpsimd.tensor_tensor(diff1[:, j - PACK, :], late[j], early[j], ALU.subtract)
+
+        pick_late(4)
+        for k in wide_first:
+            turn(4, k, sum_banks[4, k], (early[4], late[4]))
+        for i, j in enumerate((1, 2, 3, 0)):
+            take_root(j, 1, at_roots[i])
         for j in range(SUMS_BY_GPSIMD, PACK):
             turn_back(j, 1, back_banks[j, 1])
         for j in range(PACK):
             square(j, 1)
 
-        w2b = []
-        last = SLICES - 1
-        wide_first = (1, 0)
-        late_roots = {(j, k): at_roots[2 * (1 - j % 2) + k] for j in range(PACK, SLICES) for k in range(2)}
-        late_roots[last, 0] = at_roots[0] + 2 * SPLIT
-        for j in range(PACK, SLICES):
-            if j < last:
-                pick(j, ())
-                nc.gpsimd.tensor_tensor(diff1[:, j - PACK, :], late[j], early[j], ALU.subtract)
-                terms = (early[j], late[j])
-            else:
-                early[j] = rows[:, early_row[j], :]
-                nc.vector.tensor_copy(early[j], h[j][:].indirect(pos2_t[:]))
-                for k in wide_first:
-                    nc.vector.tensor_tensor(
-                        diff1[:, j - PACK, halves[k]],
-                        h[j][:].indirect(pos1_t[:, entries_of(k)]),
-                        early[j][:, halves[k]],
-                        ALU.subtract,
-                    )
-                terms = (early[j], early[j], diff1[:, j - PACK, :])
+        pick_late(5)
+        for k in wide_first:
+            turn(5, k, sum_banks[5, k], (early[5], late[5]))
+        for j in (4, 5):
             for k in wide_first:
-                turn(j, k, sum_banks[j, k], terms)
-            for k in wide_first:
-                take_root(j, k, (at_w2b[1], at_roots[3])[k] if j == PACK else late_roots[j, k])
-            for k in wide_first:
+                take_root(j, k, at_w2b[k] if j == 5 else at_roots[1 - k])
                 turn_back(j, k, back_banks[j, k])
+        for j in (4, 5):
             for k in wide_first:
                 square(j, k)
-            if j < PACK + PASSES:
-                w2b.append(weave_w2(j - PACK))
+        w2b = [weave_w2(0)]
+
+        pick_late(6)
+        for k in wide_first:
+            turn(6, k, sum_banks[6, k], (early[6], late[6]))
+        early[last] = rows[:, early_row[last], :]
+        nc.vector.tensor_copy(early[last], h[last][:].indirect(pos2_t[:]))
+        for k in wide_first:
+            nc.vector.tensor_tensor(
+                diff1[:, last - PACK, halves[k]],
+                h[last][:].indirect(pos1_t[:, entries_of(k)]),
+                early[last][:, halves[k]],
+                ALU.subtract,
+            )
+        terms = (early[last], early[last], diff1[:, last - PACK, :])
+        turn(last, 1, sum_banks[last, 1], terms)
+        for j, k in ((6, 1), (6, 0), (last, 1)):
+            if j == last:
+                w2b.append(weave_w2(1))
+            take_root(j, k, at_roots[2 * (j % 2) + 1 - k])
+            turn_back(j, k, back_banks[j, k])
+        turn(last, 0, sum_banks[last, 0], terms)
+        square(6, 1)
+        square(last, 1)
+        take_root(last, 0, at_roots[3])
+        turn_back(last, 0, back_banks[last, 0])
+        square(6, 0)
+        square(last, 0)
 
         w2c = [place(f"w2c{b}", N, U32) for b in range(PASSES)]
         w2s = [place(f"w2s{b}", N, U8, at_h[last] + N * b) for b in range(PASSES)]
-        zc = [place("zc0", PAIRS, U32, at_roots[0]), place("zc1", PAIRS, U32)]
+        zc = [place("zc0", PAIRS, U32, at_roots[2]), place("zc1", PAIRS, U32)]
         zs = [place("zs0", PAIRS, U8, at_h[last] + 2 * N), place("zs1", PAIRS, U8)]
         woven0.append(place("woven0b", PACK * SPLIT, BF16, at_h[last] + 4 * N))
         at_woven = room(2 * PACK * SPLIT)
@@ -362,7 +376,7 @@ def tile_list_vegetation_change_indices_kernel(
         ys = place("ys", PAIRS, U8)
         out_rows = out_0.rearrange("(p t) q -> p t q", t=PACK)
         out_words = out_1[0].rearrange("p m t -> p (m t)").bitcast(I32)
-        y_banks = (1, 2, 5, 6, 7, 0)
+        y_banks = (0, 1, 2, 3, 7, 5)
         yacc = {}
 
         def mix(b, c0, c1, opens):

@@ -29,7 +29,7 @@ SPLIT = 256
 PARTS = ((PAIRS - SPLIT, PAIRS), (0, PAIRS - SPLIT))
 WIDEST = max(SPLIT, PAIRS - SPLIT)
 SUMS_BY_GPSIMD = 1
-DEALT_FIRST = 1
+DEALT_FIRST = 3
 EARLY = 512
 WOVEN_BY_SCALAR = 3
 
@@ -64,27 +64,21 @@ def tile_list_vegetation_change_indices_kernel(
         at_h = [room(4 * S) for j in range(SLICES)]
         at_roots = [room(4 * PAIRS) for j in range(4)]
         at_w2b = [room(2 * PACK * N) for b in range(PASSES)]
+        at_last_words = room(4 * BANK)
         at_ident = room(H)
-        at_zero = room(64)
 
         offs_t = lists.tile([P, S // 16], U16, name="offs_t")
         pos1_t = lists.tile([P, PAIRS // 16], U16, name="pos1_t")
         pos2_t = lists.tile([P, PAIRS // 16], U16, name="pos2_t")
         tabs = place("tabs", T, U8, at_gain - T // 2)
-        zero = place("zero", 1, F32, at_zero)
-        one = place("one", 1, F32, at_roots[0])
         tabw = place("tabw", T, I32, at_table)
         zeros = tabw[:, T - 8 :]
         w1s_raw = place("w1s_raw", H, U8, at_ident)
-        w1s = place("w1s", H, U8)
         vs = place("vs", S, U8)
         nc.gpsimd.memset(w1s_raw[:].bitcast(I32), 0)
         nc.vector.memset(zeros, 0)
         nc.vector.memset(tabs[:].bitcast(I32), 0)
         nc.vector.tensor_copy(vs[:, :32].bitcast(I32), zeros)
-        nc.vector.memset(zero[:], 0.0)
-        nc.vector.memset(one[:], 1.0)
-        nc.vector.memset(w1s[:].bitcast(I32), 0)
         nc.vector.memset(vs[:, 32:].bitcast(I32), 0)
         nc.sync.dma_start(offs_t[:], offs)
         tab_rows = tab_words[0].rearrange("p t i -> p (t i)").bitcast(I32)
@@ -109,49 +103,47 @@ def tile_list_vegetation_change_indices_kernel(
             for j in range(j0, j1):
                 w1w[j] = tile[:, 2 * P * (j - j0) : 2 * P * (j - j0 + 1)]
 
-        w1s_dealt = place("w1s_dealt", H, U8)
+        w1s = place("w1s", H, U8)
         nc.vector.tensor_copy(
-            w1s_dealt[:].rearrange("p (b t m) -> p b t m", b=PASSES, t=PACK),
+            w1s[:].rearrange("p (b t m) -> p b t m", b=PASSES, t=PACK),
             w1s_raw[:].rearrange("p (b m t) -> p b t m", b=PASSES, t=PACK),
         )
         w1w_first = place("w1w_first", 2 * P * DEALT_FIRST, U8)
         deal_w1(w1w_first[:], 0, DEALT_FIRST)
-        for q in range(4):
-            (nc.gpsimd if q < 2 else nc.sync).dma_start(
-                w1s[32 * q : 32 * q + 4, :].bitcast(I32), w1s_dealt[32 * q : 32 * (q + 1) : 8, :].bitcast(I32)
-            )
+        for r in range(1, 4):
+            (nc.gpsimd if r == 1 else nc.scalar).dma_start(w1s[r:P:32, :].bitcast(I32), w1s[8 * r : P : 32, :].bitcast(I32))
 
         ident = place("ident", P, F32, at_ident)
         make_identity(nc, ident[:])
 
         spread = {}
-        for c0, c1 in ((0, 2 * BANK), (2 * BANK, S)):
+        for c0, c1 in ((0, BANK), (BANK, S)):
             spread[c0] = place(f"vs_spread{c0}", c1 - c0, U8, at_w1_rest + 2 * P * (PACK - DEALT_FIRST - 1) if c1 == S else None)
             nc.vector.tensor_copy(spread[c0][:], tabs[:].indirect(offs_t[:, c0 // 16 : c1 // 16]))
 
         def place_scales(c0, c1):
             for q in range(4):
-                nc.sync.dma_start(
+                (nc.scalar if c0 == 0 else nc.sync).dma_start(
                     vs[32 * q : 32 * q + 4, c0:c1].bitcast(I32),
                     spread[c0][32 * q : 32 * (q + 1) : 8, :].bitcast(I32),
                 )
 
         g_t = place("g_t", SLICES, F32, at_gain)
         w2_raw = [place(f"w2_raw{b}", PACK * N, F32, at_w2[b]) for b in range(PASSES)]
-        place_scales(0, 2 * BANK)
+        place_scales(0, BANK)
         nc.sync.dma_start(
             g_t[:].rearrange("p (b t) -> p b t", b=PASSES), g.rearrange("(b p t) -> p b t", b=PASSES, t=PACK)
         )
         nc.sync.dma_start(w2_raw[0][:, :N], w2_rows[0][:, :N])
-        place_scales(2 * BANK, S)
+        place_scales(BANK, S)
         for c0, c1 in ((N, 2 * N), (2 * N, PACK * N)):
             nc.sync.dma_start(w2_raw[0][:, c0:c1], w2_rows[0][:, c0:c1])
         for c0, c1 in ((0, 2 * N), (2 * N, PACK * N)):
             nc.sync.dma_start(w2_raw[1][:, c0:c1], w2_rows[1][:, c0:c1])
         vw = []
         for c in range(S // BANK):
-            vw.append(place(f"vw{c}", BANK, U32))
-            width = BANK // 2 if c == S // BANK - 1 else BANK
+            vw.append(place(f"vw{c}", BANK, U32, (None, at_roots[0], at_last_words)[c]))
+            width = BANK if c == 1 else BANK // 2
             for lo in range(0, BANK, width):
                 entries = slice((BANK * c + lo) // 16, (BANK * c + lo + width) // 16)
                 nc.vector.tensor_copy(vw[c][:, lo : lo + width], tabw[:].bitcast(U32).indirect(offs_t[:, entries]))
@@ -167,12 +159,12 @@ def tile_list_vegetation_change_indices_kernel(
         nc.vector.reciprocal(g_inv[:], g_t[:])
 
         h = [place(f"h{j}", S, F32, at_h[j]) for j in range(SLICES)]
-        pieces = []
-        for j in range(SLICES):
-            for c in range(S // BANK):
-                cuts = (0, 256, 384, BANK) if (j, c) == (0, S // BANK - 1) else (0, BANK)
-                pieces.extend((j, c, lo, hi) for lo, hi in zip(cuts, cuts[1:]))
-        first_banks = [n % BANKS for n in range(22)] + [0, 1, 2, 3]
+        mid = BANK // 2
+        pieces = [(0, 0, 0, mid), (1, 0, 0, mid), (0, 0, mid, BANK), (1, 0, mid, BANK), (2, 0, 0, mid), (0, 1, 0, BANK)]
+        pieces.extend([(0, 2, 0, mid), (0, 2, mid, 384), (0, 2, 384, BANK)])
+        pieces.extend([(2, 0, mid, BANK), (1, 1, 0, BANK), (1, 2, 0, BANK), (2, 1, 0, BANK), (2, 2, 0, BANK)])
+        pieces.extend((j, c, 0, BANK) for j in range(DEALT_FIRST, SLICES) for c in range(S // BANK))
+        first_banks = [0, 1, 2, 3, 4, 5, 6, 7, 0, 6, 7, 1, 0, 2] + [n % BANKS for n in range(11, 22)] + [0, 1, 2, 3]
         for n, (j, c, lo, hi) in enumerate(pieces):
             cols = slice(BANK * c + lo, BANK * c + hi)
             acc = bank(f"acc{n}", hi - lo, first_banks[n])
@@ -185,7 +177,7 @@ def tile_list_vegetation_change_indices_kernel(
                 start=True,
                 stop=True,
             )
-            nc.scalar.activation(h[j][:, cols], acc[:], ACT.Sigmoid, bias=zero[:], scale=one[:])
+            nc.scalar.activation(h[j][:, cols], acc[:], ACT.Sigmoid)
 
         w2_pairs = [place(f"w2_pairs{b}", PACK * N, BF16) for b in range(PASSES)]
         for b in range(PASSES):
@@ -294,7 +286,7 @@ def tile_list_vegetation_change_indices_kernel(
                     turn(j, k, sum_banks[j, k], (early[j], late[j]))
             nc.gpsimd.tensor_tensor(diff0[:, j, :], late[j], early[j], ALU.subtract)
 
-        g_root = place("g_root", SLICES, F32, at_zero)
+        g_root = place("g_root", SLICES, F32, at_last_words)
         nc.scalar.activation(g_root[:], g_inv[:], ACT.Abs_reciprocal_sqrt)
         for j in range(PACK):
             take_root(j, 0, at_roots[j])

@@ -25,13 +25,14 @@ SLICES = H // P
 BANK = 512
 BANKS = 8
 Y_COLS = 128
-SPLIT = 256
-PARTS = ((PAIRS - SPLIT, PAIRS), (0, PAIRS - SPLIT))
+SPLIT = 384
+THIRD = PAIRS // 3
+PARTS = ((PAIRS - SPLIT, PAIRS), (0, PAIRS - SPLIT)) + tuple((c, c + THIRD) for c in range(0, PAIRS, THIRD))
 WIDEST = max(SPLIT, PAIRS - SPLIT)
 SUMS_BY_GPSIMD = 1
 DEALT_FIRST = 3
 EARLY = 512
-WOVEN_BY_SCALAR = 3
+WOVEN_BY_SCALAR = 2
 
 
 def tile_list_vegetation_change_indices_kernel(
@@ -273,9 +274,9 @@ def tile_list_vegetation_change_indices_kernel(
             )
 
         sum_banks = {(1, 0): 6, (1, 1): 7, (2, 0): 4, (2, 1): 5, (3, 0): 0, (3, 1): 0}
-        sum_banks.update({(4, 1): 6, (4, 0): 4, (5, 1): 0, (5, 0): 7, (6, 1): 7, (6, 0): 6, (7, 1): 4, (7, 0): 4})
+        sum_banks.update({(4, 1): 6, (4, 0): 4, (5, 1): 0, (5, 0): 7, (6, 1): 7, (6, 0): 6, (7, 2): 4, (7, 3): 4, (7, 4): 4})
         back_banks = dict(sum_banks)
-        back_banks.update({(3, 0): 1, (3, 1): 2, (5, 0): 3, (7, 1): 5})
+        back_banks.update({(3, 0): 1, (3, 1): 2, (5, 0): 3, (7, 2): 5, (7, 3): 3})
         for j in range(PACK):
             pick(j, (0, 1) if j == PACK - 1 else ())
             if j < SUMS_BY_GPSIMD:
@@ -309,7 +310,7 @@ def tile_list_vegetation_change_indices_kernel(
         for k in wide_first:
             turn(4, k, sum_banks[4, k], (early[4], late[4]))
         for i, j in enumerate((1, 2, 3, 0)):
-            take_root(j, 1, at_roots[i])
+            take_root(j, 1, at_w2b[0] if j == 3 else at_roots[i])
         for j in range(SUMS_BY_GPSIMD, PACK):
             turn_back(j, 1, back_banks[j, 1])
         for j in range(PACK):
@@ -320,19 +321,22 @@ def tile_list_vegetation_change_indices_kernel(
             turn(5, k, sum_banks[5, k], (early[5], late[5]))
         for j in (4, 5):
             for k in wide_first:
-                take_root(j, k, at_w2b[k] if j == 5 else at_roots[1 - k])
+                take_root(j, k, at_w2b[1] if (j, k) == (5, 1) else at_roots[2 * (j % 2) + 1 - k])
                 turn_back(j, k, back_banks[j, k])
+            if j == 4:
+                w2b = [weave_w2(0)]
         for j in (4, 5):
             for k in wide_first:
                 square(j, k)
-        w2b = [weave_w2(0)]
+        w2b.append(weave_w2(1))
 
         pick_late(6)
         for k in wide_first:
             turn(6, k, sum_banks[6, k], (early[6], late[6]))
         early[last] = rows[:, early_row[last], :]
         nc.vector.tensor_copy(early[last], h[last][:].indirect(pos2_t[:]))
-        for k in wide_first:
+        thirds = (2, 3, 4)
+        for k in thirds:
             nc.vector.tensor_tensor(
                 diff1[:, last - PACK, halves[k]],
                 h[last][:].indirect(pos1_t[:, entries_of(k)]),
@@ -340,26 +344,25 @@ def tile_list_vegetation_change_indices_kernel(
                 ALU.subtract,
             )
         terms = (early[last], early[last], diff1[:, last - PACK, :])
-        turn(last, 1, sum_banks[last, 1], terms)
-        for j, k in ((6, 1), (6, 0), (last, 1)):
-            if j == last:
-                w2b.append(weave_w2(1))
-            take_root(j, k, at_roots[2 * (j % 2) + 1 - k])
-            turn_back(j, k, back_banks[j, k])
-        turn(last, 0, sum_banks[last, 0], terms)
-        square(6, 1)
-        square(last, 1)
-        take_root(last, 0, at_roots[3])
-        turn_back(last, 0, back_banks[last, 0])
-        square(6, 0)
-        square(last, 0)
+        turn(last, thirds[0], sum_banks[last, thirds[0]], terms)
+        for k in wide_first:
+            take_root(6, k, at_roots[1 - k])
+            turn_back(6, k, back_banks[6, k])
+        for i, k in enumerate(thirds):
+            take_root(last, k, (at_roots[3], at_roots[2] + 2 * THIRD, at_roots[3])[i])
+            turn_back(last, k, back_banks[last, k])
+            if i < 2:
+                turn(last, thirds[i + 1], sum_banks[last, thirds[i + 1]], terms)
+            if i != 1:
+                square(6, 1 - i // 2)
+            square(last, k)
 
         w2c = [place(f"w2c{b}", N, U32) for b in range(PASSES)]
         w2s = [place(f"w2s{b}", N, U8, at_h[last] + N * b) for b in range(PASSES)]
         zc = [place("zc0", PAIRS, U32, at_roots[2]), place("zc1", PAIRS, U32)]
         zs = [place("zs0", PAIRS, U8, at_h[last] + 2 * N), place("zs1", PAIRS, U8)]
-        woven0.append(place("woven0b", PACK * SPLIT, BF16, at_h[last] + 4 * N))
-        at_woven = room(2 * PACK * SPLIT)
+        woven0.append(place("woven0b", PACK * THIRD, BF16, at_h[last] + 4 * N))
+        at_woven = room(2 * PACK * THIRD)
 
         def quantise_z(woven, b, c0, c1):
             nc.vector.quantize_mx(out=zc[b][:, c0:c1].bitcast(FP8X4), scales=zs[b][:, c0:c1], in_=woven)
@@ -411,12 +414,12 @@ def tile_list_vegetation_change_indices_kernel(
                 out=yc[:, c0:c1].bitcast(FP8X4), scales=ys[:, c0:c1], in_=yb[:, PACK * c0 : PACK * c1]
             )
 
-        def first_pass(woven, c0):
+        def first_pass(woven, c0, c1):
             ratio(
                 nc.vector,
                 woven[:],
-                diff0[:, :, c0 : c0 + SPLIT],
-                inverse0[1][:, :, c0 : c0 + SPLIT],
+                diff0[:, :, c0:c1],
+                inverse0[1][:, :, c0:c1],
             )
 
         woven1 = {}
@@ -435,24 +438,23 @@ def tile_list_vegetation_change_indices_kernel(
 
         nc.vector.quantize_mx(out=w2c[0][:].bitcast(FP8X4), scales=w2s[0][:], in_=w2b[0][:])
         quantise_z(woven0[0][:], 0, *PARTS[0])
-        first_pass(woven0[1], 0)
+        first_pass(woven0[1], 0, THIRD)
         nc.vector.quantize_mx(out=w2c[1][:].bitcast(FP8X4), scales=w2s[1][:], in_=w2b[1][:])
-        quantise_z(woven0[1][:], 0, 0, SPLIT)
         second_pass(0)
         second_pass(1)
+        quantise_z(woven0[1][:], 0, 0, THIRD)
         close(0)
-        woven0.append(place("woven0c", PACK * SPLIT, BF16, at_woven))
-        first_pass(woven0[2], SPLIT)
+        woven0.append(place("woven0c", PACK * (PAIRS - SPLIT - THIRD), BF16, at_woven))
+        first_pass(woven0[2], THIRD, PAIRS - SPLIT)
         close(1)
         second_pass(2)
-        quantise_z(woven0[2][:], 0, SPLIT, 2 * SPLIT)
+        quantise_z(woven0[2][:], 0, THIRD, PAIRS - SPLIT)
         for n in range(3, PAIRS // Y_COLS):
             second_pass(n)
             close(n - 1)
         finish(0, 256, False)
         close(PAIRS // Y_COLS - 1)
-        finish(256, 384, False)
-        finish(384, 512, True)
+        finish(256, 512, True)
         nc.sync.dma_start(out_words[:, :512], yc[:, :512].bitcast(I32))
         finish(512, 640, True)
         finish(640, 768, True)

@@ -26,13 +26,11 @@ BANK = 512
 BANKS = 8
 Y_COLS = 128
 SPLIT = 384
-THIRD = PAIRS // 3
-PARTS = ((PAIRS - SPLIT, PAIRS), (0, PAIRS - SPLIT)) + tuple((c, c + THIRD) for c in range(0, PAIRS, THIRD))
+PARTS = ((PAIRS - SPLIT, PAIRS), (0, PAIRS - SPLIT))
 WIDEST = max(SPLIT, PAIRS - SPLIT)
 SUMS_BY_GPSIMD = 1
 DEALT_FIRST = 3
 EARLY = 512
-WOVEN_BY_SCALAR = 2
 
 
 def tile_list_vegetation_change_indices_kernel(
@@ -165,7 +163,7 @@ def tile_list_vegetation_change_indices_kernel(
         pieces.extend([(0, 2, 0, mid), (0, 2, mid, 384), (0, 2, 384, BANK)])
         pieces.extend([(2, 0, mid, BANK), (1, 1, 0, BANK), (1, 2, 0, BANK), (2, 1, 0, BANK), (2, 2, 0, BANK)])
         pieces.extend((j, c, 0, BANK) for j in range(DEALT_FIRST, SLICES) for c in range(S // BANK))
-        first_banks = [0, 1, 2, 3, 4, 5, 6, 7, 0, 6, 7, 1, 0, 2] + [n % BANKS for n in range(11, 22)] + [0, 1, 2, 3]
+        first_banks = [0, 1, 2, 3, 4, 5, 6, 7, 0, 6, 7, 1, 0, 2] + [n % BANKS for n in range(11, 26)]
         for n, (j, c, lo, hi) in enumerate(pieces):
             cols = slice(BANK * c + lo, BANK * c + hi)
             acc = bank(f"acc{n}", hi - lo, first_banks[n])
@@ -244,7 +242,7 @@ def tile_list_vegetation_change_indices_kernel(
 
         def take_root(j, k, at):
             roots[j, k] = place(f"root{j}_{k}", widths[k], F32, at)
-            if j < SUMS_BY_GPSIMD:
+            if j in total:
                 nc.scalar.activation(
                     roots[j, k][:], total[j][:, halves[k]], ACT.Abs_reciprocal_sqrt, scale=g_inv[:, j : j + 1]
                 )
@@ -260,7 +258,7 @@ def tile_list_vegetation_change_indices_kernel(
 
         def square(j, k):
             into = inverse0[k][:, j, :] if j < PACK else inverse1[:, j - PACK, halves[k]]
-            if j < SUMS_BY_GPSIMD:
+            if j in total:
                 nc.scalar.activation(into, roots[j, k][:], ACT.Square)
             else:
                 nc.scalar.activation(into, backs[j, k][:], ACT.Square, scale=g_root[:, j : j + 1])
@@ -273,10 +271,10 @@ def tile_list_vegetation_change_indices_kernel(
                 ALU.mult,
             )
 
-        sum_banks = {(1, 0): 6, (1, 1): 7, (2, 0): 4, (2, 1): 5, (3, 0): 0, (3, 1): 0}
-        sum_banks.update({(4, 1): 6, (4, 0): 4, (5, 1): 0, (5, 0): 7, (6, 1): 7, (6, 0): 6, (7, 2): 4, (7, 3): 4, (7, 4): 4})
+        sum_banks = {(1, 0): 2, (1, 1): 3, (2, 0): 4, (2, 1): 5, (3, 0): 6, (3, 1): 6}
+        sum_banks.update({(4, 1): 2, (4, 0): 4, (5, 1): 6, (5, 0): 3, (6, 0): 3, (6, 1): 2})
         back_banks = dict(sum_banks)
-        back_banks.update({(3, 0): 1, (3, 1): 2, (5, 0): 3, (7, 2): 5, (7, 3): 3})
+        back_banks.update({(3, 0): 7, (3, 1): 0, (5, 0): 1, (6, 1): 4})
         for j in range(PACK):
             pick(j, (0, 1) if j == PACK - 1 else ())
             if j < SUMS_BY_GPSIMD:
@@ -285,7 +283,8 @@ def tile_list_vegetation_change_indices_kernel(
             else:
                 for k in range(1 if j == PACK - 1 else 2):
                     turn(j, k, sum_banks[j, k], (early[j], late[j]))
-            nc.gpsimd.tensor_tensor(diff0[:, j, :], late[j], early[j], ALU.subtract)
+            for cols in halves[:2] if j == PACK - 1 else (slice(0, PAIRS),):
+                nc.gpsimd.tensor_tensor(diff0[:, j, cols], late[j][:, cols], early[j][:, cols], ALU.subtract)
 
         g_root = place("g_root", SLICES, F32, at_last_words)
         nc.scalar.activation(g_root[:], g_inv[:], ACT.Abs_reciprocal_sqrt)
@@ -331,47 +330,40 @@ def tile_list_vegetation_change_indices_kernel(
         w2b.append(weave_w2(1))
 
         pick_late(6)
-        for k in wide_first:
+        for k in range(2):
             turn(6, k, sum_banks[6, k], (early[6], late[6]))
         early[last] = rows[:, early_row[last], :]
         nc.vector.tensor_copy(early[last], h[last][:].indirect(pos2_t[:]))
-        thirds = (2, 3, 4)
-        for k in thirds:
+        total[last] = place("total_last", PAIRS, F32)[:]
+        for k in range(2):
             nc.vector.tensor_tensor(
-                diff1[:, last - PACK, halves[k]],
+                total[last][:, halves[k]],
                 h[last][:].indirect(pos1_t[:, entries_of(k)]),
                 early[last][:, halves[k]],
-                ALU.subtract,
+                ALU.add,
             )
-        terms = (early[last], early[last], diff1[:, last - PACK, :])
-        turn(last, thirds[0], sum_banks[last, thirds[0]], terms)
-        for k in wide_first:
-            take_root(6, k, at_roots[1 - k])
+        nc.vector.scalar_tensor_tensor(
+            diff1[:, last - PACK, :], early[last], -2.0, total[last], ALU.mult, ALU.add
+        )
+        for k, at in enumerate((at_roots[0], at_roots[2])):
+            take_root(6, k, at)
             turn_back(6, k, back_banks[6, k])
-        for i, k in enumerate(thirds):
-            take_root(last, k, (at_roots[3], at_roots[2] + 2 * THIRD, at_roots[3])[i])
-            turn_back(last, k, back_banks[last, k])
-            if i < 2:
-                turn(last, thirds[i + 1], sum_banks[last, thirds[i + 1]], terms)
-            if i != 1:
-                square(6, 1 - i // 2)
+        for k in range(2):
+            take_root(last, k, at_roots[1 + 2 * k])
+            square(6, k)
             square(last, k)
 
         w2c = [place(f"w2c{b}", N, U32) for b in range(PASSES)]
         w2s = [place(f"w2s{b}", N, U8, at_h[last] + N * b) for b in range(PASSES)]
-        zc = [place("zc0", PAIRS, U32, at_roots[2]), place("zc1", PAIRS, U32)]
+        zc = {}
         zs = [place("zs0", PAIRS, U8, at_h[last] + 2 * N), place("zs1", PAIRS, U8)]
-        woven0.append(place("woven0b", PACK * THIRD, BF16, at_h[last] + 4 * N))
-        at_woven = room(2 * PACK * THIRD)
 
-        def quantise_z(woven, b, c0, c1):
-            nc.vector.quantize_mx(out=zc[b][:, c0:c1].bitcast(FP8X4), scales=zs[b][:, c0:c1], in_=woven)
 
         yc = place("yc", PAIRS, U32)
         ys = place("ys", PAIRS, U8)
         out_rows = out_0.rearrange("(p t) q -> p t q", t=PACK)
         out_words = out_1[0].rearrange("p m t -> p (m t)").bitcast(I32)
-        y_banks = (0, 1, 2, 3, 7, 5)
+        y_banks = (6, 7, 0, 2, 3, 4)
         yacc = {}
 
         def mix(b, c0, c1, opens):
@@ -384,7 +376,7 @@ def tile_list_vegetation_change_indices_kernel(
                         out=yacc[s0][:, t, :],
                         lhsT=w2c[b][:, P * t : P * (t + 1)].bitcast(FP8X4),
                         lhsT_scale=w2s[b][:, P * t : P * (t + 1)],
-                        rhs=zc[b][:, cols].bitcast(FP8X4),
+                        rhs=zc[b, s0 // Y_COLS][:].bitcast(FP8X4),
                         rhs_scale=zs[b][:, cols],
                         start=(opens and t == 0),
                         stop=(not opens and t == PACK - 1),
@@ -402,7 +394,7 @@ def tile_list_vegetation_change_indices_kernel(
                         yacc[s0].rearrange("p t n -> p n t"),
                     )
                 nc.scalar.copy(yf[:, :, cols], yacc[s0])
-            (nc.scalar if c1 == PAIRS else nc.sync).dma_start(out_rows[:, :, c0:c1], yf[:, :, c0:c1])
+            (nc.scalar if by_vector else nc.sync).dma_start(out_rows[:, :, c0:c1], yf[:, :, c0:c1])
 
         def finish(c0, c1, by_vector):
             if by_vector:
@@ -414,51 +406,55 @@ def tile_list_vegetation_change_indices_kernel(
                 out=yc[:, c0:c1].bitcast(FP8X4), scales=ys[:, c0:c1], in_=yb[:, PACK * c0 : PACK * c1]
             )
 
-        def first_pass(woven, c0, c1):
-            ratio(
-                nc.vector,
-                woven[:],
-                diff0[:, :, c0:c1],
-                inverse0[1][:, :, c0:c1],
-            )
+        runs = PAIRS // Y_COLS
+        wide_runs = (PAIRS - SPLIT) // Y_COLS
+        order = list(range(wide_runs, runs)) + list(range(wide_runs))
+        half = PACK * Y_COLS
+        at_woven = {n: room(3 * half) + half for n in order}
+        woven = {}
 
-        woven1 = {}
-
-        def second_pass(n):
+        def product(b, n, at):
             cols = slice(Y_COLS * n, Y_COLS * (n + 1))
-            woven1[n] = place(f"woven1_{n}", Y_COLS * PACK, BF16, at_woven if n == 0 else None)
-            ratio(nc.vector, woven1[n][:], diff1[:, :, cols], inverse1[:, :, cols])
+            woven[b, n] = place(f"woven{b}_{n}", Y_COLS * PACK, BF16, at)
+            diff, inverse = (diff0, inverse0[1]) if b == 0 else (diff1, inverse1)
+            ratio(nc.vector, woven[b, n][:], diff[:, :, cols], inverse[:, :, cols])
+
+        def codes(b, n, at):
+            zc[b, n] = place(f"zc{b}_{n}", Y_COLS, U32, at)
+            nc.vector.quantize_mx(
+                out=zc[b, n][:].bitcast(FP8X4), scales=zs[b][:, Y_COLS * n : Y_COLS * (n + 1)], in_=woven[b, n][:]
+            )
 
         def close(n):
             c0, c1 = Y_COLS * n, Y_COLS * (n + 1)
-            quantise_z(woven1[n][:], 1, c0, c1)
+            codes(1, n, None)
             mix(0, c0, c1, True)
             mix(1, c0, c1, False)
-            hand_out(c0, c1, n >= WOVEN_BY_SCALAR)
+            hand_out(c0, c1, n == order[-1])
 
+        for n in range(wide_runs, runs):
+            first = PACK * Y_COLS * (n - wide_runs)
+            woven[0, n] = woven0[0][:, first : first + PACK * Y_COLS]
         nc.vector.quantize_mx(out=w2c[0][:].bitcast(FP8X4), scales=w2s[0][:], in_=w2b[0][:])
-        quantise_z(woven0[0][:], 0, *PARTS[0])
-        first_pass(woven0[1], 0, THIRD)
+        codes(0, order[0], at_roots[2])
         nc.vector.quantize_mx(out=w2c[1][:].bitcast(FP8X4), scales=w2s[1][:], in_=w2b[1][:])
-        second_pass(0)
-        second_pass(1)
-        quantise_z(woven0[1][:], 0, 0, THIRD)
-        close(0)
-        woven0.append(place("woven0c", PACK * (PAIRS - SPLIT - THIRD), BF16, at_woven))
-        first_pass(woven0[2], THIRD, PAIRS - SPLIT)
-        close(1)
-        second_pass(2)
-        quantise_z(woven0[2][:], 0, THIRD, PAIRS - SPLIT)
-        for n in range(3, PAIRS // Y_COLS):
-            second_pass(n)
-            close(n - 1)
+        product(1, order[0], at_woven[order[0]])
+        for before, n in zip(order, order[1:]):
+            if n < wide_runs:
+                product(0, n, at_woven[order[order.index(before) - 1]] - half)
+                close(before)
+                codes(0, n, None)
+                product(1, n, at_woven[n])
+            else:
+                product(1, n, at_woven[n])
+                close(before)
+                codes(0, n, at_woven[before] + half)
+        finish(PAIRS - SPLIT, PAIRS, False)
+        nc.sync.dma_start(out_words[:, PAIRS - SPLIT :], yc[:, PAIRS - SPLIT :].bitcast(I32))
+        close(order[-1])
         finish(0, 256, False)
-        close(PAIRS // Y_COLS - 1)
-        finish(256, 512, True)
-        nc.sync.dma_start(out_words[:, :512], yc[:, :512].bitcast(I32))
-        finish(512, 640, True)
-        finish(640, 768, True)
-        nc.sync.dma_start(out_words[:, 512:], yc[:, 512:].bitcast(I32))
+        finish(256, 384, True)
+        nc.sync.dma_start(out_words[:, : PAIRS - SPLIT], yc[:, : PAIRS - SPLIT].bitcast(I32))
         for q in range(4):
             (nc.scalar, nc.sync)[q % 2].dma_start(
                 out_2[0, 4 * q : 4 * q + 4, :].bitcast(I32), ys[32 * q : 32 * q + 4, :].bitcast(I32)

@@ -201,15 +201,15 @@ def tile_list_vegetation_change_indices_kernel(
 
         halves = [slice(c0, c1) for c0, c1 in PARTS]
         widths = [c1 - c0 for c0, c1 in PARTS]
-        work = place("work", 16 * PAIRS, F32)
+        work = place("work", 17 * PAIRS, F32)
         rows = work[:].rearrange("p (r c) -> p r c", c=PAIRS)
         diff0 = rows[:, 1:8:2, :]
         shifted = work[:, 2 * PAIRS - SPLIT : 10 * PAIRS - SPLIT].rearrange("p (t c) -> p t c", t=PACK)
         diff1 = shifted[:, :, :PAIRS]
-        early_row = (3, 5, 7, 4, 9, 11, 13, 15)
-        late_row = (1, 0, 2, 6, 10, 12, 14)
+        early_row = (3, 5, 7, 0, 9, 11, 13, 15)
+        late_row = (1, 2, 4, 16, 10, 12, 14)
         inverse0 = [
-            place("inverse0a", PACK * SPLIT, F32)[:].rearrange("p (t c) -> p t c", t=PACK),
+            rows[:, 2:9:2, :SPLIT],
             place("inverse0b", PACK * widths[1], F32)[:].rearrange("p (t c) -> p t c", t=PACK),
         ]
         inverse1 = place("inverse1", PACK * PAIRS, F32)[:].rearrange("p (t c) -> p t c", t=PACK)
@@ -272,9 +272,9 @@ def tile_list_vegetation_change_indices_kernel(
             )
 
         sum_banks = {(1, 0): 2, (1, 1): 3, (2, 0): 4, (2, 1): 5, (3, 0): 6, (3, 1): 6}
-        sum_banks.update({(4, 1): 2, (4, 0): 4, (5, 1): 6, (5, 0): 3, (6, 0): 3, (6, 1): 2})
+        sum_banks.update({(4, 1): 2, (4, 0): 4, (5, 1): 6, (5, 0): 3, (6, 0): 3, (6, 1): 4})
         back_banks = dict(sum_banks)
-        back_banks.update({(3, 0): 7, (3, 1): 0, (5, 0): 1, (6, 1): 4})
+        back_banks.update({(3, 0): 7, (3, 1): 0, (5, 0): 1})
         for j in range(PACK):
             pick(j, (0, 1) if j == PACK - 1 else ())
             if j < SUMS_BY_GPSIMD:
@@ -301,11 +301,7 @@ def tile_list_vegetation_change_indices_kernel(
         last = SLICES - 1
         wide_first = (1, 0)
 
-        def pick_late(j):
-            pick(j, ())
-            nc.gpsimd.tensor_tensor(diff1[:, j - PACK, :], late[j], early[j], ALU.subtract)
-
-        pick_late(4)
+        pick(4, ())
         for k in wide_first:
             turn(4, k, sum_banks[4, k], (early[4], late[4]))
         for i, j in enumerate((1, 2, 3, 0)):
@@ -315,25 +311,27 @@ def tile_list_vegetation_change_indices_kernel(
         for j in range(PACK):
             square(j, 1)
 
-        pick_late(5)
+        pick(5, ())
+        nc.gpsimd.tensor_tensor(diff1[:, :2, :], rows[:, 10:13:2, :], rows[:, 9:12:2, :], ALU.subtract)
         for k in wide_first:
             turn(5, k, sum_banks[5, k], (early[5], late[5]))
-        for j in (4, 5):
-            for k in wide_first:
-                take_root(j, k, at_w2b[1] if (j, k) == (5, 1) else at_roots[2 * (j % 2) + 1 - k])
-                turn_back(j, k, back_banks[j, k])
+        for j, at in ((4, at_roots[0]), (5, at_w2b[1])):
+            take_root(j, 0, at)
+            turn_back(j, 0, back_banks[j, 0])
             if j == 4:
                 w2b = [weave_w2(0)]
-        for j in (4, 5):
-            for k in wide_first:
-                square(j, k)
+        square(4, 0)
+        square(5, 0)
         w2b.append(weave_w2(1))
 
-        pick_late(6)
+        pick(6, (0, 1))
+        for cols in halves:
+            nc.gpsimd.tensor_tensor(diff1[:, 2, cols], late[6][:, cols], early[6][:, cols], ALU.subtract)
         for k in range(2):
             turn(6, k, sum_banks[6, k], (early[6], late[6]))
         early[last] = rows[:, early_row[last], :]
-        nc.vector.tensor_copy(early[last], h[last][:].indirect(pos2_t[:]))
+        for k in range(2):
+            nc.vector.tensor_copy(early[last][:, halves[k]], h[last][:].indirect(pos2_t[:, entries_of(k)]))
         total[last] = place("total_last", PAIRS, F32)[:]
         for k in range(2):
             nc.vector.tensor_tensor(
@@ -342,16 +340,17 @@ def tile_list_vegetation_change_indices_kernel(
                 early[last][:, halves[k]],
                 ALU.add,
             )
-        nc.vector.scalar_tensor_tensor(
-            diff1[:, last - PACK, :], early[last], -2.0, total[last], ALU.mult, ALU.add
-        )
-        for k, at in enumerate((at_roots[0], at_roots[2])):
-            take_root(6, k, at)
-            turn_back(6, k, back_banks[6, k])
-        for k in range(2):
-            take_root(last, k, at_roots[1 + 2 * k])
-            square(6, k)
-            square(last, k)
+        take_root(6, 0, at_roots[2])
+        turn_back(6, 0, back_banks[6, 0])
+        take_root(last, 0, at_roots[2] + 4 * Y_COLS)
+        square(6, 0)
+        square(last, 0)
+        for j, at in ((4, at_roots[3]), (5, at_roots[0]), (6, at_roots[1]), (last, at_roots[2] + 4 * Y_COLS)):
+            take_root(j, 1, at)
+            if j < last:
+                turn_back(j, 1, back_banks[j, 1])
+        for j in range(PACK, SLICES):
+            square(j, 1)
 
         w2c = [place(f"w2c{b}", N, U32) for b in range(PASSES)]
         w2s = [place(f"w2s{b}", N, U8, at_h[last] + N * b) for b in range(PASSES)]
@@ -363,23 +362,27 @@ def tile_list_vegetation_change_indices_kernel(
         ys = place("ys", PAIRS, U8)
         out_rows = out_0.rearrange("(p t) q -> p t q", t=PACK)
         out_words = out_1[0].rearrange("p m t -> p (m t)").bitcast(I32)
-        y_banks = (6, 7, 0, 2, 3, 4)
+        y_banks = ((1,), (3,), (2, 6), (7,), (0,), (5,))
         yacc = {}
 
         def mix(b, c0, c1, opens):
             for s0 in range(c0, c1, Y_COLS):
                 cols = slice(s0, s0 + Y_COLS)
+                share = PACK // len(y_banks[s0 // Y_COLS])
                 if opens:
-                    yacc[s0] = bank(f"yacc{s0}", BANK, y_banks[s0 // Y_COLS])[:].rearrange("p (t n) -> p t n", t=PACK)
+                    yacc[s0] = [
+                        bank(f"yacc{s0}_{number}", share * Y_COLS, number)[:].rearrange("p (t n) -> p t n", t=share)
+                        for number in y_banks[s0 // Y_COLS]
+                    ]
                 for t in range(PACK):
                     nc.tensor.matmul_mx(
-                        out=yacc[s0][:, t, :],
+                        out=yacc[s0][t // share][:, t % share, :],
                         lhsT=w2c[b][:, P * t : P * (t + 1)].bitcast(FP8X4),
                         lhsT_scale=w2s[b][:, P * t : P * (t + 1)],
                         rhs=zc[b, s0 // Y_COLS][:].bitcast(FP8X4),
                         rhs_scale=zs[b][:, cols],
-                        start=(opens and t == 0),
-                        stop=(not opens and t == PACK - 1),
+                        start=(opens and t % share == 0),
+                        stop=(not opens and t % share == share - 1),
                     )
 
         yf = place("yf", PACK * PAIRS, F32, at_table + 2048)[:].rearrange("p (t c) -> p t c", t=PACK)
@@ -391,9 +394,12 @@ def tile_list_vegetation_change_indices_kernel(
                 if not by_vector:
                     nc.scalar.copy(
                         yb[:, PACK * s0 : PACK * (s0 + Y_COLS)].rearrange("p (n t) -> p n t", t=PACK),
-                        yacc[s0].rearrange("p t n -> p n t"),
+                        yacc[s0][0].rearrange("p t n -> p n t"),
                     )
-                nc.scalar.copy(yf[:, :, cols], yacc[s0])
+                    nc.scalar.copy(yf[:, :, cols], yacc[s0][0])
+                else:
+                    nc.scalar.copy(yf[:, :2, cols], yacc[s0][0])
+                    nc.vector.tensor_copy(yf[:, 2:, cols], yacc[s0][1])
             (nc.scalar if by_vector else nc.sync).dma_start(out_rows[:, :, c0:c1], yf[:, :, c0:c1])
 
         def finish(c0, c1, by_vector):
@@ -436,6 +442,9 @@ def tile_list_vegetation_change_indices_kernel(
             first = PACK * Y_COLS * (n - wide_runs)
             woven[0, n] = woven0[0][:, first : first + PACK * Y_COLS]
         nc.vector.quantize_mx(out=w2c[0][:].bitcast(FP8X4), scales=w2s[0][:], in_=w2b[0][:])
+        nc.vector.scalar_tensor_tensor(
+            diff1[:, last - PACK, :], early[last], -2.0, total[last], ALU.mult, ALU.add
+        )
         codes(0, order[0], at_roots[2])
         nc.vector.quantize_mx(out=w2c[1][:].bitcast(FP8X4), scales=w2s[1][:], in_=w2b[1][:])
         product(1, order[0], at_woven[order[0]])
@@ -452,8 +461,8 @@ def tile_list_vegetation_change_indices_kernel(
         finish(PAIRS - SPLIT, PAIRS, False)
         nc.sync.dma_start(out_words[:, PAIRS - SPLIT :], yc[:, PAIRS - SPLIT :].bitcast(I32))
         close(order[-1])
-        finish(0, 256, False)
-        finish(256, 384, True)
+        finish(0, PAIRS - SPLIT - Y_COLS, False)
+        finish(PAIRS - SPLIT - Y_COLS, PAIRS - SPLIT, True)
         nc.sync.dma_start(out_words[:, : PAIRS - SPLIT], yc[:, : PAIRS - SPLIT].bitcast(I32))
         for q in range(4):
             (nc.scalar, nc.sync)[q % 2].dma_start(

@@ -295,13 +295,19 @@ def tile_list_vegetation_change_indices_kernel(
         turn(PACK - 1, 1, sum_banks[PACK - 1, 1], (early[PACK - 1], late[PACK - 1]))
         for j in range(PACK):
             square(j, 0)
-        woven0 = [place("woven0a", PACK * SPLIT, BF16)]
-        ratio(nc.gpsimd, woven0[0][:], diff0[:, :, halves[0]], inverse0[0], 2)
+        paired = place("paired", PACK * SPLIT, BF16)
+        nc.gpsimd.tensor_tensor(
+            paired[:].rearrange("p (u c e) -> p u e c", u=2, e=2),
+            diff0[:, :, halves[0]].rearrange("p (u e) c -> p u e c", u=2),
+            inverse0[0].rearrange("p (u e) c -> p u e c", u=2),
+            ALU.mult,
+        )
 
         last = SLICES - 1
         wide_first = (1, 0)
 
         pick(4, ())
+        nc.gpsimd.tensor_tensor(diff1[:, 0, :], late[4], early[4], ALU.subtract)
         for k in wide_first:
             turn(4, k, sum_banks[4, k], (early[4], late[4]))
         for i, j in enumerate((1, 2, 3, 0)):
@@ -312,7 +318,7 @@ def tile_list_vegetation_change_indices_kernel(
             square(j, 1)
 
         pick(5, ())
-        nc.gpsimd.tensor_tensor(diff1[:, :2, :], rows[:, 10:13:2, :], rows[:, 9:12:2, :], ALU.subtract)
+        nc.gpsimd.tensor_tensor(diff1[:, 1, :], late[5], early[5], ALU.subtract)
         for k in wide_first:
             turn(5, k, sum_banks[5, k], (early[5], late[5]))
         for j, at in ((4, at_roots[0]), (5, at_w2b[1])):
@@ -323,6 +329,11 @@ def tile_list_vegetation_change_indices_kernel(
         square(4, 0)
         square(5, 0)
         w2b.append(weave_w2(1))
+        woven0 = [place("woven0a", PACK * SPLIT, BF16)]
+        nc.scalar.copy(
+            woven0[0][:].bitcast(U32).rearrange("p (c u) -> p c u", u=2),
+            paired[:].bitcast(U32).rearrange("p (u c) -> p c u", u=2),
+        )
 
         pick(6, (0, 1))
         for cols in halves:
@@ -461,9 +472,11 @@ def tile_list_vegetation_change_indices_kernel(
         finish(PAIRS - SPLIT, PAIRS, False)
         nc.sync.dma_start(out_words[:, PAIRS - SPLIT :], yc[:, PAIRS - SPLIT :].bitcast(I32))
         close(order[-1])
-        finish(0, PAIRS - SPLIT - Y_COLS, False)
-        finish(PAIRS - SPLIT - Y_COLS, PAIRS - SPLIT, True)
-        nc.sync.dma_start(out_words[:, : PAIRS - SPLIT], yc[:, : PAIRS - SPLIT].bitcast(I32))
+        rest = PAIRS - SPLIT - Y_COLS
+        finish(0, rest, False)
+        nc.sync.dma_start(out_words[:, :rest], yc[:, :rest].bitcast(I32))
+        finish(rest, PAIRS - SPLIT, True)
+        nc.sync.dma_start(out_words[:, rest : PAIRS - SPLIT], yc[:, rest : PAIRS - SPLIT].bitcast(I32))
         for q in range(4):
             (nc.scalar, nc.sync)[q % 2].dma_start(
                 out_2[0, 4 * q : 4 * q + 4, :].bitcast(I32), ys[32 * q : 32 * q + 4, :].bitcast(I32)

@@ -29,7 +29,7 @@ SPLIT = 384
 PARTS = ((PAIRS - SPLIT, PAIRS), (0, PAIRS - SPLIT))
 WIDEST = max(SPLIT, PAIRS - SPLIT)
 SUMS_BY_GPSIMD = 1
-DEALT_FIRST = 3
+FILLING = 3
 EARLY = 512
 
 
@@ -59,7 +59,6 @@ def tile_list_vegetation_change_indices_kernel(
         at_w2_late = room(4 * PACK * N)
         at_gain = room(64)
         at_w2 = [room(4 * PACK * N), at_w2_late]
-        at_w1_rest = room(2 * P * (SLICES - DEALT_FIRST))
         at_h = [room(4 * S) for j in range(SLICES)]
         at_roots = [room(4 * PAIRS) for j in range(4)]
         at_w2b = [room(2 * PACK * N) for b in range(PASSES)]
@@ -91,24 +90,16 @@ def tile_list_vegetation_change_indices_kernel(
         nc.sync.dma_start(pos2_t[:], pos2)
         nc.sync.dma_start(pos1_t[:], pos1)
 
-        w1w = {}
-
-        def deal_w1(tile, j0, j1):
-            b, t0 = divmod(j0, PACK)
-            nc.vector.tensor_copy(
-                tile.bitcast(U16).rearrange("p (t m) -> p t m", t=j1 - j0),
-                w1w_raw[:, H * b : H * (b + 1)].bitcast(U16).rearrange("p (m t) -> p t m", t=PACK)[:, t0 : t0 + j1 - j0],
-            )
-            for j in range(j0, j1):
-                w1w[j] = tile[:, 2 * P * (j - j0) : 2 * P * (j - j0 + 1)]
-
+        w1w = place("w1w", 2 * H, U8)
+        nc.vector.tensor_copy(
+            w1w[:].bitcast(U16).rearrange("p (b t m) -> p b t m", b=PASSES, t=PACK),
+            w1w_raw[:].bitcast(U16).rearrange("p (b m t) -> p b t m", b=PASSES, t=PACK),
+        )
         w1s = place("w1s", H, U8)
         nc.vector.tensor_copy(
             w1s[:].rearrange("p (b t m) -> p b t m", b=PASSES, t=PACK),
             w1s_raw[:].rearrange("p (b m t) -> p b t m", b=PASSES, t=PACK),
         )
-        w1w_first = place("w1w_first", 2 * P * DEALT_FIRST, U8)
-        deal_w1(w1w_first[:], 0, DEALT_FIRST)
         for r in range(1, 4):
             (nc.gpsimd if r == 1 else nc.scalar).dma_start(w1s[r:P:32, :].bitcast(I32), w1s[8 * r : P : 32, :].bitcast(I32))
 
@@ -117,7 +108,7 @@ def tile_list_vegetation_change_indices_kernel(
 
         spread = {}
         for c0, c1 in ((0, BANK), (BANK, S)):
-            spread[c0] = place(f"vs_spread{c0}", c1 - c0, U8, at_w1_rest + 2 * P * (PACK - DEALT_FIRST - 1) if c1 == S else None)
+            spread[c0] = place(f"vs_spread{c0}", c1 - c0, U8)
             nc.vector.tensor_copy(spread[c0][:], tabs[:].indirect(offs_t[:, c0 // 16 : c1 // 16]))
 
         def place_scales(c0, c1):
@@ -152,9 +143,6 @@ def tile_list_vegetation_change_indices_kernel(
         g_inv = place("g_inv", SLICES, F32)
         nc.gpsimd.tensor_scalar(g_pos[:], g_t[:], 0.0, 2.0, ALU.is_ge, ALU.mult)
         nc.gpsimd.tensor_scalar(g_sign[:], g_pos[:], 1.0, -1.0, ALU.mult, ALU.add)
-        w1w_rest = place("w1w_rest", 2 * P * (SLICES - DEALT_FIRST), U8, at_w1_rest)
-        deal_w1(w1w_rest[:, : 2 * P * (PACK - DEALT_FIRST)], DEALT_FIRST, PACK)
-        deal_w1(w1w_rest[:, 2 * P * (PACK - DEALT_FIRST) :], PACK, SLICES)
         nc.vector.reciprocal(g_inv[:], g_t[:])
 
         h = [place(f"h{j}", S, F32, at_h[j]) for j in range(SLICES)]
@@ -162,14 +150,14 @@ def tile_list_vegetation_change_indices_kernel(
         pieces = [(0, 0, 0, mid), (1, 0, 0, mid), (0, 0, mid, BANK), (1, 0, mid, BANK), (2, 0, 0, mid), (0, 1, 0, BANK)]
         pieces.extend([(0, 2, 0, mid), (0, 2, mid, 384), (0, 2, 384, BANK)])
         pieces.extend([(2, 0, mid, BANK), (1, 1, 0, BANK), (1, 2, 0, BANK), (2, 1, 0, BANK), (2, 2, 0, BANK)])
-        pieces.extend((j, c, 0, BANK) for j in range(DEALT_FIRST, SLICES) for c in range(S // BANK))
-        first_banks = [0, 1, 2, 3, 4, 5, 6, 7, 0, 6, 7, 1, 0, 2] + [n % BANKS for n in range(11, 26)]
+        pieces.extend((j, c, 0, BANK) for j in range(FILLING, SLICES) for c in range(S // BANK))
+        first_banks = [0, 1, 2, 3, 4, 5, 6, 7, 0, 6, 7, 1, 0, 2] + [5, 4, 3] + [n % BANKS for n in range(14, 26)]
         for n, (j, c, lo, hi) in enumerate(pieces):
             cols = slice(BANK * c + lo, BANK * c + hi)
             acc = bank(f"acc{n}", hi - lo, first_banks[n])
             nc.tensor.matmul_mx(
                 out=acc[:],
-                lhsT=w1w[j].bitcast(FP4X4),
+                lhsT=w1w[:, 2 * P * j : 2 * P * (j + 1)].bitcast(FP4X4),
                 lhsT_scale=w1s[:, P * j : P * (j + 1)],
                 rhs=vw[c][:, lo:hi].bitcast(FP8X4),
                 rhs_scale=vs[:, cols],

from contextlib import ExitStack

import concourse.mybir as mybir
from concourse.masks import make_identity

K, T, S, PAIRS, H, N = 512, 4096, 1536, 768, 1024, 512
FLOPS = 2 * K * H * S + 2 * H * N * PAIRS

F32 = mybir.dt.float32
BF16 = mybir.dt.bfloat16
I32 = mybir.dt.int32
U32 = mybir.dt.uint32
U16 = mybir.dt.uint16
U8 = mybir.dt.uint8
FP8X4 = mybir.dt.float8_e4m3fn_x4
FP4X4 = mybir.dt.float4_e2m1fn_x4
ACT = mybir.ActivationFunctionType
ALU = mybir.AluOpType
SIZE = {F32: 4, BF16: 2, I32: 4, U32: 4, U16: 2, U8: 1}

P = 128
PACK = 4
PASSES = H // (P * PACK)
SLICES = H // P
BANK = 512
BANKS = 8
Y_COLS = 128
SPLIT = 384
PARTS = ((PAIRS - SPLIT, PAIRS), (0, PAIRS - SPLIT))
WIDEST = max(SPLIT, PAIRS - SPLIT)
SUMS_BY_GPSIMD = 1
FILLING = 3
EARLY = 512


def tile_list_vegetation_change_indices_kernel(
    tc, tab_words, tab_scales, w1_words, w1_scales, g, w2, offs, pos1, pos2, out_0, out_1, out_2
):
    nc = tc.nc
    with ExitStack() as ctx:
        lists = ctx.enter_context(tc.tile_pool(name="lists", bufs=1))
        arena = ctx.enter_context(tc.tile_pool(name="arena", bufs=1))
        psum = ctx.enter_context(tc.psum_pool(name="psum", bufs=1))
        free = [0]

        def room(width):
            at = free[0]
            free[0] = at + -(-width // 64) * 64
            return at

        def place(name, cols, dtype, at=None):
            at = room(cols * SIZE[dtype]) if at is None else at
            return arena.tile([P, cols], dtype, name=name, align_bytes=64, offset=at)

        def bank(name, cols, number):
            return psum.tile([P, cols], F32, name=name, offset=4 * BANK * number)

        at_table = room(4 * T)
        at_w2_late = room(4 * PACK * N)
        at_gain = room(64)
        at_w2 = [room(4 * PACK * N), at_w2_late]
        at_h = [room(4 * S) for j in range(SLICES)]
        at_roots = [room(4 * PAIRS) for j in range(4)]
        at_w2b = [room(2 * PACK * N) for b in range(PASSES)]
        at_last_words = room(4 * BANK)
        at_ident = room(H)

        offs_t = lists.tile([P, S // 16], U16, name="offs_t")
        pos1_t = lists.tile([P, PAIRS // 16], U16, name="pos1_t")
        pos2_t = lists.tile([P, PAIRS // 16], U16, name="pos2_t")
        tabs = place("tabs", T, U8, at_gain - T // 2)
        tabw = place("tabw", T, I32, at_table)
        zeros = tabw[:, T - 8 :]
        w1s_raw = place("w1s_raw", H, U8, at_ident)
        vs = place("vs", S, U8)
        nc.gpsimd.memset(w1s_raw[:].bitcast(I32), 0)
        nc.vector.memset(zeros, 0)
        nc.vector.memset(tabs[:].bitcast(I32), 0)
        nc.vector.tensor_copy(vs[:, :32].bitcast(I32), zeros)
        nc.vector.memset(vs[:, 32:].bitcast(I32), 0)
        nc.sync.dma_start(offs_t[:], offs)
        tab_rows = tab_words[0].rearrange("p t i -> p (t i)").bitcast(I32)
        nc.sync.dma_start(tabw[:, :EARLY], tab_rows[:, :EARLY])
        w1w_raw = place("w1w_raw", 2 * H, U8)
        nc.scalar.dma_start(w1w_raw[:].bitcast(I32), w1_words[0].bitcast(I32))
        nc.scalar.dma_start(w1s_raw[0:P:8, :].bitcast(I32), w1_scales[0].bitcast(I32))
        nc.sync.dma_start(tabs[0:P:8, :].bitcast(I32), tab_scales[0].bitcast(I32))
        nc.sync.dma_start(tabw[:, EARLY:], tab_rows[:, EARLY:])
        w2_rows = w2.rearrange("(b p j) n -> b p (j n)", b=PASSES, j=PACK)
        nc.sync.dma_start(pos2_t[:], pos2)
        nc.sync.dma_start(pos1_t[:], pos1)

        w1w = place("w1w", 2 * H, U8)
        nc.vector.tensor_copy(
            w1w[:].bitcast(U16).rearrange("p (b t m) -> p b t m", b=PASSES, t=PACK),
            w1w_raw[:].bitcast(U16).rearrange("p (b m t) -> p b t m", b=PASSES, t=PACK),
        )
        w1s = place("w1s", H, U8)
        nc.vector.tensor_copy(
            w1s[:].rearrange("p (b t m) -> p b t m", b=PASSES, t=PACK),
            w1s_raw[:].rearrange("p (b m t) -> p b t m", b=PASSES, t=PACK),
        )
        for r in range(1, 4):
            (nc.gpsimd if r == 1 else nc.scalar).dma_start(w1s[r:P:32, :].bitcast(I32), w1s[8 * r : P : 32, :].bitcast(I32))

        ident = place("ident", P, F32, at_ident)
        make_identity(nc, ident[:])

        spread = {}
        for c0, c1 in ((0, BANK), (BANK, S)):
            spread[c0] = place(f"vs_spread{c0}", c1 - c0, U8)
            nc.vector.tensor_copy(spread[c0][:], tabs[:].indirect(offs_t[:, c0 // 16 : c1 // 16]))

        def place_scales(c0, c1):
            for q in range(4):
                (nc.scalar if c0 == 0 else nc.sync).dma_start(
                    vs[32 * q : 32 * q + 4, c0:c1].bitcast(I32),
                    spread[c0][32 * q : 32 * (q + 1) : 8, :].bitcast(I32),
                )

        g_t = place("g_t", SLICES, F32, at_gain)
        w2_raw = [place(f"w2_raw{b}", PACK * N, F32, at_w2[b]) for b in range(PASSES)]
        place_scales(0, BANK)
        nc.sync.dma_start(
            g_t[:].rearrange("p (b t) -> p b t", b=PASSES), g.rearrange("(b p t) -> p b t", b=PASSES, t=PACK)
        )
        nc.sync.dma_start(w2_raw[0][:, :N], w2_rows[0][:, :N])
        place_scales(BANK, S)
        for c0, c1 in ((N, 2 * N), (2 * N, PACK * N)):
            nc.sync.dma_start(w2_raw[0][:, c0:c1], w2_rows[0][:, c0:c1])
        for c0, c1 in ((0, 2 * N), (2 * N, PACK * N)):
            nc.sync.dma_start(w2_raw[1][:, c0:c1], w2_rows[1][:, c0:c1])
        vw = []
        for c in range(S // BANK):
            vw.append(place(f"vw{c}", BANK, U32, (None, at_roots[0], at_last_words)[c]))
            width = BANK if c == 1 else BANK // 2
            for lo in range(0, BANK, width):
                entries = slice((BANK * c + lo) // 16, (BANK * c + lo + width) // 16)
                nc.vector.tensor_copy(vw[c][:, lo : lo + width], tabw[:].bitcast(U32).indirect(offs_t[:, entries]))

        g_pos = place("g_pos", SLICES, F32)
        g_sign = place("g_sign", SLICES, F32)
        g_inv = place("g_inv", SLICES, F32)
        nc.gpsimd.tensor_scalar(g_pos[:], g_t[:], 0.0, 2.0, ALU.is_ge, ALU.mult)
        nc.gpsimd.tensor_scalar(g_sign[:], g_pos[:], 1.0, -1.0, ALU.mult, ALU.add)
        nc.vector.reciprocal(g_inv[:], g_t[:])

        h = [place(f"h{j}", S, F32, at_h[j]) for j in range(SLICES)]
        mid = BANK // 2
        pieces = [(0, 0, 0, mid), (1, 0, 0, mid), (0, 0, mid, BANK), (1, 0, mid, BANK), (2, 0, 0, mid), (0, 1, 0, BANK)]
        pieces.extend([(0, 2, 0, mid), (0, 2, mid, 384), (0, 2, 384, BANK)])
        pieces.extend([(2, 0, mid, BANK), (1, 1, 0, BANK), (1, 2, 0, BANK), (2, 1, 0, BANK), (2, 2, 0, BANK)])
        pieces.extend((j, c, 0, BANK) for j in range(FILLING, SLICES) for c in range(S // BANK))
        first_banks = [0, 1, 2, 3, 4, 5, 6, 7, 0, 6, 7, 1, 0, 2] + [5, 4, 3] + [n % BANKS for n in range(14, 26)]
        for n, (j, c, lo, hi) in enumerate(pieces):
            cols = slice(BANK * c + lo, BANK * c + hi)
            acc = bank(f"acc{n}", hi - lo, first_banks[n])
            nc.tensor.matmul_mx(
                out=acc[:],
                lhsT=w1w[:, 2 * P * j : 2 * P * (j + 1)].bitcast(FP4X4),
                lhsT_scale=w1s[:, P * j : P * (j + 1)],
                rhs=vw[c][:, lo:hi].bitcast(FP8X4),
                rhs_scale=vs[:, cols],
                start=True,
                stop=True,
            )
            nc.scalar.activation(h[j][:, cols], acc[:], ACT.Sigmoid)

        w2_pairs = [place(f"w2_pairs{b}", PACK * N, BF16) for b in range(PASSES)]
        for b in range(PASSES):
            pairs = w2_pairs[b][:].rearrange("p (u n e) -> p u n e", u=2, e=2)
            for j in range(PACK):
                nc.gpsimd.tensor_scalar(
                    pairs[:, j // 2, :, j % 2],
                    w2_raw[b][:, N * j : N * (j + 1)],
                    g_sign[:, PACK * b + j : PACK * b + j + 1],
                    0.0,
                    ALU.mult,
                    ALU.add,
                )

        def weave_w2(b):
            woven = place(f"w2b{b}", PACK * N, BF16, at_w2b[b])
            nc.scalar.copy(
                woven[:].bitcast(U32).rearrange("p (t m u) -> p m u t", t=PACK, u=2),
                w2_pairs[b][:].bitcast(U32).rearrange("p (u m t) -> p m u t", u=2, t=PACK),
            )
            return woven

        halves = [slice(c0, c1) for c0, c1 in PARTS]
        widths = [c1 - c0 for c0, c1 in PARTS]
        work = place("work", 17 * PAIRS, F32)
        rows = work[:].rearrange("p (r c) -> p r c", c=PAIRS)
        diff0 = rows[:, 1:8:2, :]
        shifted = work[:, 2 * PAIRS - SPLIT : 10 * PAIRS - SPLIT].rearrange("p (t c) -> p t c", t=PACK)
        diff1 = shifted[:, :, :PAIRS]
        early_row = (3, 5, 7, 0, 9, 11, 13, 15)
        late_row = (1, 2, 4, 16, 10, 12, 14)
        inverse0 = [
            rows[:, 2:9:2, :SPLIT],
            place("inverse0b", PACK * widths[1], F32)[:].rearrange("p (t c) -> p t c", t=PACK),
        ]
        inverse1 = place("inverse1", PACK * PAIRS, F32)[:].rearrange("p (t c) -> p t c", t=PACK)
        early, late, total, turned, roots = {}, {}, {}, {}, {}

        def entries_of(k):
            return slice(PARTS[k][0] // 16, PARTS[k][1] // 16)

        def pick(j, order):
            early[j], late[j] = rows[:, early_row[j], :], rows[:, late_row[j], :]
            nc.vector.tensor_copy(early[j], h[j][:].indirect(pos2_t[:]))
            if order:
                for k in order:
                    nc.vector.tensor_copy(late[j][:, halves[k]], h[j][:].indirect(pos1_t[:, entries_of(k)]))
            else:
                nc.vector.tensor_copy(late[j], h[j][:].indirect(pos1_t[:]))

        def turn(j, k, number, terms):
            turned[j, k] = bank(f"turned{j}_{k}", widths[k], number)
            for i, term in enumerate(terms):
                for c in range(0, widths[k], P):
                    nc.tensor.matmul(
                        turned[j, k][:, c : c + P],
                        term[:, PARTS[k][0] + c : PARTS[k][0] + c + P],
                        ident[:],
                        start=(i == 0 and c == 0),
                        stop=(i == len(terms) - 1 and c == widths[k] - P),
                        is_transpose=True,
                    )

        def take_root(j, k, at):
            roots[j, k] = place(f"root{j}_{k}", widths[k], F32, at)
            if j in total:
                nc.scalar.activation(
                    roots[j, k][:], total[j][:, halves[k]], ACT.Abs_reciprocal_sqrt, scale=g_inv[:, j : j + 1]
                )
            else:
                nc.scalar.activation(roots[j, k][:], turned[j, k][:], ACT.Abs_reciprocal_sqrt)

        backs = {}

        def turn_back(j, k, number):
            backs[j, k] = bank(f"back{j}_{k}", widths[k], number)
            for c in range(0, widths[k], P):
                nc.tensor.transpose(backs[j, k][:, c : c + P], roots[j, k][:, c : c + P], ident[:])

        def square(j, k):
            into = inverse0[k][:, j, :] if j < PACK else inverse1[:, j - PACK, halves[k]]
            if j in total:
                nc.scalar.activation(into, roots[j, k][:], ACT.Square)
            else:
                nc.scalar.activation(into, backs[j, k][:], ACT.Square, scale=g_root[:, j : j + 1])

        def ratio(engine, woven, diff, inverse, step=4):
            engine.tensor_tensor(
                woven.rearrange("p (c i t) -> p c t i", i=step, t=PACK),
                diff.rearrange("p t (c i) -> p c t i", i=step),
                inverse.rearrange("p t (c i) -> p c t i", i=step),
                ALU.mult,
            )

        sum_banks = {(1, 0): 2, (1, 1): 3, (2, 0): 4, (2, 1): 5, (3, 0): 6, (3, 1): 6}
        sum_banks.update({(4, 1): 2, (4, 0): 4, (5, 1): 6, (5, 0): 3, (6, 0): 3, (6, 1): 4})
        back_banks = dict(sum_banks)
        back_banks.update({(3, 0): 7, (3, 1): 0, (5, 0): 1})
        for j in range(PACK):
            pick(j, (0, 1) if j == PACK - 1 else ())
            if j < SUMS_BY_GPSIMD:
                total[j] = place("total0", PAIRS, F32, at_w2[1] + 4 * (PACK * N - PAIRS))[:]
                nc.gpsimd.tensor_tensor(total[j], late[j], early[j], ALU.add)
            else:
                for k in range(1 if j == PACK - 1 else 2):
                    turn(j, k, sum_banks[j, k], (early[j], late[j]))
            for cols in halves[:2] if j == PACK - 1 else (slice(0, PAIRS),):
                nc.gpsimd.tensor_tensor(diff0[:, j, cols], late[j][:, cols], early[j][:, cols], ALU.subtract)

        g_root = place("g_root", SLICES, F32, at_last_words)
        nc.scalar.activation(g_root[:], g_inv[:], ACT.Abs_reciprocal_sqrt)
        for j in range(PACK):
            take_root(j, 0, at_roots[j])
        for j in range(SUMS_BY_GPSIMD, PACK):
            turn_back(j, 0, back_banks[j, 0])
        turn(PACK - 1, 1, sum_banks[PACK - 1, 1], (early[PACK - 1], late[PACK - 1]))
        for j in range(PACK):
            square(j, 0)
        paired = place("paired", PACK * SPLIT, BF16)
        nc.gpsimd.tensor_tensor(
            paired[:].rearrange("p (u c e) -> p u e c", u=2, e=2),
            diff0[:, :, halves[0]].rearrange("p (u e) c -> p u e c", u=2),
            inverse0[0].rearrange("p (u e) c -> p u e c", u=2),
            ALU.mult,
        )

        last = SLICES - 1
        wide_first = (1, 0)

        pick(4, ())
        nc.gpsimd.tensor_tensor(diff1[:, 0, :], late[4], early[4], ALU.subtract)
        for k in wide_first:
            turn(4, k, sum_banks[4, k], (early[4], late[4]))
        for i, j in enumerate((1, 2, 3, 0)):
            take_root(j, 1, at_w2b[0] if j == 3 else at_roots[i])
        for j in range(SUMS_BY_GPSIMD, PACK):
            turn_back(j, 1, back_banks[j, 1])
        for j in range(PACK):
            square(j, 1)

        pick(5, ())
        nc.gpsimd.tensor_tensor(diff1[:, 1, :], late[5], early[5], ALU.subtract)
        for k in wide_first:
            turn(5, k, sum_banks[5, k], (early[5], late[5]))
        for j, at in ((4, at_roots[0]), (5, at_w2b[1])):
            take_root(j, 0, at)
            turn_back(j, 0, back_banks[j, 0])
            if j == 4:
                w2b = [weave_w2(0)]
        square(4, 0)
        square(5, 0)
        w2b.append(weave_w2(1))
        woven0 = [place("woven0a", PACK * SPLIT, BF16)]
        nc.scalar.copy(
            woven0[0][:].bitcast(U32).rearrange("p (c u) -> p c u", u=2),
            paired[:].bitcast(U32).rearrange("p (u c) -> p c u", u=2),
        )

        pick(6, (0, 1))
        for cols in halves:
            nc.gpsimd.tensor_tensor(diff1[:, 2, cols], late[6][:, cols], early[6][:, cols], ALU.subtract)
        for k in range(2):
            turn(6, k, sum_banks[6, k], (early[6], late[6]))
        early[last] = rows[:, early_row[last], :]
        for k in range(2):
            nc.vector.tensor_copy(early[last][:, halves[k]], h[last][:].indirect(pos2_t[:, entries_of(k)]))
        total[last] = place("total_last", PAIRS, F32)[:]
        for k in range(2):
            nc.vector.tensor_tensor(
                total[last][:, halves[k]],
                h[last][:].indirect(pos1_t[:, entries_of(k)]),
                early[last][:, halves[k]],
                ALU.add,
            )
        take_root(6, 0, at_roots[2])
        turn_back(6, 0, back_banks[6, 0])
        take_root(last, 0, at_roots[2] + 4 * Y_COLS)
        square(6, 0)
        square(last, 0)
        for j, at in ((4, at_roots[3]), (5, at_roots[0]), (6, at_roots[1]), (last, at_roots[2] + 4 * Y_COLS)):
            take_root(j, 1, at)
            if j < last:
                turn_back(j, 1, back_banks[j, 1])
        for j in range(PACK, SLICES):
            square(j, 1)

        w2c = [place(f"w2c{b}", N, U32) for b in range(PASSES)]
        w2s = [place(f"w2s{b}", N, U8, at_h[last] + N * b) for b in range(PASSES)]
        zc = {}
        zs = [place("zs0", PAIRS, U8, at_h[last] + 2 * N), place("zs1", PAIRS, U8)]


        yc = place("yc", PAIRS, U32)
        ys = place("ys", PAIRS, U8)
        out_rows = out_0.rearrange("(p t) q -> p t q", t=PACK)
        out_words = out_1[0].rearrange("p m t -> p (m t)").bitcast(I32)
        y_banks = ((1,), (3,), (2, 6), (7,), (0,), (5,))
        yacc = {}

        def mix(b, c0, c1, opens):
            for s0 in range(c0, c1, Y_COLS):
                cols = slice(s0, s0 + Y_COLS)
                share = PACK // len(y_banks[s0 // Y_COLS])
                if opens:
                    yacc[s0] = [
                        bank(f"yacc{s0}_{number}", share * Y_COLS, number)[:].rearrange("p (t n) -> p t n", t=share)
                        for number in y_banks[s0 // Y_COLS]
                    ]
                for t in range(PACK):
                    nc.tensor.matmul_mx(
                        out=yacc[s0][t // share][:, t % share, :],
                        lhsT=w2c[b][:, P * t : P * (t + 1)].bitcast(FP8X4),
                        lhsT_scale=w2s[b][:, P * t : P * (t + 1)],
                        rhs=zc[b, s0 // Y_COLS][:].bitcast(FP8X4),
                        rhs_scale=zs[b][:, cols],
                        start=(opens and t % share == 0),
                        stop=(not opens and t % share == share - 1),
                    )

        yf = place("yf", PACK * PAIRS, F32, at_table + 2048)[:].rearrange("p (t c) -> p t c", t=PACK)
        yb = place("yb", PAIRS * PACK, BF16)

        def hand_out(c0, c1, by_vector):
            for s0 in range(c0, c1, Y_COLS):
                cols = slice(s0, s0 + Y_COLS)
                if not by_vector:
                    nc.scalar.copy(
                        yb[:, PACK * s0 : PACK * (s0 + Y_COLS)].rearrange("p (n t) -> p n t", t=PACK),
                        yacc[s0][0].rearrange("p t n -> p n t"),
                    )
                    nc.scalar.copy(yf[:, :, cols], yacc[s0][0])
                else:
                    nc.scalar.copy(yf[:, :2, cols], yacc[s0][0])
                    nc.vector.tensor_copy(yf[:, 2:, cols], yacc[s0][1])
            (nc.scalar if by_vector else nc.sync).dma_start(out_rows[:, :, c0:c1], yf[:, :, c0:c1])

        def finish(c0, c1, by_vector):
            if by_vector:
                nc.vector.tensor_copy(
                    yb[:, PACK * c0 : PACK * c1].rearrange("p (c i t) -> p c t i", i=4, t=PACK),
                    yf[:, :, c0:c1].rearrange("p t (c i) -> p c t i", i=4),
                )
            nc.vector.quantize_mx(
                out=yc[:, c0:c1].bitcast(FP8X4), scales=ys[:, c0:c1], in_=yb[:, PACK * c0 : PACK * c1]
            )

        runs = PAIRS // Y_COLS
        wide_runs = (PAIRS - SPLIT) // Y_COLS
        order = list(range(wide_runs, runs)) + list(range(wide_runs))
        half = PACK * Y_COLS
        at_woven = {n: room(3 * half) + half for n in order}
        woven = {}

        def product(b, n, at):
            cols = slice(Y_COLS * n, Y_COLS * (n + 1))
            woven[b, n] = place(f"woven{b}_{n}", Y_COLS * PACK, BF16, at)
            diff, inverse = (diff0, inverse0[1]) if b == 0 else (diff1, inverse1)
            ratio(nc.vector, woven[b, n][:], diff[:, :, cols], inverse[:, :, cols])

        def codes(b, n, at):
            zc[b, n] = place(f"zc{b}_{n}", Y_COLS, U32, at)
            nc.vector.quantize_mx(
                out=zc[b, n][:].bitcast(FP8X4), scales=zs[b][:, Y_COLS * n : Y_COLS * (n + 1)], in_=woven[b, n][:]
            )

        def close(n):
            c0, c1 = Y_COLS * n, Y_COLS * (n + 1)
            codes(1, n, None)
            mix(0, c0, c1, True)
            mix(1, c0, c1, False)
            hand_out(c0, c1, n == order[-1])

        for n in range(wide_runs, runs):
            first = PACK * Y_COLS * (n - wide_runs)
            woven[0, n] = woven0[0][:, first : first + PACK * Y_COLS]
        nc.vector.quantize_mx(out=w2c[0][:].bitcast(FP8X4), scales=w2s[0][:], in_=w2b[0][:])
        nc.vector.scalar_tensor_tensor(
            diff1[:, last - PACK, :], early[last], -2.0, total[last], ALU.mult, ALU.add
        )
        codes(0, order[0], at_roots[2])
        nc.vector.quantize_mx(out=w2c[1][:].bitcast(FP8X4), scales=w2s[1][:], in_=w2b[1][:])
        product(1, order[0], at_woven[order[0]])
        for before, n in zip(order, order[1:]):
            if n < wide_runs:
                product(0, n, at_woven[order[order.index(before) - 1]] - half)
                close(before)
                codes(0, n, None)
                product(1, n, at_woven[n])
            else:
                product(1, n, at_woven[n])
                close(before)
                codes(0, n, at_woven[before] + half)
        finish(PAIRS - SPLIT, PAIRS, False)
        nc.sync.dma_start(out_words[:, PAIRS - SPLIT :], yc[:, PAIRS - SPLIT :].bitcast(I32))
        close(order[-1])
        rest = PAIRS - SPLIT - Y_COLS
        finish(0, rest, False)
        nc.sync.dma_start(out_words[:, :rest], yc[:, :rest].bitcast(I32))
        finish(rest, PAIRS - SPLIT, True)
        nc.sync.dma_start(out_words[:, rest : PAIRS - SPLIT], yc[:, rest : PAIRS - SPLIT].bitcast(I32))
        for q in range(4):
            (nc.scalar, nc.sync)[q % 2].dma_start(
                out_2[0, 4 * q : 4 * q + 4, :].bitcast(I32), ys[32 * q : 32 * q + 4, :].bitcast(I32)
            )
